import numpy as np
import ml_dtypes


def mxq(x, axis, fmt="e4m3"):
    dtype, down = {"e4m3": (ml_dtypes.float8_e4m3fn, 7), "e5m2": (ml_dtypes.float8_e5m2, 14)}[fmt]
    v = np.moveaxis(np.asarray(x, np.float32).astype(ml_dtypes.bfloat16).astype(np.float64), axis, -1)
    blocks = v.reshape(v.shape[:-1] + (-1, 32))
    amax = np.abs(blocks).max(-1, keepdims=True)
    byte = np.maximum(np.where(amax > 0, np.frexp(amax)[1] - 1 + 127, 0) - down, 1)
    scale = np.exp2(byte - 127.0)
    codes = (blocks / scale).astype(np.float32).astype(dtype).astype(np.float64)
    return np.moveaxis((codes * scale).reshape(v.shape), -1, axis)


WIDE = False


def mx_kscale(k):
    if not WIDE:
        return np.ones(k)
    levels = np.array([10, -10, 5, -5, 0])
    if k % 512:
        return np.exp2(np.random.permutation(np.resize(levels, k // 32))).repeat(32)
    a = np.empty((k // 512, 16))
    for p in range(k // 512):
        a[p, :8] = np.random.permutation(np.resize(levels, 8))
        for g in range(8):
            far = levels[np.abs(levels - a[p, g]) >= 10]
            a[p, g + 8] = far[np.random.randint(len(far))]
    return np.exp2(a.ravel()).repeat(32)


def f64(x):
    return np.asarray(x).astype(np.float64)


def striped(idx):
    return np.tile(idx.reshape(-1, 16).T, (8, 1)).astype(np.uint16)


def unstriped(offs):
    return offs[:16].T.reshape(-1).astype(np.int64)


E2M1 = np.array([0.0, 0.5, 1.0, 1.5, 2.0, 3.0, 4.0, 6.0, -0.0, -0.5, -1.0, -1.5, -2.0, -3.0, -4.0, -6.0])


def pack_weight(w, fmt):
    k, n = w.shape
    w = f64(np.asarray(w, np.float32).astype(ml_dtypes.bfloat16)).reshape(k // 32, 32, n)
    amax = np.abs(w).max(1)
    if fmt == "e4m3":
        byte = np.frexp(amax)[1] - 1 + 127 - 7
    else:
        mant, ex = np.frexp(amax / 6.0)
        byte = np.where(mant > 0.5, ex, ex - 1) + 127
    byte = np.clip(np.where(amax > 0, byte, 1), 1, 254)
    scaled = (w * np.exp2(127.0 - byte)[:, None, :]).reshape(k, n).astype(np.float32)
    by_word = np.ascontiguousarray(scaled.reshape(k // 512, 128, 4, n).transpose(0, 1, 3, 2))
    if fmt == "e4m3":
        words = by_word.astype(ml_dtypes.float8_e4m3fn).view(np.uint8)
    else:
        c = by_word.astype(ml_dtypes.float4_e2m1fn).view(np.uint8) & 0xF
        words = (c[..., 0::2] | (c[..., 1::2] << 4)).reshape(k // 512, 128, 2 * n)
    return np.ascontiguousarray(words), np.ascontiguousarray(byte.astype(np.uint8).reshape(k // 512, 16, n))


def unpack_weight(words, scales, fmt):
    g, _, n = scales.shape
    words = np.ascontiguousarray(words).reshape(g, 128, n, -1)
    if fmt == "e4m3":
        vals = words.view(ml_dtypes.float8_e4m3fn).astype(np.float64)
    else:
        nib = np.empty((g, 128, n, 4), np.uint8)
        nib[..., 0::2] = words & 0xF
        nib[..., 1::2] = words >> 4
        vals = E2M1[nib]
    vals = vals * np.repeat(np.exp2(scales.astype(np.float64) - 127.0), 8, axis=1)[..., None]
    return vals.transpose(0, 1, 3, 2).reshape(g * 512, n)


def planes(y):
    n, m = y.shape
    v = y.astype(np.float32).astype(ml_dtypes.bfloat16).astype(np.float64).reshape(n // 32, 32, m)
    top = np.abs(v).max(1)
    byte = np.clip(np.where(top > 0, np.frexp(top)[1] - 1 + 127 - 7, 1), 1, 254)
    codes = (v * np.exp2(127.0 - byte)[:, None, :]).reshape(n, m).astype(np.float32).astype(ml_dtypes.float8_e4m3fn).view(np.uint8)
    words = codes.reshape(n // 512, 128, 4, m).transpose(0, 1, 3, 2)
    return np.ascontiguousarray(words), np.ascontiguousarray(byte.astype(np.uint8).reshape(n // 512, 16, m))


def relu(v):
    return np.maximum(v, 0.0)


K, T, E, C, H, N = 1024, 512, 2, 256, 512, 512


def by_expert(wq, xq):
    return np.concatenate([wq[e].T @ xq[:, e * C:(e + 1) * C] for e in range(E)], axis=1)


def setup_inputs():
    n = np.random.standard_normal
    s = mx_kscale(K)
    u = mx_kscale(H)
    slot_token = np.random.permutation(T)[:E * C]
    x = pack_weight(n((K, T)) * s[:, None], "e4m3")
    wa = [pack_weight(m, "e2m1") for m in n((E, K, H)) / np.sqrt(K) / s[None, :, None] * u]
    wb = [pack_weight(m, "e2m1") for m in n((E, H, N)) / np.sqrt(H) / u[None, :, None]]
    return {
        "x_words": x[0],
        "x_scales": x[1],
        "w": (n((K, N)) / np.sqrt(K) / s[:, None]).astype(np.float32),
        "wa_words": np.stack([m[0] for m in wa]),
        "wa_scales": np.stack([m[1] for m in wa]),
        "wb_words": np.stack([m[0] for m in wb]),
        "wb_scales": np.stack([m[1] for m in wb]),
        "gate": np.tile(np.random.uniform(0.2, 1.0, E * C), (128, 1)).astype(np.float32),
        "offs": striped(slot_token),
    }


def reference(x_words, x_scales, w, wa_words, wa_scales, wb_words, wb_scales, gate, offs):
    wq = mxq(f64(w), 0, "e4m3")
    wa = np.stack([unpack_weight(wa_words[e], wa_scales[e], "e2m1") for e in range(E)])
    wb = np.stack([unpack_weight(wb_words[e], wb_scales[e], "e2m1") for e in range(E)])
    idx = unstriped(offs)
    x = unpack_weight(x_words, x_scales, "e4m3")
    base = wq.T @ x
    h = relu(by_expert(wa, x[:, idx]))
    y = by_expert(wb, mxq(h, 0, "e4m3"))
    c = np.zeros((N, T))
    c[:, idx] = f64(gate[:1]) * y
    out_0 = base + c
    return (out_0,) + planes(out_0)

@@ -1,0 +1,285 @@
+from contextlib import ExitStack
+
+import concourse.mybir as mybir
+from concourse.masks import make_identity
+
+K, T, E, C, H, N = 1024, 512, 2, 256, 512, 512
+FLOPS = 2 * K * N * T + 2 * K * H * T + 2 * H * N * T
+
+F32 = mybir.dt.float32
+BF16 = mybir.dt.bfloat16
+I32 = mybir.dt.int32
+U32 = mybir.dt.uint32
+U16 = mybir.dt.uint16
+U8 = mybir.dt.uint8
+FP8X4 = mybir.dt.float8_e4m3fn_x4
+FP4X4 = mybir.dt.float4_e2m1fn_x4
+ACT = mybir.ActivationFunctionType
+ALU = mybir.AluOpType
+
+P = 128
+PASSES = K // 512
+GROUPS = [(0, 128), (128, 128), (256, 256)]
+
+
+def tile_moe_adp_relu_kernel(
+    tc, x_words, x_scales, w, wa_words, wa_scales, wb_words, wb_scales, gate, offs, out_0, out_1, out_2
+):
+    nc = tc.nc
+    with ExitStack() as ctx:
+        keep = ctx.enter_context(tc.tile_pool(name="keep", bufs=1))
+        ring = ctx.enter_context(tc.tile_pool(name="ring", bufs=2))
+        psum = ctx.enter_context(tc.psum_pool(name="psum", bufs=1))
+
+        def held(shape, dtype, name, tag=None):
+            return keep.tile(shape, dtype, name=name, tag=tag or name, align_bytes=64)
+
+        offsets = keep.tile([P, T // 16], U16, name="offsets")
+        xw = [held([P, T], I32, "xw%d" % s) for s in range(PASSES)]
+        xs = held([P, PASSES * T], U8, "xs")
+        waw = [held([P, PASSES * 2 * H], U8, "waw%d" % e) for e in range(E)]
+        was = held([P, E * PASSES * H], U8, "was")
+        wbw = held([P, E * 2 * N], U8, "wbw")
+        wbs = held([P, E * N], U8, "wbs")
+        gcol = held([P, T // P], F32, "gcol")
+        wraw = [held([P, 4 * N], F32, "wraw%d" % s) for s in range(PASSES)]
+        ident = held([P, P], F32, "ident")
+
+        def load_scales(tile, rows, queues):
+            for q in range(4):
+                queues[q].dma_start(
+                    out=tile[32 * q : 32 * q + 4, :].bitcast(I32).rearrange("r (g c) -> r g c", c=128),
+                    in_=rows[4 * q : 4 * q + 4],
+                )
+
+        nc.gpsimd.memset(xs[:].bitcast(I32), 0)
+        nc.vector.memset(was[:].bitcast(I32), 0)
+        nc.vector.memset(wbs[:].bitcast(I32), 0)
+        make_identity(nc, ident[:])
+
+        nc.sync.dma_start(offsets[:], offs)
+        nc.sync.dma_start(out=xw[0][:], in_=x_words[0].rearrange("p n d -> p (n d)").bitcast(I32))
+        load_scales(xs, x_scales.bitcast(I32).rearrange("s b c -> b s c"), [nc.scalar] * 4)
+        nc.sync.dma_start(out=xw[1][:], in_=x_words[1].rearrange("p n d -> p (n d)").bitcast(I32))
+
+        def load_wa(e):
+            nc.sync.dma_start(
+                out=waw[e][:].bitcast(I32).rearrange("p (s c) -> p s c", s=PASSES),
+                in_=wa_words[e].bitcast(I32).rearrange("s p c -> p s c"),
+            )
+
+        load_wa(0)
+        load_scales(was, wa_scales.bitcast(I32).rearrange("e s b c -> b (e s) c"), [nc.sync, nc.scalar] * 2)
+        nc.sync.dma_start(
+            out=wbw[:].bitcast(I32).rearrange("p (e c) -> p e c", e=E),
+            in_=wb_words.bitcast(I32).rearrange("e s p c -> p (e s) c"),
+        )
+        load_scales(wbs, wb_scales.bitcast(I32).rearrange("e s b c -> b (e s) c"), [nc.scalar] * 4)
+        with nc.allow_non_contiguous_dma(reason="one gate value a partition"):
+            nc.scalar.dma_start(out=gcol[:], in_=gate[0].rearrange("(c p) -> p c", p=P))
+        load_wa(1)
+        for s in range(PASSES):
+            nc.sync.dma_start(
+                out=wraw[s][:], in_=w[512 * s : 512 * (s + 1), :].rearrange("(p j) n -> p (j n)", j=4)
+            )
+
+        gw = {}
+        gs = {}
+
+        def gather(g, s, tag=None):
+            first, width = GROUPS[g]
+            lst = offsets[:, first // 16 : (first + width) // 16]
+            gw[g, s] = held([P, width], I32, "gw%d_%d" % (g, s), tag)
+            gs[g, s] = held([P, width], U8, "gs%d_%d" % (g, s))
+            nc.vector.tensor_copy(gw[g, s][:].bitcast(U32), xw[s][:].bitcast(U32).indirect(lst))
+            nc.vector.tensor_copy(gs[g, s][:], xs[:, s * T : (s + 1) * T].indirect(lst))
+
+        hq = {}
+
+        def layer_a(g, b, bank):
+            first, width = GROUPS[g]
+            e = first // C
+            cols = slice(b * P, (b + 1) * P)
+            acc = psum.tile([P, H], F32, name="acc", tag="mm" + bank)
+            for s in range(PASSES):
+                nc.tensor.matmul_mx(
+                    out=acc[:],
+                    lhsT=gw[g, s][:, cols].bitcast(FP8X4),
+                    lhsT_scale=gs[g, s][:, cols],
+                    rhs=waw[e][:, s * 2 * H : (s + 1) * 2 * H].bitcast(FP4X4),
+                    rhs_scale=was[:, (e * PASSES + s) * H : (e * PASSES + s + 1) * H],
+                    start=(s == 0),
+                    stop=(s == PASSES - 1),
+                )
+            hrow = ring.tile([P, H], BF16, name="hrow", align_bytes=64)
+            nc.scalar.activation(
+                out=hrow[:].rearrange("s (u p e) -> s u p e", u=2, e=2),
+                in_=acc[:].rearrange("s (p u e) -> s u p e", u=2, e=2),
+                func=ACT.Relu,
+            )
+            turned = psum.tile([P, 4 * P], F32, name="turned", tag="tr" + bank)
+            for u in range(2):
+                nc.tensor.transpose(
+                    turned[:, u * P : (u + 1) * P], hrow[:].bitcast(F32)[:, u * P : (u + 1) * P], ident[:]
+                )
+            hcol = held([P, 4 * P], BF16, "hcol%d_%d" % (g, b))
+            nc.scalar.copy(
+                out=hcol[:].bitcast(F32).rearrange("p (s u) -> p s u", u=2),
+                in_=turned[:, 0 : 2 * P].rearrange("p (u s) -> p s u", u=2),
+            )
+            codes = held([P, P], U32, "hq%d_%d" % (g, b))
+            scales = held([P, P], U8, "hs%d_%d" % (g, b))
+            nc.vector.quantize_mx(out=codes[:].bitcast(FP8X4), scales=scales[:], in_=hcol[:])
+            hq[g, b] = (codes, scales)
+
+        ys = {}
+
+        def layer_b(g, b, bank):
+            first, width = GROUPS[g]
+            e = first // C
+            if b == 0:
+                ys[g] = held([P, 4 * width], F32, "ys%d" % g)
+            codes, scales = hq[g, b]
+            acc = psum.tile([P, N], F32, name="acc", tag="mm" + bank)
+            nc.tensor.matmul_mx(
+                out=acc[:],
+                lhsT=codes[:].bitcast(FP8X4),
+                lhsT_scale=scales[:],
+                rhs=wbw[:, e * 2 * N : (e + 1) * 2 * N].bitcast(FP4X4),
+                rhs_scale=wbs[:, e * N : (e + 1) * N],
+                start=True,
+                stop=True,
+            )
+            yrow = ring.tile([P, N], F32, name="yrow", align_bytes=64)
+            block = first // P + b
+            nc.scalar.activation(
+                out=yrow[:].rearrange("s (d m) -> s d m", d=4),
+                in_=acc[:].rearrange("s (m d) -> s d m", d=4),
+                func=ACT.Copy,
+                scale=gcol[:, block : block + 1],
+            )
+            turned = psum.tile([P, 4 * P], F32, name="turned", tag="tr" + bank)
+            for d in range(4):
+                nc.tensor.transpose(turned[:, d * P : (d + 1) * P], yrow[:, d * P : (d + 1) * P], ident[:])
+            nc.scalar.copy(
+                out=ys[g][:].rearrange("p (d s) -> p d s", d=4)[:, :, b * P : (b + 1) * P],
+                in_=turned[:].rearrange("p (d s) -> p d s", d=4),
+            )
+
+        placed = {}
+
+        def scatter(g, d, tag=None):
+            first, width = GROUPS[g]
+            if g == 0:
+                placed[d] = held([P, T], F32, "placed%d" % d, tag)
+            lst = offsets[:, first // 16 : (first + width) // 16]
+            nc.vector.tensor_copy(placed[d][:].indirect(lst), ys[g][:, d * width : (d + 1) * width])
+
+        wbf = [held([P, 4 * N], BF16, "wbf%d" % s) for s in range(PASSES)]
+        wq = [held([P, N], U32, "wq%d" % s) for s in range(PASSES)]
+        wsc = [held([P, N], U8, "wsc%d" % s) for s in range(PASSES)]
+
+        def round_w(s):
+            nc.gpsimd.tensor_scalar(
+                out=wbf[s][:].rearrange("p (d m j) -> p m d j", d=4, j=4),
+                in0=wraw[s][:].rearrange("p (j m d) -> p m d j", d=4, j=4),
+                scalar1=1.0,
+                scalar2=0.0,
+                op0=ALU.mult,
+                op1=ALU.add,
+            )
+
+        def quant_w(s):
+            nc.vector.quantize_mx(out=wq[s][:].bitcast(FP8X4), scales=wsc[s][:], in_=wbf[s][:])
+
+        base = {}
+
+        def frozen(d, bank):
+            base[d] = psum.tile([P, T], F32, name="base%d" % d, tag=bank)
+            for s in range(PASSES):
+                nc.tensor.matmul_mx(
+                    out=base[d][:],
+                    lhsT=wq[s][:, d * P : (d + 1) * P].bitcast(FP8X4),
+                    lhsT_scale=wsc[s][:, d * P : (d + 1) * P],
+                    rhs=xw[s][:].bitcast(FP8X4),
+                    rhs_scale=xs[:, s * T : (s + 1) * T],
+                    start=(s == 0),
+                    stop=(s == PASSES - 1),
+                )
+
+        total = [held([P, 2 * T], F32, "total%d" % i) for i in range(2)]
+        rows = out_0.rearrange("(p d) t -> p d t", d=4)
+
+        def total_of(d):
+            return total[d // 2][:, (d % 2) * T : (d % 2 + 1) * T]
+
+        def add_early(d):
+            moved = ring.tile([P, T], F32, name="moved", align_bytes=64)
+            nc.scalar.copy(out=moved[:], in_=base[d][:])
+            nc.gpsimd.tensor_tensor(out=total_of(d), in0=moved[:], in1=placed[d][:], op=ALU.add)
+            nc.sync.dma_start(out=rows[:, d, :], in_=total_of(d))
+
+        ow = held([P, T], U32, "ow")
+        osc = held([P, T], U8, "osc")
+        obf = held([P, 4 * T], BF16, "obf")
+
+        def round_pair(copy, i, cols):
+            copy(
+                out=obf[:].rearrange("p (t d) -> p t d", d=4)[:, cols, 2 * i : 2 * i + 2],
+                in_=total[i][:].rearrange("p (d t) -> p t d", d=2)[:, cols, :],
+            )
+
+        gather(0, 0)
+        gather(0, 1)
+        gather(1, 0)
+        gather(1, 1)
+        gather(2, 0)
+        layer_a(0, 0, "A")
+        gather(2, 1, "hcol0_0")
+        layer_a(1, 0, "B")
+        layer_b(0, 0, "C")
+        scatter(0, 0)
+        scatter(0, 1)
+        layer_a(2, 0, "D")
+        scatter(0, 2, "hcol2_0")
+        layer_b(1, 0, "A")
+        layer_a(2, 1, "B")
+        scatter(0, 3, "hcol2_1")
+        layer_b(2, 0, "C")
+        layer_b(2, 1, "D")
+        round_w(0)
+        round_w(1)
+        scatter(1, 0)
+        scatter(1, 1)
+        quant_w(0)
+        scatter(1, 2)
+        scatter(1, 3)
+        quant_w(1)
+        for d, bank in enumerate(("mmD", "trC", "trD")):
+            frozen(d, bank)
+            scatter(2, d)
+            add_early(d)
+        frozen(3, "mmD")
+        round_pair(nc.scalar.copy, 0, slice(0, T))
+        scatter(2, 3)
+        parts = [slice(256, 512), slice(0, 128), slice(128, 256)]
+        for cols in parts:
+            nc.vector.tensor_tensor(
+                out=total_of(3)[:, cols], in0=base[3][:, cols], in1=placed[3][:, cols], op=ALU.add
+            )
+        nc.sync.dma_start(out=rows[:, 3, :], in_=total_of(3))
+        round_pair(nc.vector.tensor_copy, 1, parts[0])
+        round_pair(nc.scalar.copy, 1, parts[1])
+        round_pair(nc.vector.tensor_copy, 1, parts[2])
+        words_out = out_1[0].rearrange("p n d -> p (n d)").bitcast(I32)
+        for first in (256, 0):
+            cols = slice(first, first + 256)
+            nc.vector.quantize_mx(
+                out=ow[:, cols].bitcast(FP8X4), scales=osc[:, cols], in_=obf[:, 4 * first : 4 * first + 1024]
+            )
+            nc.sync.dma_start(out=words_out[:, cols], in_=ow[:, cols].bitcast(I32))
+        for q in range(4):
+            eng = nc.sync if q % 2 else nc.scalar
+            eng.dma_start(
+                out=out_2[0, 4 * q : 4 * q + 4, :].bitcast(I32), in_=osc[32 * q : 32 * q + 4, :].bitcast(I32)
+            )

@@ -41,47 +41,55 @@ def tile_moe_adp_relu_kernel(
         was = held([P, E * PASSES * H], U8, "was")
         wbw = held([P, E * 2 * N], U8, "wbw")
         wbs = held([P, E * N], U8, "wbs")
-        gcol = held([P, T // P], F32, "gcol")
+        gates = held([P, T], F32, "gates")
         wraw = [held([P, 4 * N], F32, "wraw%d" % s) for s in range(PASSES)]
         ident = held([P, P], F32, "ident")
 
-        def load_scales(tile, rows, queues):
-            for q in range(4):
-                queues[q].dma_start(
-                    out=tile[32 * q : 32 * q + 4, :].bitcast(I32).rearrange("r (g c) -> r g c", c=128),
-                    in_=rows[4 * q : 4 * q + 4],
-                )
+        def load_scales(tile, rows, q, queue):
+            queue.dma_start(
+                out=tile[32 * q : 32 * q + 4, :].bitcast(I32).rearrange("r (g c) -> r g c", c=128),
+                in_=rows[4 * q : 4 * q + 4],
+            )
 
-        nc.gpsimd.memset(xs[:].bitcast(I32), 0)
-        nc.vector.memset(was[:].bitcast(I32), 0)
-        nc.vector.memset(wbs[:].bitcast(I32), 0)
-        make_identity(nc, ident[:])
+        def load_x(s, queue):
+            queue.dma_start(out=xw[s][:], in_=x_words[s].rearrange("p n d -> p (n d)").bitcast(I32))
 
-        nc.sync.dma_start(offsets[:], offs)
-        nc.sync.dma_start(out=xw[0][:], in_=x_words[0].rearrange("p n d -> p (n d)").bitcast(I32))
-        load_scales(xs, x_scales.bitcast(I32).rearrange("s b c -> b s c"), [nc.scalar] * 4)
-        nc.sync.dma_start(out=xw[1][:], in_=x_words[1].rearrange("p n d -> p (n d)").bitcast(I32))
-
-        def load_wa(e):
-            nc.sync.dma_start(
+        def load_wa(e, queue):
+            queue.dma_start(
                 out=waw[e][:].bitcast(I32).rearrange("p (s c) -> p s c", s=PASSES),
                 in_=wa_words[e].bitcast(I32).rearrange("s p c -> p s c"),
             )
 
-        load_wa(0)
-        load_scales(was, wa_scales.bitcast(I32).rearrange("e s b c -> b (e s) c"), [nc.sync, nc.scalar] * 2)
+        def load_w(s):
+            nc.sync.dma_start(
+                out=wraw[s][:], in_=w[512 * s : 512 * (s + 1), :].rearrange("(p j) n -> p (j n)", j=4)
+            )
+
+        xs_rows = x_scales.bitcast(I32).rearrange("s b c -> b s c")
+        was_rows = wa_scales.bitcast(I32).rearrange("e s b c -> b (e s) c")
+        wbs_rows = wb_scales.bitcast(I32).rearrange("e s b c -> b (e s) c")
+
+        nc.vector.memset(xs[:].bitcast(I32), 0)
+        nc.vector.memset(wbs[:].bitcast(I32), 0)
+        make_identity(nc, ident[:])
+        load_x(0, nc.sync)
+        load_x(1, nc.scalar)
+        for q in range(4):
+            load_scales(xs, xs_rows, q, nc.sync if q < 2 else nc.scalar)
+        nc.sync.dma_start(offsets[:], offs)
+        load_wa(0, nc.scalar)
+        for q, queue in enumerate((nc.sync, nc.scalar, nc.sync, nc.scalar)):
+            load_scales(was, was_rows, q, queue)
         nc.sync.dma_start(
             out=wbw[:].bitcast(I32).rearrange("p (e c) -> p e c", e=E),
             in_=wb_words.bitcast(I32).rearrange("e s p c -> p (e s) c"),
         )
-        load_scales(wbs, wb_scales.bitcast(I32).rearrange("e s b c -> b (e s) c"), [nc.scalar] * 4)
-        with nc.allow_non_contiguous_dma(reason="one gate value a partition"):
-            nc.scalar.dma_start(out=gcol[:], in_=gate[0].rearrange("(c p) -> p c", p=P))
-        load_wa(1)
-        for s in range(PASSES):
-            nc.sync.dma_start(
-                out=wraw[s][:], in_=w[512 * s : 512 * (s + 1), :].rearrange("(p j) n -> p (j n)", j=4)
-            )
+        for q in range(4):
+            load_scales(wbs, wbs_rows, q, nc.gpsimd if q < 2 else nc.sync)
+        load_wa(1, nc.sync)
+        nc.sync.dma_start(out=gates[:], in_=gate)
+        load_w(0)
+        load_w(1)
 
         gw = {}
         gs = {}
@@ -95,12 +103,13 @@ def tile_moe_adp_relu_kernel(
             nc.vector.tensor_copy(gs[g, s][:], xs[:, s * T : (s + 1) * T].indirect(lst))
 
         hq = {}
+        hcol = {}
 
-        def layer_a(g, b, bank):
+        def layer_a(g, b, bank, turn_bank):
             first, width = GROUPS[g]
             e = first // C
             cols = slice(b * P, (b + 1) * P)
-            acc = psum.tile([P, H], F32, name="acc", tag="mm" + bank)
+            acc = psum.tile([P, H], F32, name="acc", tag=bank)
             for s in range(PASSES):
                 nc.tensor.matmul_mx(
                     out=acc[:],
@@ -117,76 +126,75 @@ def tile_moe_adp_relu_kernel(
                 in_=acc[:].rearrange("s (p u e) -> s u p e", u=2, e=2),
                 func=ACT.Relu,
             )
-            turned = psum.tile([P, 4 * P], F32, name="turned", tag="tr" + bank)
+            turned = psum.tile([P, 4 * P], F32, name="turned", tag=turn_bank)
             for u in range(2):
                 nc.tensor.transpose(
                     turned[:, u * P : (u + 1) * P], hrow[:].bitcast(F32)[:, u * P : (u + 1) * P], ident[:]
                 )
-            hcol = held([P, 4 * P], BF16, "hcol%d_%d" % (g, b))
+            if b == 0:
+                hcol[g] = held([P, 4 * width], BF16, "hcol%d" % g)
             nc.scalar.copy(
-                out=hcol[:].bitcast(F32).rearrange("p (s u) -> p s u", u=2),
+                out=hcol[g][:, 4 * P * b : 4 * P * (b + 1)].bitcast(F32).rearrange("p (s u) -> p s u", u=2),
                 in_=turned[:, 0 : 2 * P].rearrange("p (u s) -> p s u", u=2),
             )
-            codes = held([P, P], U32, "hq%d_%d" % (g, b))
-            scales = held([P, P], U8, "hs%d_%d" % (g, b))
-            nc.vector.quantize_mx(out=codes[:].bitcast(FP8X4), scales=scales[:], in_=hcol[:])
-            hq[g, b] = (codes, scales)
 
-        ys = {}
+        def quant_h(g):
+            width = GROUPS[g][1]
+            codes = held([P, width], U32, "hq%d" % g)
+            scales = held([P, width], U8, "hs%d" % g)
+            nc.vector.quantize_mx(out=codes[:].bitcast(FP8X4), scales=scales[:], in_=hcol[g][:])
+            hq[g] = (codes, scales)
 
-        def layer_b(g, b, bank):
+        wbw_dealt = {}
+        wbs_dealt = {}
+
+        def deal_wb(e, words_tag=None, scales_tag=None):
+            wbw_dealt[e] = held([P, 2 * N], U8, "wbw_dealt%d" % e, words_tag)
+            wbs_dealt[e] = held([P, N], U8, "wbs_dealt%d" % e, scales_tag)
+            nc.vector.tensor_copy(
+                wbw_dealt[e][:].bitcast(U16).rearrange("p (d a b) -> p a d b", d=4, b=8),
+                wbw[:, e * 2 * N : (e + 1) * 2 * N].bitcast(U16).rearrange("p (a b d) -> p a d b", d=4, b=8),
+            )
+            nc.vector.tensor_copy(
+                wbs_dealt[e][:].rearrange("p (d a b) -> p a d b", d=4, b=16),
+                wbs[:, e * N : (e + 1) * N].rearrange("p (a b d) -> p a d b", d=4, b=16),
+            )
+
+        def layer_b(g, ds, bank):
             first, width = GROUPS[g]
             e = first // C
-            if b == 0:
-                ys[g] = held([P, 4 * width], F32, "ys%d" % g)
-            codes, scales = hq[g, b]
-            acc = psum.tile([P, N], F32, name="acc", tag="mm" + bank)
-            nc.tensor.matmul_mx(
-                out=acc[:],
-                lhsT=codes[:].bitcast(FP8X4),
-                lhsT_scale=scales[:],
-                rhs=wbw[:, e * 2 * N : (e + 1) * 2 * N].bitcast(FP4X4),
-                rhs_scale=wbs[:, e * N : (e + 1) * N],
-                start=True,
-                stop=True,
-            )
-            yrow = ring.tile([P, N], F32, name="yrow", align_bytes=64)
-            block = first // P + b
-            nc.scalar.activation(
-                out=yrow[:].rearrange("s (d m) -> s d m", d=4),
-                in_=acc[:].rearrange("s (m d) -> s d m", d=4),
-                func=ACT.Copy,
-                scale=gcol[:, block : block + 1],
-            )
-            turned = psum.tile([P, 4 * P], F32, name="turned", tag="tr" + bank)
-            for d in range(4):
-                nc.tensor.transpose(turned[:, d * P : (d + 1) * P], yrow[:, d * P : (d + 1) * P], ident[:])
-            nc.scalar.copy(
-                out=ys[g][:].rearrange("p (d s) -> p d s", d=4)[:, :, b * P : (b + 1) * P],
-                in_=turned[:].rearrange("p (d s) -> p d s", d=4),
-            )
+            codes, scales = hq[g]
+            acc = psum.tile([P, N], F32, name="yacc", tag=bank)
+            for i, d in enumerate(ds):
+                nc.tensor.matmul_mx(
+                    out=acc[:, i * width : (i + 1) * width],
+                    lhsT=wbw_dealt[e][:, d * 2 * P : (d + 1) * 2 * P].bitcast(FP4X4),
+                    lhsT_scale=wbs_dealt[e][:, d * P : (d + 1) * P],
+                    rhs=codes[:].bitcast(FP8X4),
+                    rhs_scale=scales[:],
+                    start=True,
+                    stop=True,
+                )
+            return acc
 
         placed = {}
 
-        def scatter(g, d, tag=None):
-            first, width = GROUPS[g]
-            if g == 0:
+        def scatter(d, first, values, tag=None):
+            width = values.shape[1]
+            if d not in placed:
                 placed[d] = held([P, T], F32, "placed%d" % d, tag)
             lst = offsets[:, first // 16 : (first + width) // 16]
-            nc.vector.tensor_copy(placed[d][:].indirect(lst), ys[g][:, d * width : (d + 1) * width])
+            nc.vector.tensor_tensor(placed[d][:].indirect(lst), values, gates[:, first : first + width], ALU.mult)
 
         wbf = [held([P, 4 * N], BF16, "wbf%d" % s) for s in range(PASSES)]
         wq = [held([P, N], U32, "wq%d" % s) for s in range(PASSES)]
         wsc = [held([P, N], U8, "wsc%d" % s) for s in range(PASSES)]
 
-        def round_w(s):
-            nc.gpsimd.tensor_scalar(
-                out=wbf[s][:].rearrange("p (d m j) -> p m d j", d=4, j=4),
-                in0=wraw[s][:].rearrange("p (j m d) -> p m d j", d=4, j=4),
-                scalar1=1.0,
-                scalar2=0.0,
-                op0=ALU.mult,
-                op1=ALU.add,
+        def round_w(s, part):
+            ms = slice(32 * part, 32 * (part + 1))
+            nc.scalar.copy(
+                out=wbf[s][:].rearrange("p (d m j) -> p m d j", d=4, j=4)[:, ms],
+                in_=wraw[s][:].rearrange("p (j m d) -> p m d j", d=4, j=4)[:, ms],
             )
 
         def quant_w(s):
@@ -214,9 +222,7 @@ def tile_moe_adp_relu_kernel(
             return total[d // 2][:, (d % 2) * T : (d % 2 + 1) * T]
 
         def add_early(d):
-            moved = ring.tile([P, T], F32, name="moved", align_bytes=64)
-            nc.scalar.copy(out=moved[:], in_=base[d][:])
-            nc.gpsimd.tensor_tensor(out=total_of(d), in0=moved[:], in1=placed[d][:], op=ALU.add)
+            nc.vector.tensor_tensor(out=total_of(d), in0=base[d][:], in1=placed[d][:], op=ALU.add)
             nc.sync.dma_start(out=rows[:, d, :], in_=total_of(d))
 
         ow = held([P, T], U32, "ow")
@@ -233,35 +239,58 @@ def tile_moe_adp_relu_kernel(
         gather(0, 1)
         gather(1, 0)
         gather(1, 1)
+        deal_wb(0)
         gather(2, 0)
-        layer_a(0, 0, "A")
-        gather(2, 1, "hcol0_0")
-        layer_a(1, 0, "B")
-        layer_b(0, 0, "C")
-        scatter(0, 0)
-        scatter(0, 1)
-        layer_a(2, 0, "D")
-        scatter(0, 2, "hcol2_0")
-        layer_b(1, 0, "A")
-        layer_a(2, 1, "B")
-        scatter(0, 3, "hcol2_1")
-        layer_b(2, 0, "C")
-        layer_b(2, 1, "D")
-        round_w(0)
-        round_w(1)
-        scatter(1, 0)
-        scatter(1, 1)
+        layer_a(0, 0, "mmA", "trA")
+        quant_h(0)
+        gather(2, 1, "hcol0")
+        layer_a(1, 0, "mmB", "trB")
+        quant_h(1)
+        late = held([P, 2 * C], F32, "late")
+        late_view = late[:].rearrange("p (d s) -> p d s", d=2)
+        acc = layer_b(0, [0, 1, 2, 3], "mmC")
+        y00 = held([P, P], F32, "y00")
+        y01 = held([P, P], F32, "y01")
+        nc.scalar.copy(out=y00[:], in_=acc[:, 0:P])
+        scatter(0, 0, y00[:])
+        nc.scalar.copy(out=y01[:], in_=acc[:, P : 2 * P])
+        scatter(1, 0, y01[:])
+        nc.scalar.copy(out=late_view[:, :, 0:P], in_=acc[:, 2 * P : 4 * P].rearrange("p (d s) -> p d s", d=2))
+        acc = layer_b(1, [0, 1, 2, 3], "mmD")
+        y1 = held([P, 2 * P], F32, "y1")
+        nc.scalar.copy(out=y1[:], in_=acc[:, 0 : 2 * P])
+        nc.scalar.copy(out=late_view[:, :, P:C], in_=acc[:, 2 * P : 4 * P].rearrange("p (d s) -> p d s", d=2))
+        scatter(0, P, y1[:, 0:P])
+        scatter(1, P, y1[:, P : 2 * P])
+        deal_wb(1, "y01", "y00")
+        layer_a(2, 0, "trB", "mmA")
+        layer_a(2, 1, "mmC", "mmB")
+        quant_h(2)
+        scatter(2, 0, late[:, 0:C], "hcol2")
+        acc = layer_b(2, [0, 1], "mmC")
+        y2 = held([P, 2 * C], F32, "y2")
+        nc.scalar.copy(out=y2[:], in_=acc[:])
+        for s in range(PASSES):
+            for part in range(4):
+                round_w(s, part)
         quant_w(0)
-        scatter(1, 2)
-        scatter(1, 3)
+        scatter(0, C, y2[:, 0:C])
         quant_w(1)
-        for d, bank in enumerate(("mmD", "trC", "trD")):
+        scatter(3, 0, late[:, C : 2 * C], "wbf1")
+        for d, bank in enumerate(("mmA", "mmB", "trA", "trB")):
             frozen(d, bank)
-            scatter(2, d)
-            add_early(d)
-        frozen(3, "mmD")
+        scatter(1, C, y2[:, C : 2 * C])
+        add_early(0)
+        add_early(1)
+        acc = layer_b(2, [2, 3], "mmD")
+        y22 = held([P, C], F32, "y22")
+        nc.scalar.copy(out=y22[:], in_=acc[:, 0:C])
+        y23 = held([P, C], F32, "y23", "placed0")
+        nc.scalar.copy(out=y23[:], in_=acc[:, C : 2 * C])
+        scatter(2, C, y22[:])
+        add_early(2)
         round_pair(nc.scalar.copy, 0, slice(0, T))
-        scatter(2, 3)
+        scatter(3, C, y23[:])
         parts = [slice(256, 512), slice(0, 128), slice(128, 256)]
         for cols in parts:
             nc.vector.tensor_tensor(

@@ -71,21 +71,21 @@ def tile_moe_adp_relu_kernel(
 
         nc.vector.memset(xs[:].bitcast(I32), 0)
         nc.vector.memset(wbs[:].bitcast(I32), 0)
-        make_identity(nc, ident[:])
-        load_x(0, nc.sync)
-        load_x(1, nc.scalar)
-        for q in range(4):
-            load_scales(xs, xs_rows, q, nc.sync if q < 2 else nc.scalar)
         nc.sync.dma_start(offsets[:], offs)
-        load_wa(0, nc.scalar)
-        for q, queue in enumerate((nc.sync, nc.scalar, nc.sync, nc.scalar)):
-            load_scales(was, was_rows, q, queue)
+        load_x(0, nc.sync)
+        load_x(1, nc.sync)
+        for q in range(4):
+            load_scales(xs, xs_rows, q, nc.scalar)
+        load_wa(0, nc.sync)
+        for q in range(4):
+            load_scales(was, was_rows, q, nc.scalar if q % 2 else nc.sync)
+        make_identity(nc, ident[:])
         nc.sync.dma_start(
             out=wbw[:].bitcast(I32).rearrange("p (e c) -> p e c", e=E),
             in_=wb_words.bitcast(I32).rearrange("e s p c -> p (e s) c"),
         )
         for q in range(4):
-            load_scales(wbs, wbs_rows, q, nc.gpsimd if q < 2 else nc.sync)
+            load_scales(wbs, wbs_rows, q, nc.scalar if q < 2 else nc.sync)
         load_wa(1, nc.sync)
         nc.sync.dma_start(out=gates[:], in_=gate)
         load_w(0)
@@ -240,8 +240,8 @@ def tile_moe_adp_relu_kernel(
         gather(1, 0)
         gather(1, 1)
         deal_wb(0)
-        gather(2, 0)
         layer_a(0, 0, "mmA", "trA")
+        gather(2, 0, "gw0_0")
         quant_h(0)
         gather(2, 1, "hcol0")
         layer_a(1, 0, "mmB", "trB")
@@ -262,7 +262,7 @@ def tile_moe_adp_relu_kernel(
         nc.scalar.copy(out=late_view[:, :, P:C], in_=acc[:, 2 * P : 4 * P].rearrange("p (d s) -> p d s", d=2))
         scatter(0, P, y1[:, 0:P])
         scatter(1, P, y1[:, P : 2 * P])
-        deal_wb(1, "y01", "y00")
+        deal_wb(1, None, "y00")
         layer_a(2, 0, "trB", "mmA")
         layer_a(2, 1, "mmC", "mmB")
         quant_h(2)

@@ -18,8 +18,13 @@ ACT = mybir.ActivationFunctionType
 ALU = mybir.AluOpType
 
 P = 128
-PASSES = K // 512
-GROUPS = [(0, 128), (128, 128), (256, 256)]
+PACK = 4
+K_PASS = P * PACK
+PASSES = K // K_PASS
+QUADS = 4
+LIST_ROWS = 16
+GROUPS = [(0, P), (P, P), (C, C)]
+W_PIECES = 4
 
 
 def tile_moe_adp_relu_kernel(
@@ -31,10 +36,10 @@ def tile_moe_adp_relu_kernel(
         ring = ctx.enter_context(tc.tile_pool(name="ring", bufs=2))
         psum = ctx.enter_context(tc.psum_pool(name="psum", bufs=1))
 
-        def held(shape, dtype, name, tag=None):
-            return keep.tile(shape, dtype, name=name, tag=tag or name, align_bytes=64)
+        def held(shape, dtype, name, after=None):
+            return keep.tile(shape, dtype, name=name, tag=after or name, align_bytes=64)
 
-        offsets = keep.tile([P, T // 16], U16, name="offsets")
+        offsets = keep.tile([P, T // LIST_ROWS], U16, name="offsets")
         xw = [held([P, T], I32, "xw%d" % s) for s in range(PASSES)]
         xs = held([P, PASSES * T], U8, "xs")
         waw = [held([P, PASSES * 2 * H], U8, "waw%d" % e) for e in range(E)]
@@ -42,27 +47,27 @@ def tile_moe_adp_relu_kernel(
         wbw = held([P, E * 2 * N], U8, "wbw")
         wbs = held([P, E * N], U8, "wbs")
         gates = held([P, T], F32, "gates")
-        wraw = [held([P, 4 * N], F32, "wraw%d" % s) for s in range(PASSES)]
+        wraw = [held([P, PACK * N], F32, "wraw%d" % s) for s in range(PASSES)]
         ident = held([P, P], F32, "ident")
 
-        def load_scales(tile, rows, q, queue):
+        def load_scales(tile, scale_rows, q, queue):
             queue.dma_start(
-                out=tile[32 * q : 32 * q + 4, :].bitcast(I32).rearrange("r (g c) -> r g c", c=128),
-                in_=rows[4 * q : 4 * q + 4],
+                out=tile[32 * q : 32 * q + 4, :].bitcast(I32).rearrange("r (g c) -> r g c", g=scale_rows.shape[1]),
+                in_=scale_rows[4 * q : 4 * q + 4],
             )
 
-        def load_x(s, queue):
-            queue.dma_start(out=xw[s][:], in_=x_words[s].rearrange("p n d -> p (n d)").bitcast(I32))
+        def load_x(s):
+            nc.sync.dma_start(out=xw[s][:], in_=x_words[s].rearrange("p n d -> p (n d)").bitcast(I32))
 
-        def load_wa(e, queue):
-            queue.dma_start(
+        def load_wa(e):
+            nc.sync.dma_start(
                 out=waw[e][:].bitcast(I32).rearrange("p (s c) -> p s c", s=PASSES),
                 in_=wa_words[e].bitcast(I32).rearrange("s p c -> p s c"),
             )
 
         def load_w(s):
             nc.sync.dma_start(
-                out=wraw[s][:], in_=w[512 * s : 512 * (s + 1), :].rearrange("(p j) n -> p (j n)", j=4)
+                out=wraw[s][:], in_=w[K_PASS * s : K_PASS * (s + 1), :].rearrange("(p j) n -> p (j n)", j=PACK)
             )
 
         xs_rows = x_scales.bitcast(I32).rearrange("s b c -> b s c")
@@ -72,21 +77,22 @@ def tile_moe_adp_relu_kernel(
         nc.vector.memset(xs[:].bitcast(I32), 0)
         nc.vector.memset(wbs[:].bitcast(I32), 0)
         nc.sync.dma_start(offsets[:], offs)
-        load_x(0, nc.sync)
-        load_x(1, nc.sync)
-        for q in range(4):
-            load_scales(xs, xs_rows, q, nc.scalar)
-        load_wa(0, nc.sync)
-        for q in range(4):
-            load_scales(was, was_rows, q, nc.scalar if q % 2 else nc.sync)
+        load_scales(was, was_rows, 0, nc.scalar)
+        load_x(0)
+        load_x(1)
+        for q, queue in enumerate((nc.scalar, nc.scalar, nc.scalar, nc.sync)):
+            load_scales(xs, xs_rows, q, queue)
+        load_wa(0)
+        for q, queue in ((2, nc.scalar), (1, nc.sync), (3, nc.scalar)):
+            load_scales(was, was_rows, q, queue)
         make_identity(nc, ident[:])
         nc.sync.dma_start(
             out=wbw[:].bitcast(I32).rearrange("p (e c) -> p e c", e=E),
             in_=wb_words.bitcast(I32).rearrange("e s p c -> p (e s) c"),
         )
-        for q in range(4):
-            load_scales(wbs, wbs_rows, q, nc.scalar if q < 2 else nc.sync)
-        load_wa(1, nc.sync)
+        for q, queue in enumerate((nc.scalar, nc.scalar, nc.sync, nc.sync)):
+            load_scales(wbs, wbs_rows, q, queue)
+        load_wa(1)
         nc.sync.dma_start(out=gates[:], in_=gate)
         load_w(0)
         load_w(1)
@@ -94,25 +100,25 @@ def tile_moe_adp_relu_kernel(
         gw = {}
         gs = {}
 
-        def gather(g, s, tag=None):
+        def gather(g, s, after=None):
             first, width = GROUPS[g]
-            lst = offsets[:, first // 16 : (first + width) // 16]
-            gw[g, s] = held([P, width], I32, "gw%d_%d" % (g, s), tag)
+            slots = offsets[:, first // LIST_ROWS : (first + width) // LIST_ROWS]
+            gw[g, s] = held([P, width], I32, "gw%d_%d" % (g, s), after)
             gs[g, s] = held([P, width], U8, "gs%d_%d" % (g, s))
-            nc.vector.tensor_copy(gw[g, s][:].bitcast(U32), xw[s][:].bitcast(U32).indirect(lst))
-            nc.vector.tensor_copy(gs[g, s][:], xs[:, s * T : (s + 1) * T].indirect(lst))
+            nc.vector.tensor_copy(gw[g, s][:].bitcast(U32), xw[s][:].bitcast(U32).indirect(slots))
+            nc.vector.tensor_copy(gs[g, s][:], xs[:, s * T : (s + 1) * T].indirect(slots))
 
-        hq = {}
         hcol = {}
+        hq = {}
 
-        def layer_a(g, b, bank, turn_bank):
+        def first_layer(g, b, bank, turn_bank):
             first, width = GROUPS[g]
             e = first // C
             cols = slice(b * P, (b + 1) * P)
-            acc = psum.tile([P, H], F32, name="acc", tag=bank)
+            sums = psum.tile([P, H], F32, name="h_sums", tag=bank)
             for s in range(PASSES):
                 nc.tensor.matmul_mx(
-                    out=acc[:],
+                    out=sums[:],
                     lhsT=gw[g, s][:, cols].bitcast(FP8X4),
                     lhsT_scale=gs[g, s][:, cols],
                     rhs=waw[e][:, s * 2 * H : (s + 1) * 2 * H].bitcast(FP4X4),
@@ -122,23 +128,23 @@ def tile_moe_adp_relu_kernel(
                 )
             hrow = ring.tile([P, H], BF16, name="hrow", align_bytes=64)
             nc.scalar.activation(
-                out=hrow[:].rearrange("s (u p e) -> s u p e", u=2, e=2),
-                in_=acc[:].rearrange("s (p u e) -> s u p e", u=2, e=2),
+                out=hrow[:].rearrange("j (u p r) -> j u p r", u=2, r=2),
+                in_=sums[:].rearrange("j (p u r) -> j u p r", u=2, r=2),
                 func=ACT.Relu,
             )
-            turned = psum.tile([P, 4 * P], F32, name="turned", tag=turn_bank)
+            turned = psum.tile([P, PACK * P], F32, name="h_turned", tag=turn_bank)
             for u in range(2):
                 nc.tensor.transpose(
                     turned[:, u * P : (u + 1) * P], hrow[:].bitcast(F32)[:, u * P : (u + 1) * P], ident[:]
                 )
             if b == 0:
-                hcol[g] = held([P, 4 * width], BF16, "hcol%d" % g)
+                hcol[g] = held([P, PACK * width], BF16, "hcol%d" % g)
             nc.scalar.copy(
-                out=hcol[g][:, 4 * P * b : 4 * P * (b + 1)].bitcast(F32).rearrange("p (s u) -> p s u", u=2),
-                in_=turned[:, 0 : 2 * P].rearrange("p (u s) -> p s u", u=2),
+                out=hcol[g][:, PACK * P * b : PACK * P * (b + 1)].bitcast(F32).rearrange("p (j u) -> p j u", u=2),
+                in_=turned[:, 0 : 2 * P].rearrange("p (u j) -> p j u", u=2),
             )
 
-        def quant_h(g):
+        def quantise_h(g):
             width = GROUPS[g][1]
             codes = held([P, width], U32, "hq%d" % g)
             scales = held([P, width], U8, "hs%d" % g)
@@ -148,26 +154,26 @@ def tile_moe_adp_relu_kernel(
         wbw_dealt = {}
         wbs_dealt = {}
 
-        def deal_wb(e, words_tag=None, scales_tag=None):
-            wbw_dealt[e] = held([P, 2 * N], U8, "wbw_dealt%d" % e, words_tag)
-            wbs_dealt[e] = held([P, N], U8, "wbs_dealt%d" % e, scales_tag)
+        def deal_wb(e, scales_after=None):
+            wbw_dealt[e] = held([P, 2 * N], U8, "wbw_dealt%d" % e)
+            wbs_dealt[e] = held([P, N], U8, "wbs_dealt%d" % e, scales_after)
             nc.vector.tensor_copy(
-                wbw_dealt[e][:].bitcast(U16).rearrange("p (d a b) -> p a d b", d=4, b=8),
-                wbw[:, e * 2 * N : (e + 1) * 2 * N].bitcast(U16).rearrange("p (a b d) -> p a d b", d=4, b=8),
+                wbw_dealt[e][:].bitcast(U16).rearrange("p (d a b) -> p a d b", d=PACK, b=8),
+                wbw[:, e * 2 * N : (e + 1) * 2 * N].bitcast(U16).rearrange("p (a b d) -> p a d b", d=PACK, b=8),
             )
             nc.vector.tensor_copy(
-                wbs_dealt[e][:].rearrange("p (d a b) -> p a d b", d=4, b=16),
-                wbs[:, e * N : (e + 1) * N].rearrange("p (a b d) -> p a d b", d=4, b=16),
+                wbs_dealt[e][:].rearrange("p (d a b) -> p a d b", d=PACK, b=16),
+                wbs[:, e * N : (e + 1) * N].rearrange("p (a b d) -> p a d b", d=PACK, b=16),
             )
 
-        def layer_b(g, ds, bank):
+        def second_layer(g, planes, bank):
             first, width = GROUPS[g]
             e = first // C
             codes, scales = hq[g]
-            acc = psum.tile([P, N], F32, name="yacc", tag=bank)
-            for i, d in enumerate(ds):
+            sums = psum.tile([P, N], F32, name="y_sums", tag=bank)
+            for i, d in enumerate(planes):
                 nc.tensor.matmul_mx(
-                    out=acc[:, i * width : (i + 1) * width],
+                    out=sums[:, i * width : (i + 1) * width],
                     lhsT=wbw_dealt[e][:, d * 2 * P : (d + 1) * 2 * P].bitcast(FP4X4),
                     lhsT_scale=wbs_dealt[e][:, d * P : (d + 1) * P],
                     rhs=codes[:].bitcast(FP8X4),
@@ -175,29 +181,29 @@ def tile_moe_adp_relu_kernel(
                     start=True,
                     stop=True,
                 )
-            return acc
+            return sums
 
         placed = {}
 
-        def scatter(d, first, values, tag=None):
+        def scatter(d, first, values, after=None):
             width = values.shape[1]
             if d not in placed:
-                placed[d] = held([P, T], F32, "placed%d" % d, tag)
-            lst = offsets[:, first // 16 : (first + width) // 16]
-            nc.vector.tensor_tensor(placed[d][:].indirect(lst), values, gates[:, first : first + width], ALU.mult)
+                placed[d] = held([P, T], F32, "placed%d" % d, after)
+            slots = offsets[:, first // LIST_ROWS : (first + width) // LIST_ROWS]
+            nc.vector.tensor_tensor(placed[d][:].indirect(slots), values, gates[:, first : first + width], ALU.mult)
 
-        wbf = [held([P, 4 * N], BF16, "wbf%d" % s) for s in range(PASSES)]
+        wbf = [held([P, PACK * N], BF16, "wbf%d" % s) for s in range(PASSES)]
         wq = [held([P, N], U32, "wq%d" % s) for s in range(PASSES)]
         wsc = [held([P, N], U8, "wsc%d" % s) for s in range(PASSES)]
 
-        def round_w(s, part):
-            ms = slice(32 * part, 32 * (part + 1))
+        def round_w(s, piece):
+            ms = slice(piece * P // W_PIECES, (piece + 1) * P // W_PIECES)
             nc.scalar.copy(
-                out=wbf[s][:].rearrange("p (d m j) -> p m d j", d=4, j=4)[:, ms],
-                in_=wraw[s][:].rearrange("p (j m d) -> p m d j", d=4, j=4)[:, ms],
+                out=wbf[s][:].rearrange("p (d m j) -> p m d j", d=PACK, j=PACK)[:, ms],
+                in_=wraw[s][:].rearrange("p (j m d) -> p m d j", d=PACK, j=PACK)[:, ms],
             )
 
-        def quant_w(s):
+        def quantise_w(s):
             nc.vector.quantize_mx(out=wq[s][:].bitcast(FP8X4), scales=wsc[s][:], in_=wbf[s][:])
 
         base = {}
@@ -216,99 +222,105 @@ def tile_moe_adp_relu_kernel(
                 )
 
         total = [held([P, 2 * T], F32, "total%d" % i) for i in range(2)]
-        rows = out_0.rearrange("(p d) t -> p d t", d=4)
+        out_planes = out_0.rearrange("(p d) t -> p d t", d=PACK)
 
         def total_of(d):
             return total[d // 2][:, (d % 2) * T : (d % 2 + 1) * T]
 
-        def add_early(d):
-            nc.vector.tensor_tensor(out=total_of(d), in0=base[d][:], in1=placed[d][:], op=ALU.add)
-            nc.sync.dma_start(out=rows[:, d, :], in_=total_of(d))
+        def add(d, tokens):
+            nc.vector.tensor_tensor(
+                out=total_of(d)[:, tokens], in0=base[d][:, tokens], in1=placed[d][:, tokens], op=ALU.add
+            )
+
+        def store(d):
+            nc.sync.dma_start(out=out_planes[:, d, :], in_=total_of(d))
 
         ow = held([P, T], U32, "ow")
         osc = held([P, T], U8, "osc")
-        obf = held([P, 4 * T], BF16, "obf")
+        obf = held([P, PACK * T], BF16, "obf")
 
-        def round_pair(copy, i, cols):
+        def round_pair(copy, i, tokens):
             copy(
-                out=obf[:].rearrange("p (t d) -> p t d", d=4)[:, cols, 2 * i : 2 * i + 2],
-                in_=total[i][:].rearrange("p (d t) -> p t d", d=2)[:, cols, :],
+                out=obf[:].rearrange("p (t d) -> p t d", d=PACK)[:, tokens, 2 * i : 2 * i + 2],
+                in_=total[i][:].rearrange("p (d t) -> p t d", d=2)[:, tokens, :],
             )
 
-        gather(0, 0)
-        gather(0, 1)
-        gather(1, 0)
-        gather(1, 1)
+        for g in range(2):
+            for s in range(PASSES):
+                gather(g, s)
         deal_wb(0)
-        layer_a(0, 0, "mmA", "trA")
-        gather(2, 0, "gw0_0")
-        quant_h(0)
-        gather(2, 1, "hcol0")
-        layer_a(1, 0, "mmB", "trB")
-        quant_h(1)
-        late = held([P, 2 * C], F32, "late")
-        late_view = late[:].rearrange("p (d s) -> p d s", d=2)
-        acc = layer_b(0, [0, 1, 2, 3], "mmC")
-        y00 = held([P, P], F32, "y00")
-        y01 = held([P, P], F32, "y01")
-        nc.scalar.copy(out=y00[:], in_=acc[:, 0:P])
-        scatter(0, 0, y00[:])
-        nc.scalar.copy(out=y01[:], in_=acc[:, P : 2 * P])
-        scatter(1, 0, y01[:])
-        nc.scalar.copy(out=late_view[:, :, 0:P], in_=acc[:, 2 * P : 4 * P].rearrange("p (d s) -> p d s", d=2))
-        acc = layer_b(1, [0, 1, 2, 3], "mmD")
-        y1 = held([P, 2 * P], F32, "y1")
-        nc.scalar.copy(out=y1[:], in_=acc[:, 0 : 2 * P])
-        nc.scalar.copy(out=late_view[:, :, P:C], in_=acc[:, 2 * P : 4 * P].rearrange("p (d s) -> p d s", d=2))
-        scatter(0, P, y1[:, 0:P])
-        scatter(1, P, y1[:, P : 2 * P])
-        deal_wb(1, None, "y00")
-        layer_a(2, 0, "trB", "mmA")
-        layer_a(2, 1, "mmC", "mmB")
-        quant_h(2)
-        scatter(2, 0, late[:, 0:C], "hcol2")
-        acc = layer_b(2, [0, 1], "mmC")
-        y2 = held([P, 2 * C], F32, "y2")
-        nc.scalar.copy(out=y2[:], in_=acc[:])
+        first_layer(0, 0, "bank0", "bank1")
+        gather(2, 0, after="gw0_0")
+        quantise_h(0)
+        gather(2, 1, after="hcol0")
+        first_layer(1, 0, "bank2", "bank3")
+        quantise_h(1)
+        y_late = held([P, 2 * C], F32, "y_late")
+        y_late_planes = y_late[:].rearrange("p (d j) -> p d j", d=2)
+        sums = second_layer(0, range(PACK), "bank4")
+        y_first = [held([P, P], F32, "y_first%d" % d) for d in range(2)]
+        for d in range(2):
+            nc.scalar.copy(out=y_first[d][:], in_=sums[:, d * P : (d + 1) * P])
+            scatter(d, 0, y_first[d][:])
+        nc.scalar.copy(out=y_late_planes[:, :, 0:P], in_=sums[:, 2 * P : 4 * P].rearrange("p (d j) -> p d j", d=2))
+        sums = second_layer(1, range(PACK), "bank5")
+        y_second = held([P, 2 * P], F32, "y_second")
+        nc.scalar.copy(out=y_second[:], in_=sums[:, 0 : 2 * P])
+        nc.scalar.copy(out=y_late_planes[:, :, P:C], in_=sums[:, 2 * P : 4 * P].rearrange("p (d j) -> p d j", d=2))
+        for d in range(2):
+            scatter(d, P, y_second[:, d * P : (d + 1) * P])
+
+        deal_wb(1, scales_after="y_first0")
+        first_layer(2, 0, "bank3", "bank0")
+        first_layer(2, 1, "bank4", "bank2")
+        quantise_h(2)
+        scatter(2, 0, y_late[:, 0:C], after="hcol2")
+        sums = second_layer(2, range(2), "bank4")
+        y_third = held([P, 2 * C], F32, "y_third")
+        nc.scalar.copy(out=y_third[:], in_=sums[:])
+
         for s in range(PASSES):
-            for part in range(4):
-                round_w(s, part)
-        quant_w(0)
-        scatter(0, C, y2[:, 0:C])
-        quant_w(1)
-        scatter(3, 0, late[:, C : 2 * C], "wbf1")
-        for d, bank in enumerate(("mmA", "mmB", "trA", "trB")):
+            for piece in range(W_PIECES):
+                round_w(s, piece)
+        quantise_w(0)
+        scatter(0, C, y_third[:, 0:C])
+        quantise_w(1)
+        scatter(3, 0, y_late[:, C : 2 * C], after="wbf1")
+        for d, bank in enumerate(("bank0", "bank2", "bank1", "bank3")):
             frozen(d, bank)
-        scatter(1, C, y2[:, C : 2 * C])
-        add_early(0)
-        add_early(1)
-        acc = layer_b(2, [2, 3], "mmD")
-        y22 = held([P, C], F32, "y22")
-        nc.scalar.copy(out=y22[:], in_=acc[:, 0:C])
-        y23 = held([P, C], F32, "y23", "placed0")
-        nc.scalar.copy(out=y23[:], in_=acc[:, C : 2 * C])
-        scatter(2, C, y22[:])
-        add_early(2)
-        round_pair(nc.scalar.copy, 0, slice(0, T))
-        scatter(3, C, y23[:])
-        parts = [slice(256, 512), slice(0, 128), slice(128, 256)]
-        for cols in parts:
-            nc.vector.tensor_tensor(
-                out=total_of(3)[:, cols], in0=base[3][:, cols], in1=placed[3][:, cols], op=ALU.add
-            )
-        nc.sync.dma_start(out=rows[:, 3, :], in_=total_of(3))
-        round_pair(nc.vector.tensor_copy, 1, parts[0])
-        round_pair(nc.scalar.copy, 1, parts[1])
-        round_pair(nc.vector.tensor_copy, 1, parts[2])
+        scatter(1, C, y_third[:, C : 2 * C])
+
+        all_tokens = slice(0, T)
+        for d in range(2):
+            add(d, all_tokens)
+            store(d)
+        sums = second_layer(2, range(2, PACK), "bank5")
+        y_plane2 = held([P, C], F32, "y_plane2")
+        nc.scalar.copy(out=y_plane2[:], in_=sums[:, 0:C])
+        y_plane3 = held([P, C], F32, "y_plane3", after="placed0")
+        nc.scalar.copy(out=y_plane3[:], in_=sums[:, C : 2 * C])
+        scatter(2, C, y_plane2[:])
+        add(2, all_tokens)
+        store(2)
+        round_pair(nc.scalar.copy, 0, all_tokens)
+        scatter(3, C, y_plane3[:])
+
+        first_quarter, second_quarter, upper_half = slice(0, T // 4), slice(T // 4, T // 2), slice(T // 2, T)
+        for tokens in (upper_half, first_quarter, second_quarter):
+            add(3, tokens)
+        store(3)
+        round_pair(nc.vector.tensor_copy, 1, upper_half)
+        round_pair(nc.scalar.copy, 1, first_quarter)
+        round_pair(nc.vector.tensor_copy, 1, second_quarter)
         words_out = out_1[0].rearrange("p n d -> p (n d)").bitcast(I32)
-        for first in (256, 0):
-            cols = slice(first, first + 256)
+        for tokens in (upper_half, slice(0, T // 2)):
             nc.vector.quantize_mx(
-                out=ow[:, cols].bitcast(FP8X4), scales=osc[:, cols], in_=obf[:, 4 * first : 4 * first + 1024]
+                out=ow[:, tokens].bitcast(FP8X4),
+                scales=osc[:, tokens],
+                in_=obf[:, PACK * tokens.start : PACK * tokens.stop],
             )
-            nc.sync.dma_start(out=words_out[:, cols], in_=ow[:, cols].bitcast(I32))
-        for q in range(4):
-            eng = nc.sync if q % 2 else nc.scalar
-            eng.dma_start(
+            nc.sync.dma_start(out=words_out[:, tokens], in_=ow[:, tokens].bitcast(I32))
+        for q, queue in enumerate((nc.scalar, nc.sync, nc.scalar, nc.sync)):
+            queue.dma_start(
                 out=out_2[0, 4 * q : 4 * q + 4, :].bitcast(I32), in_=osc[32 * q : 32 * q + 4, :].bitcast(I32)
             )

@@ -23,8 +23,8 @@ K_PASS = P * PACK
 PASSES = K // K_PASS
 QUADS = 4
 LIST_ROWS = 16
-GROUPS = [(0, P), (P, P), (C, C)]
 W_PIECES = 4
+REST = T - P
 
 
 def tile_moe_adp_relu_kernel(
@@ -33,7 +33,6 @@ def tile_moe_adp_relu_kernel(
     nc = tc.nc
     with ExitStack() as ctx:
         keep = ctx.enter_context(tc.tile_pool(name="keep", bufs=1))
-        ring = ctx.enter_context(tc.tile_pool(name="ring", bufs=2))
         psum = ctx.enter_context(tc.psum_pool(name="psum", bufs=1))
 
         def held(shape, dtype, name, after=None):
@@ -47,13 +46,13 @@ def tile_moe_adp_relu_kernel(
         wbw = held([P, E * 2 * N], U8, "wbw")
         wbs = held([P, E * N], U8, "wbs")
         gates = held([P, T], F32, "gates")
-        wraw = [held([P, PACK * N], F32, "wraw%d" % s) for s in range(PASSES)]
+        wraw = [[held([P, PACK * N // 2], F32, "wraw%d_%d" % (s, h)) for h in range(2)] for s in range(PASSES)]
         ident = held([P, P], F32, "ident")
 
         def load_scales(tile, scale_rows, q, queue):
             queue.dma_start(
-                out=tile[32 * q : 32 * q + 4, :].bitcast(I32).rearrange("r (g c) -> r g c", g=scale_rows.shape[1]),
-                in_=scale_rows[4 * q : 4 * q + 4],
+                out=tile[q:P:32, :].bitcast(I32).rearrange("r (g c) -> r g c", g=scale_rows.shape[1]),
+                in_=scale_rows[q:16:4],
             )
 
         def load_x(s):
@@ -65,9 +64,10 @@ def tile_moe_adp_relu_kernel(
                 in_=wa_words[e].bitcast(I32).rearrange("s p c -> p s c"),
             )
 
-        def load_w(s):
+        def load_w(s, h):
+            rows = w[K_PASS * s : K_PASS * (s + 1), :].rearrange("(p j) n -> p j n", j=PACK)
             nc.sync.dma_start(
-                out=wraw[s][:], in_=w[K_PASS * s : K_PASS * (s + 1), :].rearrange("(p j) n -> p (j n)", j=PACK)
+                out=wraw[s][h][:].rearrange("p (j n) -> p j n", j=PACK), in_=rows[:, :, h * N // 2 : (h + 1) * N // 2]
             )
 
         xs_rows = x_scales.bitcast(I32).rearrange("s b c -> b s c")
@@ -79,11 +79,11 @@ def tile_moe_adp_relu_kernel(
         nc.sync.dma_start(offsets[:], offs)
         load_scales(was, was_rows, 0, nc.scalar)
         load_x(0)
-        load_x(1)
-        for q, queue in enumerate((nc.scalar, nc.scalar, nc.scalar, nc.sync)):
+        for q, queue in enumerate((nc.scalar, nc.sync, nc.scalar, nc.scalar)):
             load_scales(xs, xs_rows, q, queue)
+        load_x(1)
         load_wa(0)
-        for q, queue in ((2, nc.scalar), (1, nc.sync), (3, nc.scalar)):
+        for q, queue in ((1, nc.scalar), (2, nc.sync), (3, nc.scalar)):
             load_scales(was, was_rows, q, queue)
         make_identity(nc, ident[:])
         nc.sync.dma_start(
@@ -94,39 +94,40 @@ def tile_moe_adp_relu_kernel(
             load_scales(wbs, wbs_rows, q, queue)
         load_wa(1)
         nc.sync.dma_start(out=gates[:], in_=gate)
-        load_w(0)
-        load_w(1)
+        load_w(0, 0)
+        load_w(0, 1)
+        load_w(1, 0)
+        load_w(1, 1)
 
-        gw = {}
-        gs = {}
+        def slots_of(first, width):
+            return offsets[:, first // LIST_ROWS : (first + width) // LIST_ROWS]
 
-        def gather(g, s, after=None):
-            first, width = GROUPS[g]
-            slots = offsets[:, first // LIST_ROWS : (first + width) // LIST_ROWS]
-            gw[g, s] = held([P, width], I32, "gw%d_%d" % (g, s), after)
-            gs[g, s] = held([P, width], U8, "gs%d_%d" % (g, s))
-            nc.vector.tensor_copy(gw[g, s][:].bitcast(U32), xw[s][:].bitcast(U32).indirect(slots))
-            nc.vector.tensor_copy(gs[g, s][:], xs[:, s * T : (s + 1) * T].indirect(slots))
+        def gather_words(s, first, width, name, after=None):
+            tile = held([P, width], I32, name, after)
+            nc.vector.tensor_copy(tile[:].bitcast(U32), xw[s][:].bitcast(U32).indirect(slots_of(first, width)))
+            return tile
 
-        hcol = {}
-        hq = {}
+        def gather_scales(s, first, width, name, after=None):
+            tile = held([P, width], U8, name, after)
+            nc.vector.tensor_copy(tile[:], xs[:, s * T : (s + 1) * T].indirect(slots_of(first, width)))
+            return tile
 
-        def first_layer(g, b, bank, turn_bank):
-            first, width = GROUPS[g]
-            e = first // C
-            cols = slice(b * P, (b + 1) * P)
+        def first_layer(e, words, scales, bank):
             sums = psum.tile([P, H], F32, name="h_sums", tag=bank)
             for s in range(PASSES):
                 nc.tensor.matmul_mx(
                     out=sums[:],
-                    lhsT=gw[g, s][:, cols].bitcast(FP8X4),
-                    lhsT_scale=gs[g, s][:, cols],
+                    lhsT=words[s].bitcast(FP8X4),
+                    lhsT_scale=scales[s],
                     rhs=waw[e][:, s * 2 * H : (s + 1) * 2 * H].bitcast(FP4X4),
                     rhs_scale=was[:, (e * PASSES + s) * H : (e * PASSES + s + 1) * H],
                     start=(s == 0),
                     stop=(s == PASSES - 1),
                 )
-            hrow = ring.tile([P, H], BF16, name="hrow", align_bytes=64)
+            return sums
+
+        def turn_h(sums, hcol, turn_bank, row_name):
+            hrow = held([P, H], BF16, "hrow", row_name)
             nc.scalar.activation(
                 out=hrow[:].rearrange("j (u p r) -> j u p r", u=2, r=2),
                 in_=sums[:].rearrange("j (p u r) -> j u p r", u=2, r=2),
@@ -137,26 +138,24 @@ def tile_moe_adp_relu_kernel(
                 nc.tensor.transpose(
                     turned[:, u * P : (u + 1) * P], hrow[:].bitcast(F32)[:, u * P : (u + 1) * P], ident[:]
                 )
-            if b == 0:
-                hcol[g] = held([P, PACK * width], BF16, "hcol%d" % g)
             nc.scalar.copy(
-                out=hcol[g][:, PACK * P * b : PACK * P * (b + 1)].bitcast(F32).rearrange("p (j u) -> p j u", u=2),
+                out=hcol.bitcast(F32).rearrange("p (j u) -> p j u", u=2),
                 in_=turned[:, 0 : 2 * P].rearrange("p (u j) -> p j u", u=2),
             )
 
-        def quantise_h(g):
-            width = GROUPS[g][1]
-            codes = held([P, width], U32, "hq%d" % g)
-            scales = held([P, width], U8, "hs%d" % g)
-            nc.vector.quantize_mx(out=codes[:].bitcast(FP8X4), scales=scales[:], in_=hcol[g][:])
-            hq[g] = (codes, scales)
+        def quantise_h(hcol, width, name):
+            codes = held([P, width], U32, "hq" + name)
+            scales = held([P, width], U8, "hs" + name)
+            nc.vector.quantize_mx(out=codes[:].bitcast(FP8X4), scales=scales[:], in_=hcol[:])
+            return codes, scales
 
         wbw_dealt = {}
         wbs_dealt = {}
 
-        def deal_wb(e, scales_after=None):
-            wbw_dealt[e] = held([P, 2 * N], U8, "wbw_dealt%d" % e)
-            wbs_dealt[e] = held([P, N], U8, "wbs_dealt%d" % e, scales_after)
+        def deal_wb(e, after=None):
+            dealt = held([P, 3 * N], U8, "wb_dealt%d" % e, after)
+            wbw_dealt[e] = dealt[:, 0 : 2 * N]
+            wbs_dealt[e] = dealt[:, 2 * N : 3 * N]
             nc.vector.tensor_copy(
                 wbw_dealt[e][:].bitcast(U16).rearrange("p (d a b) -> p a d b", d=PACK, b=8),
                 wbw[:, e * 2 * N : (e + 1) * 2 * N].bitcast(U16).rearrange("p (a b d) -> p a d b", d=PACK, b=8),
@@ -166,10 +165,9 @@ def tile_moe_adp_relu_kernel(
                 wbs[:, e * N : (e + 1) * N].rearrange("p (a b d) -> p a d b", d=PACK, b=16),
             )
 
-        def second_layer(g, planes, bank):
-            first, width = GROUPS[g]
-            e = first // C
-            codes, scales = hq[g]
+        def second_layer(e, hq, planes, bank):
+            codes, scales = hq
+            width = codes.shape[1]
             sums = psum.tile([P, N], F32, name="y_sums", tag=bank)
             for i, d in enumerate(planes):
                 nc.tensor.matmul_mx(
@@ -185,22 +183,27 @@ def tile_moe_adp_relu_kernel(
 
         placed = {}
 
-        def scatter(d, first, values, after=None):
-            width = values.shape[1]
+        def window(d, after=None):
             if d not in placed:
                 placed[d] = held([P, T], F32, "placed%d" % d, after)
-            slots = offsets[:, first // LIST_ROWS : (first + width) // LIST_ROWS]
-            nc.vector.tensor_tensor(placed[d][:].indirect(slots), values, gates[:, first : first + width], ALU.mult)
+            return placed[d]
 
-        wbf = [held([P, PACK * N], BF16, "wbf%d" % s) for s in range(PASSES)]
+        def scatter_gated(d, first, values, after=None):
+            width = values.shape[1]
+            nc.vector.tensor_tensor(
+                window(d, after)[:].indirect(slots_of(first, width)), values, gates[:, first : first + width], ALU.mult
+            )
+
+        wbf = {}
         wq = [held([P, N], U32, "wq%d" % s) for s in range(PASSES)]
         wsc = [held([P, N], U8, "wsc%d" % s) for s in range(PASSES)]
 
         def round_w(s, piece):
-            ms = slice(piece * P // W_PIECES, (piece + 1) * P // W_PIECES)
+            h, pair = divmod(piece, 2)
+            ms = slice(h * P // 2, (h + 1) * P // 2)
             nc.scalar.copy(
-                out=wbf[s][:].rearrange("p (d m j) -> p m d j", d=PACK, j=PACK)[:, ms],
-                in_=wraw[s][:].rearrange("p (j m d) -> p m d j", d=PACK, j=PACK)[:, ms],
+                out=wbf[s][:].rearrange("p (a e m j) -> p a m j e", a=2, e=2, j=PACK)[:, pair, ms],
+                in_=wraw[s][h][:].rearrange("p (j m a e) -> p a m j e", a=2, e=2, j=PACK)[:, pair],
             )
 
         def quantise_w(s):
@@ -245,65 +248,74 @@ def tile_moe_adp_relu_kernel(
                 in_=total[i][:].rearrange("p (d t) -> p t d", d=2)[:, tokens, :],
             )
 
-        for g in range(2):
-            for s in range(PASSES):
-                gather(g, s)
+        words0 = [gather_words(s, 0, P, "gw0_%d" % s) for s in range(PASSES)]
+        scales0 = [gather_scales(s, 0, P, "gs0_%d" % s) for s in range(PASSES)]
+        words1 = [gather_words(s, P, P, "gw1_%d" % s) for s in range(PASSES)]
+        scales1 = [gather_scales(s, P, P, "gs1_%d" % s) for s in range(PASSES)]
+        scales_b = [gather_scales(s, C, C, "gsb_%d" % s) for s in range(PASSES)]
+        sums0 = first_layer(0, [t[:] for t in words0], [t[:] for t in scales0], "bank0")
+        words2 = [gather_words(s, C, C, "gw2_%d" % s, "gw0_%d" % s) for s in range(PASSES)]
         deal_wb(0)
-        first_layer(0, 0, "bank0", "bank1")
-        gather(2, 0, after="gw0_0")
-        quantise_h(0)
-        gather(2, 1, after="hcol0")
-        first_layer(1, 0, "bank2", "bank3")
-        quantise_h(1)
-        y_late = held([P, 2 * C], F32, "y_late")
-        y_late_planes = y_late[:].rearrange("p (d j) -> p d j", d=2)
-        sums = second_layer(0, range(PACK), "bank4")
-        y_first = [held([P, P], F32, "y_first%d" % d) for d in range(2)]
-        for d in range(2):
-            nc.scalar.copy(out=y_first[d][:], in_=sums[:, d * P : (d + 1) * P])
-            scatter(d, 0, y_first[d][:])
-        nc.scalar.copy(out=y_late_planes[:, :, 0:P], in_=sums[:, 2 * P : 4 * P].rearrange("p (d j) -> p d j", d=2))
-        sums = second_layer(1, range(PACK), "bank5")
-        y_second = held([P, 2 * P], F32, "y_second")
-        nc.scalar.copy(out=y_second[:], in_=sums[:, 0 : 2 * P])
-        nc.scalar.copy(out=y_late_planes[:, :, P:C], in_=sums[:, 2 * P : 4 * P].rearrange("p (d j) -> p d j", d=2))
-        for d in range(2):
-            scatter(d, P, y_second[:, d * P : (d + 1) * P])
+        hcol0 = held([P, PACK * P], BF16, "hcol0")
+        turn_h(sums0, hcol0[:], "bank2", "hrow_a")
+        hq0 = quantise_h(hcol0, P, "0")
+        deal_wb(1, "hcol0")
+        sums1 = first_layer(0, [t[:] for t in words1], [t[:] for t in scales1], "bank1")
 
-        deal_wb(1, scales_after="y_first0")
-        first_layer(2, 0, "bank3", "bank0")
-        first_layer(2, 1, "bank4", "bank2")
-        quantise_h(2)
-        scatter(2, 0, y_late[:, 0:C], after="hcol2")
-        sums = second_layer(2, range(2), "bank4")
-        y_third = held([P, 2 * C], F32, "y_third")
-        nc.scalar.copy(out=y_third[:], in_=sums[:])
+        def late_first_layer(b, bank):
+            cols = slice(b * P, (b + 1) * P)
+            return first_layer(1, [t[:, cols] for t in words2], [t[:, cols] for t in scales_b], bank)
 
-        for s in range(PASSES):
+        hcol1 = held([P, PACK * P], BF16, "hcol1")
+        turn_h(sums1, hcol1[:], "bank3", "hrow_b")
+        hq1 = quantise_h(hcol1, P, "1")
+        ysums = second_layer(0, hq0, [0], "bank4")
+        y0_first = held([P, P], F32, "y0_first")
+        nc.scalar.copy(out=y0_first[:], in_=ysums[:, 0:P])
+        scatter_gated(0, 0, y0_first[:])
+
+        ysums0 = second_layer(0, hq0, [1, 2, 3], "bank5")
+        y0 = held([P, 3 * P], F32, "y0")
+        nc.scalar.copy(out=y0[:], in_=ysums0[:, 0 : 3 * P])
+        for d in range(1, PACK):
+            scatter_gated(d, 0, y0[:, (d - 1) * P : d * P])
+        ysums1 = second_layer(0, hq1, range(PACK), "bank2")
+        y1 = held([P, 2 * P], F32, "y1")
+        nc.scalar.copy(out=y1[:], in_=ysums1[:, 0 : 2 * P])
+        for d in range(2):
+            scatter_gated(d, P, y1[:, d * P : (d + 1) * P])
+        hcol2 = held([P, PACK * C], BF16, "hcol2")
+        for b, bank, turn_bank, row in ((0, "bank4", "bank6", "hrow_a"), (1, "bank5", "bank1", "hrow_b")):
+            turn_h(late_first_layer(b, bank), hcol2[:, PACK * P * b : PACK * P * (b + 1)], turn_bank, row)
+        hq2 = quantise_h(hcol2, C, "2")
+        y1_late = held([P, 2 * P], F32, "y1_late", "hrow_b")
+        nc.scalar.copy(out=y1_late[:], in_=ysums1[:, 2 * P : 4 * P])
+        for d in range(2, PACK):
+            scatter_gated(d, P, y1_late[:, (d - 2) * P : (d - 1) * P])
+
+        ysums = [second_layer(1, hq2, (0, 1), "bank7"), second_layer(1, hq2, (2, 3), "bank3")]
+
+        def late_scatter(d, after):
+            y = held([P, C], F32, "y2_%d" % d, after)
+            nc.scalar.copy(out=y[:], in_=ysums[d // 2][:, (d % 2) * C : (d % 2 + 1) * C])
+            scatter_gated(d, C, y[:])
+
+        late_scatter(0, None)
+        for s, after in enumerate(("hrow_a", "wraw0_0")):
+            wbf[s] = held([P, PACK * N], BF16, "wbf%d" % s, after)
             for piece in range(W_PIECES):
                 round_w(s, piece)
-        quantise_w(0)
-        scatter(0, C, y_third[:, 0:C])
-        quantise_w(1)
-        scatter(3, 0, y_late[:, C : 2 * C], after="wbf1")
-        for d, bank in enumerate(("bank0", "bank2", "bank1", "bank3")):
-            frozen(d, bank)
-        scatter(1, C, y_third[:, C : 2 * C])
+            quantise_w(s)
+            late_scatter(s + 1, "wraw%d_1" % s)
 
         all_tokens = slice(0, T)
-        for d in range(2):
+        for d, bank in enumerate(("bank0", "bank1", "bank4", "bank5")):
+            frozen(d, bank)
+        for d in range(3):
             add(d, all_tokens)
             store(d)
-        sums = second_layer(2, range(2, PACK), "bank5")
-        y_plane2 = held([P, C], F32, "y_plane2")
-        nc.scalar.copy(out=y_plane2[:], in_=sums[:, 0:C])
-        y_plane3 = held([P, C], F32, "y_plane3", after="placed0")
-        nc.scalar.copy(out=y_plane3[:], in_=sums[:, C : 2 * C])
-        scatter(2, C, y_plane2[:])
-        add(2, all_tokens)
-        store(2)
         round_pair(nc.scalar.copy, 0, all_tokens)
-        scatter(3, C, y_plane3[:])
+        late_scatter(3, "placed0")
 
         first_quarter, second_quarter, upper_half = slice(0, T // 4), slice(T // 4, T // 2), slice(T // 2, T)
         for tokens in (upper_half, first_quarter, second_quarter):
@@ -322,5 +334,5 @@ def tile_moe_adp_relu_kernel(
             nc.sync.dma_start(out=words_out[:, tokens], in_=ow[:, tokens].bitcast(I32))
         for q, queue in enumerate((nc.scalar, nc.sync, nc.scalar, nc.sync)):
             queue.dma_start(
-                out=out_2[0, 4 * q : 4 * q + 4, :].bitcast(I32), in_=osc[32 * q : 32 * q + 4, :].bitcast(I32)
+                out=out_2[0, q:16:4, :].bitcast(I32), in_=osc[q:P:32, :].bitcast(I32)
             )

@@ -301,7 +301,7 @@ def tile_moe_adp_relu_kernel(
             scatter_gated(d, C, y[:])
 
         late_scatter(0, None)
-        for s, after in enumerate(("hrow_a", "wraw0_0")):
+        for s, after in enumerate(("hcol1", "wraw0_0")):
             wbf[s] = held([P, PACK * N], BF16, "wbf%d" % s, after)
             for piece in range(W_PIECES):
                 round_w(s, piece)

@@ -194,30 +194,36 @@ def tile_moe_adp_relu_kernel(
                 window(d, after)[:].indirect(slots_of(first, width)), values, gates[:, first : first + width], ALU.mult
             )
 
-        wbf = {}
-        wq = [held([P, N], U32, "wq%d" % s) for s in range(PASSES)]
-        wsc = [held([P, N], U8, "wsc%d" % s) for s in range(PASSES)]
+        def scatter_plain(d, first, values):
+            nc.vector.tensor_copy(window(d)[:].indirect(slots_of(first, values.shape[1])), values)
 
-        def round_w(s, piece):
-            h, pair = divmod(piece, 2)
-            ms = slice(h * P // 2, (h + 1) * P // 2)
-            nc.scalar.copy(
-                out=wbf[s][:].rearrange("p (a e m j) -> p a m j e", a=2, e=2, j=PACK)[:, pair, ms],
-                in_=wraw[s][h][:].rearrange("p (j m a e) -> p a m j e", a=2, e=2, j=PACK)[:, pair],
-            )
+        wq = {}
 
-        def quantise_w(s):
-            nc.vector.quantize_mx(out=wq[s][:].bitcast(FP8X4), scales=wsc[s][:], in_=wbf[s][:])
+        def prepare_w(pair, after):
+            rounded = held([P, PACK * N], BF16, "wbf%d" % pair, after)
+            view = rounded[:].rearrange("p (s e m j) -> p s m j e", s=PASSES, e=2, j=PACK)
+            for s in range(PASSES):
+                for h in range(2):
+                    nc.scalar.copy(
+                        out=view[:, s, h * P // 2 : (h + 1) * P // 2],
+                        in_=wraw[s][h][:].rearrange("p (j m a e) -> p a m j e", a=2, e=2, j=PACK)[:, pair],
+                    )
+            codes = held([P, N], U32, "wq%d" % pair)
+            scales = held([P, N], U8, "wsc%d" % pair)
+            nc.vector.quantize_mx(out=codes[:].bitcast(FP8X4), scales=scales[:], in_=rounded[:])
+            wq[pair] = (codes, scales)
 
         base = {}
 
         def frozen(d, bank):
+            codes, scales = wq[d // 2]
             base[d] = psum.tile([P, T], F32, name="base%d" % d, tag=bank)
             for s in range(PASSES):
+                cols = slice((2 * s + d % 2) * P, (2 * s + d % 2 + 1) * P)
                 nc.tensor.matmul_mx(
                     out=base[d][:],
-                    lhsT=wq[s][:, d * P : (d + 1) * P].bitcast(FP8X4),
-                    lhsT_scale=wsc[s][:, d * P : (d + 1) * P],
+                    lhsT=codes[:, cols].bitcast(FP8X4),
+                    lhsT_scale=scales[:, cols],
                     rhs=xw[s][:].bitcast(FP8X4),
                     rhs_scale=xs[:, s * T : (s + 1) * T],
                     start=(s == 0),
@@ -294,33 +300,46 @@ def tile_moe_adp_relu_kernel(
             scatter_gated(d, P, y1_late[:, (d - 2) * P : (d - 1) * P])
 
         ysums = [second_layer(1, hq2, (0, 1), "bank7"), second_layer(1, hq2, (2, 3), "bank3")]
+        late_gates = gates[:, C : 2 * C]
 
-        def late_scatter(d, after):
-            y = held([P, C], F32, "y2_%d" % d, after)
-            nc.scalar.copy(out=y[:], in_=ysums[d // 2][:, (d % 2) * C : (d % 2 + 1) * C])
-            scatter_gated(d, C, y[:])
-
-        late_scatter(0, None)
-        for s, after in enumerate(("hcol1", "wraw0_0")):
-            wbf[s] = held([P, PACK * N], BF16, "wbf%d" % s, after)
-            for piece in range(W_PIECES):
-                round_w(s, piece)
-            quantise_w(s)
-            late_scatter(s + 1, "wraw%d_1" % s)
+        def add_aside(d):
+            base_sb = held([P, T], F32, "base_sb%d" % d)
+            nc.scalar.copy(out=base_sb[:], in_=base[d][:])
+            nc.gpsimd.tensor_tensor(out=total_of(d), in0=base_sb[:], in1=placed[d][:], op=ALU.add)
 
         all_tokens = slice(0, T)
-        for d, bank in enumerate(("bank0", "bank1", "bank4", "bank5")):
-            frozen(d, bank)
-        for d in range(3):
-            add(d, all_tokens)
-            store(d)
+        prepare_w(0, "hcol1")
+        y2_0 = held([P, C], F32, "y2_0", None)
+        nc.scalar.copy(out=y2_0[:], in_=ysums[0][:, 0:C])
+        scatter_gated(0, C, y2_0[:])
+        frozen(0, "bank0")
+        frozen(1, "bank1")
+        prepare_w(1, "hcol2")
+        add_aside(0)
+        store(0)
+
+        gated = held([P, 3 * C], F32, "gated", "wraw1_1")
+        for d in range(1, PACK):
+            nc.vector.tensor_tensor(
+                out=gated[:, (d - 1) * C : d * C],
+                in0=ysums[d // 2][:, (d % 2) * C : (d % 2 + 1) * C],
+                in1=late_gates,
+                op=ALU.mult,
+            )
+        frozen(2, "bank4")
+        frozen(3, "bank5")
+        scatter_plain(1, C, gated[:, 0:C])
+        add_aside(1)
+        store(1)
+        scatter_plain(2, C, gated[:, C : 2 * C])
+        add_aside(2)
         round_pair(nc.scalar.copy, 0, all_tokens)
-        late_scatter(3, "placed0")
+        scatter_plain(3, C, gated[:, 2 * C : 3 * C])
 
         first_quarter, second_quarter, upper_half = slice(0, T // 4), slice(T // 4, T // 2), slice(T // 2, T)
         for tokens in (upper_half, first_quarter, second_quarter):
             add(3, tokens)
-        store(3)
+        nc.sync.dma_start(out=out_planes[:, 2:4, :], in_=total[1][:].rearrange("p (d t) -> p d t", d=2))
         round_pair(nc.vector.tensor_copy, 1, upper_half)
         round_pair(nc.scalar.copy, 1, first_quarter)
         round_pair(nc.vector.tensor_copy, 1, second_quarter)

@@ -208,6 +208,9 @@ def tile_moe_adp_relu_kernel(
                         out=view[:, s, h * P // 2 : (h + 1) * P // 2],
                         in_=wraw[s][h][:].rearrange("p (j m a e) -> p a m j e", a=2, e=2, j=PACK)[:, pair],
                     )
+            return rounded
+
+        def quantise_w(pair, rounded):
             codes = held([P, N], U32, "wq%d" % pair)
             scales = held([P, N], U8, "wsc%d" % pair)
             nc.vector.quantize_mx(out=codes[:].bitcast(FP8X4), scales=scales[:], in_=rounded[:])
@@ -230,7 +233,7 @@ def tile_moe_adp_relu_kernel(
                     stop=(s == PASSES - 1),
                 )
 
-        total = [held([P, 2 * T], F32, "total%d" % i) for i in range(2)]
+        total = {1: held([P, 2 * T], F32, "total1")}
         out_planes = out_0.rearrange("(p d) t -> p d t", d=PACK)
 
         def total_of(d):
@@ -308,33 +311,41 @@ def tile_moe_adp_relu_kernel(
             nc.gpsimd.tensor_tensor(out=total_of(d), in0=base_sb[:], in1=placed[d][:], op=ALU.add)
 
         all_tokens = slice(0, T)
-        prepare_w(0, "hcol1")
+        quantise_w(0, prepare_w(0, "hcol1"))
         y2_0 = held([P, C], F32, "y2_0", None)
         nc.scalar.copy(out=y2_0[:], in_=ysums[0][:, 0:C])
         scatter_gated(0, C, y2_0[:])
         frozen(0, "bank0")
         frozen(1, "bank1")
-        prepare_w(1, "hcol2")
+        rounded = prepare_w(1, "hcol2")
+
+        gated = [held([P, C], F32, "gated1", "wraw1_1")]
+        nc.vector.tensor_tensor(out=gated[0][:], in0=ysums[0][:, C : 2 * C], in1=late_gates, op=ALU.mult)
+        quantise_w(1, rounded)
+        aside = held([P, 2 * T + 2 * C], F32, "aside", "hcol2")
+        total[0] = aside[:, 0 : 2 * T]
+        gated.extend([aside[:, 2 * T : 2 * T + C], aside[:, 2 * T + C : 2 * T + 2 * C]])
+        y2_late = held([P, 2 * C], F32, "y2_late", "wraw1_0")
+        nc.scalar.copy(out=y2_late[:], in_=ysums[1][:])
+
+        def gate_aside(d):
+            nc.gpsimd.tensor_tensor(
+                out=gated[d - 1][:], in0=y2_late[:, (d - 2) * C : (d - 1) * C], in1=late_gates, op=ALU.mult
+            )
+
+        gate_aside(2)
         add_aside(0)
         store(0)
-
-        gated = held([P, 3 * C], F32, "gated", "wraw1_1")
-        for d in range(1, PACK):
-            nc.vector.tensor_tensor(
-                out=gated[:, (d - 1) * C : d * C],
-                in0=ysums[d // 2][:, (d % 2) * C : (d % 2 + 1) * C],
-                in1=late_gates,
-                op=ALU.mult,
-            )
+        gate_aside(3)
         frozen(2, "bank4")
         frozen(3, "bank5")
-        scatter_plain(1, C, gated[:, 0:C])
+        scatter_plain(1, C, gated[0][:])
         add_aside(1)
         store(1)
-        scatter_plain(2, C, gated[:, C : 2 * C])
+        scatter_plain(2, C, gated[1][:])
         add_aside(2)
         round_pair(nc.scalar.copy, 0, all_tokens)
-        scatter_plain(3, C, gated[:, 2 * C : 3 * C])
+        scatter_plain(3, C, gated[2][:])
 
         first_quarter, second_quarter, upper_half = slice(0, T // 4), slice(T // 4, T // 2), slice(T // 2, T)
         for tokens in (upper_half, first_quarter, second_quarter):

@@ -86,12 +86,12 @@ def tile_moe_adp_relu_kernel(
         for q, queue in ((1, nc.scalar), (2, nc.sync), (3, nc.scalar)):
             load_scales(was, was_rows, q, queue)
         make_identity(nc, ident[:])
+        for q, queue in enumerate((nc.scalar, nc.scalar, nc.sync, nc.sync)):
+            load_scales(wbs, wbs_rows, q, queue)
         nc.sync.dma_start(
             out=wbw[:].bitcast(I32).rearrange("p (e c) -> p e c", e=E),
             in_=wb_words.bitcast(I32).rearrange("e s p c -> p (e s) c"),
         )
-        for q, queue in enumerate((nc.scalar, nc.scalar, nc.sync, nc.sync)):
-            load_scales(wbs, wbs_rows, q, queue)
         load_wa(1)
         nc.sync.dma_start(out=gates[:], in_=gate)
         load_w(0, 0)
@@ -126,13 +126,15 @@ def tile_moe_adp_relu_kernel(
                 )
             return sums
 
-        def turn_h(sums, hcol, turn_bank, row_name):
+        def turn_h(parts, hcol, turn_bank, row_name):
             hrow = held([P, H], BF16, "hrow", row_name)
-            nc.scalar.activation(
-                out=hrow[:].rearrange("j (u p r) -> j u p r", u=2, r=2),
-                in_=sums[:].rearrange("j (p u r) -> j u p r", u=2, r=2),
-                func=ACT.Relu,
-            )
+            span = P // len(parts)
+            for i, part in enumerate(parts):
+                nc.scalar.activation(
+                    out=hrow[:].rearrange("j (u p r) -> j u p r", u=2, r=2)[:, :, i * span : (i + 1) * span],
+                    in_=part.rearrange("j (p u r) -> j u p r", u=2, r=2),
+                    func=ACT.Relu,
+                )
             turned = psum.tile([P, PACK * P], F32, name="h_turned", tag=turn_bank)
             for u in range(2):
                 nc.tensor.transpose(
@@ -153,14 +155,14 @@ def tile_moe_adp_relu_kernel(
         wbs_dealt = {}
 
         def deal_wb(e, after=None):
-            dealt = held([P, 3 * N], U8, "wb_dealt%d" % e, after)
+            dealt = held([P, 2 * N], U8, "wb_dealt%d" % e, after)
             wbw_dealt[e] = dealt[:, 0 : 2 * N]
-            wbs_dealt[e] = dealt[:, 2 * N : 3 * N]
+            wbs_dealt[e] = held([P, N], U8, "wbs_dealt%d" % e)[:]
             nc.vector.tensor_copy(
                 wbw_dealt[e][:].bitcast(U16).rearrange("p (d a b) -> p a d b", d=PACK, b=8),
                 wbw[:, e * 2 * N : (e + 1) * 2 * N].bitcast(U16).rearrange("p (a b d) -> p a d b", d=PACK, b=8),
             )
-            nc.vector.tensor_copy(
+            nc.gpsimd.tensor_copy(
                 wbs_dealt[e][:].rearrange("p (d a b) -> p a d b", d=PACK, b=16),
                 wbs[:, e * N : (e + 1) * N].rearrange("p (a b d) -> p a d b", d=PACK, b=16),
             )
@@ -199,16 +201,13 @@ def tile_moe_adp_relu_kernel(
 
         wq = {}
 
-        def prepare_w(pair, after):
-            rounded = held([P, PACK * N], BF16, "wbf%d" % pair, after)
+        def round_w(rounded, pair, s):
             view = rounded[:].rearrange("p (s e m j) -> p s m j e", s=PASSES, e=2, j=PACK)
-            for s in range(PASSES):
-                for h in range(2):
-                    nc.scalar.copy(
-                        out=view[:, s, h * P // 2 : (h + 1) * P // 2],
-                        in_=wraw[s][h][:].rearrange("p (j m a e) -> p a m j e", a=2, e=2, j=PACK)[:, pair],
-                    )
-            return rounded
+            for h in range(2):
+                nc.scalar.copy(
+                    out=view[:, s, h * P // 2 : (h + 1) * P // 2],
+                    in_=wraw[s][h][:].rearrange("p (j m a e) -> p a m j e", a=2, e=2, j=PACK)[:, pair],
+                )
 
         def quantise_w(pair, rounded):
             codes = held([P, N], U32, "wq%d" % pair)
@@ -257,26 +256,54 @@ def tile_moe_adp_relu_kernel(
                 in_=total[i][:].rearrange("p (d t) -> p t d", d=2)[:, tokens, :],
             )
 
+        unread = psum.tile([P, T], F32, name="unread", tag="bank6")
+        for i in range(2):
+            nc.tensor.matmul_mx(
+                out=unread[:],
+                lhsT=xw[0][:, 0:P].bitcast(FP8X4),
+                lhsT_scale=xs[:, 0:P],
+                rhs=xw[0][:].bitcast(FP8X4),
+                rhs_scale=xs[:, 0:T],
+                start=True,
+                stop=True,
+            )
+
         words0 = [gather_words(s, 0, P, "gw0_%d" % s) for s in range(PASSES)]
         scales0 = [gather_scales(s, 0, P, "gs0_%d" % s) for s in range(PASSES)]
         words1 = [gather_words(s, P, P, "gw1_%d" % s) for s in range(PASSES)]
         scales1 = [gather_scales(s, P, P, "gs1_%d" % s) for s in range(PASSES)]
         scales_b = [gather_scales(s, C, C, "gsb_%d" % s) for s in range(PASSES)]
-        sums0 = first_layer(0, [t[:] for t in words0], [t[:] for t in scales0], "bank0")
-        words2 = [gather_words(s, C, C, "gw2_%d" % s, "gw0_%d" % s) for s in range(PASSES)]
-        deal_wb(0)
+        halves = []
+        for half, bank in enumerate(("bank0", "bank7")):
+            sums = psum.tile([P, H // 2], F32, name="h_half", tag=bank)
+            for i in range(2):
+                first = half * H // 2 + i * P
+                for s in range(PASSES):
+                    nc.tensor.matmul_mx(
+                        out=sums[:, i * P : (i + 1) * P],
+                        lhsT=words0[s][:].bitcast(FP8X4),
+                        lhsT_scale=scales0[s][:],
+                        rhs=waw[0][:, 2 * (s * H + first) : 2 * (s * H + first + P)].bitcast(FP4X4),
+                        rhs_scale=was[:, s * H + first : s * H + first + P],
+                        start=(s == 0),
+                        stop=(s == PASSES - 1),
+                    )
+            halves.append(sums[:])
+        words2 = [gather_words(0, C, C, "gw2_0", "gw0_0")]
         hcol0 = held([P, PACK * P], BF16, "hcol0")
-        turn_h(sums0, hcol0[:], "bank2", "hrow_a")
+        turn_h(halves, hcol0[:], "bank2", "hrow_a")
         hq0 = quantise_h(hcol0, P, "0")
-        deal_wb(1, "hcol0")
+        words2.append(gather_words(1, C, C, "gw2_1", "hcol0"))
         sums1 = first_layer(0, [t[:] for t in words1], [t[:] for t in scales1], "bank1")
+        deal_wb(0, "gw1_0")
+        deal_wb(1, "gw1_1")
 
         def late_first_layer(b, bank):
             cols = slice(b * P, (b + 1) * P)
             return first_layer(1, [t[:, cols] for t in words2], [t[:, cols] for t in scales_b], bank)
 
         hcol1 = held([P, PACK * P], BF16, "hcol1")
-        turn_h(sums1, hcol1[:], "bank3", "hrow_b")
+        turn_h([sums1[:]], hcol1[:], "bank3", "hrow_b")
         hq1 = quantise_h(hcol1, P, "1")
         ysums = second_layer(0, hq0, [0], "bank4")
         y0_first = held([P, P], F32, "y0_first")
@@ -295,7 +322,7 @@ def tile_moe_adp_relu_kernel(
             scatter_gated(d, P, y1[:, d * P : (d + 1) * P])
         hcol2 = held([P, PACK * C], BF16, "hcol2")
         for b, bank, turn_bank, row in ((0, "bank4", "bank6", "hrow_a"), (1, "bank5", "bank1", "hrow_b")):
-            turn_h(late_first_layer(b, bank), hcol2[:, PACK * P * b : PACK * P * (b + 1)], turn_bank, row)
+            turn_h([late_first_layer(b, bank)[:]], hcol2[:, PACK * P * b : PACK * P * (b + 1)], turn_bank, row)
         hq2 = quantise_h(hcol2, C, "2")
         y1_late = held([P, 2 * P], F32, "y1_late", "hrow_b")
         nc.scalar.copy(out=y1_late[:], in_=ysums1[:, 2 * P : 4 * P])
@@ -311,18 +338,23 @@ def tile_moe_adp_relu_kernel(
             nc.gpsimd.tensor_tensor(out=total_of(d), in0=base_sb[:], in1=placed[d][:], op=ALU.add)
 
         all_tokens = slice(0, T)
-        quantise_w(0, prepare_w(0, "hcol1"))
-        y2_0 = held([P, C], F32, "y2_0", None)
-        nc.scalar.copy(out=y2_0[:], in_=ysums[0][:, 0:C])
-        scatter_gated(0, C, y2_0[:])
+        rounded = held([P, PACK * N], BF16, "wbf0", "hq0")
+        for s in range(PASSES):
+            round_w(rounded, 0, s)
+        quantise_w(0, rounded)
         frozen(0, "bank0")
         frozen(1, "bank1")
-        rounded = prepare_w(1, "hcol2")
+        rounded = held([P, PACK * N], BF16, "wbf1", "hrow_a")
+        round_w(rounded, 1, 0)
+        y2_0 = held([P, C], F32, "y2_0", "wraw0_0")
+        nc.scalar.copy(out=y2_0[:], in_=ysums[0][:, 0:C])
+        scatter_gated(0, C, y2_0[:])
+        round_w(rounded, 1, 1)
 
         gated = [held([P, C], F32, "gated1", "wraw1_1")]
         nc.vector.tensor_tensor(out=gated[0][:], in0=ysums[0][:, C : 2 * C], in1=late_gates, op=ALU.mult)
         quantise_w(1, rounded)
-        aside = held([P, 2 * T + 2 * C], F32, "aside", "hcol2")
+        aside = held([P, 2 * T + 2 * C], F32, "aside", "hrow_a")
         total[0] = aside[:, 0 : 2 * T]
         gated.extend([aside[:, 2 * T : 2 * T + C], aside[:, 2 * T + C : 2 * T + 2 * C]])
         y2_late = held([P, 2 * C], F32, "y2_late", "wraw1_0")

@@ -128,13 +128,15 @@ def tile_moe_adp_relu_kernel(
 
         def turn_h(parts, hcol, turn_bank, row_name):
             hrow = held([P, H], BF16, "hrow", row_name)
-            span = P // len(parts)
-            for i, part in enumerate(parts):
+            first = 0
+            for part in parts:
+                span = part.shape[1] // PACK
                 nc.scalar.activation(
-                    out=hrow[:].rearrange("j (u p r) -> j u p r", u=2, r=2)[:, :, i * span : (i + 1) * span],
+                    out=hrow[:].rearrange("j (u p r) -> j u p r", u=2, r=2)[:, :, first : first + span],
                     in_=part.rearrange("j (p u r) -> j u p r", u=2, r=2),
                     func=ACT.Relu,
                 )
+                first = first + span
             turned = psum.tile([P, PACK * P], F32, name="h_turned", tag=turn_bank)
             for u in range(2):
                 nc.tensor.transpose(
@@ -151,21 +153,19 @@ def tile_moe_adp_relu_kernel(
             nc.vector.quantize_mx(out=codes[:].bitcast(FP8X4), scales=scales[:], in_=hcol[:])
             return codes, scales
 
-        wbw_dealt = {}
-        wbs_dealt = {}
-
-        def deal_wb(e, after=None):
-            dealt = held([P, 2 * N], U8, "wb_dealt%d" % e, after)
-            wbw_dealt[e] = dealt[:, 0 : 2 * N]
-            wbs_dealt[e] = held([P, N], U8, "wbs_dealt%d" % e)[:]
+        def deal_wb(after):
+            words = held([P, E * 2 * N], U8, "wbw_dealt", after)
+            scales = held([P, E * N], U8, "wbs_dealt")
             nc.vector.tensor_copy(
-                wbw_dealt[e][:].bitcast(U16).rearrange("p (d a b) -> p a d b", d=PACK, b=8),
-                wbw[:, e * 2 * N : (e + 1) * 2 * N].bitcast(U16).rearrange("p (a b d) -> p a d b", d=PACK, b=8),
+                words[:].bitcast(U16).rearrange("p (e d a b) -> p e a d b", e=E, d=PACK, b=8),
+                wbw[:].bitcast(U16).rearrange("p (e a b d) -> p e a d b", e=E, d=PACK, b=8),
             )
-            nc.gpsimd.tensor_copy(
-                wbs_dealt[e][:].rearrange("p (d a b) -> p a d b", d=PACK, b=16),
-                wbs[:, e * N : (e + 1) * N].rearrange("p (a b d) -> p a d b", d=PACK, b=16),
-            )
+            for e in range(E):
+                nc.gpsimd.tensor_copy(
+                    scales[:, e * N : (e + 1) * N].rearrange("p (d a b) -> p a d b", d=PACK, b=16),
+                    wbs[:, e * N : (e + 1) * N].rearrange("p (a b d) -> p a d b", d=PACK, b=16),
+                )
+            return words, scales
 
         def second_layer(e, hq, planes, bank):
             codes, scales = hq
@@ -174,8 +174,8 @@ def tile_moe_adp_relu_kernel(
             for i, d in enumerate(planes):
                 nc.tensor.matmul_mx(
                     out=sums[:, i * width : (i + 1) * width],
-                    lhsT=wbw_dealt[e][:, d * 2 * P : (d + 1) * 2 * P].bitcast(FP4X4),
-                    lhsT_scale=wbs_dealt[e][:, d * P : (d + 1) * P],
+                    lhsT=wbw_dealt[:, 2 * (e * N + d * P) : 2 * (e * N + (d + 1) * P)].bitcast(FP4X4),
+                    lhsT_scale=wbs_dealt[:, e * N + d * P : e * N + (d + 1) * P],
                     rhs=codes[:].bitcast(FP8X4),
                     rhs_scale=scales[:],
                     start=True,
@@ -270,37 +270,37 @@ def tile_moe_adp_relu_kernel(
 
         words0 = [gather_words(s, 0, P, "gw0_%d" % s) for s in range(PASSES)]
         scales0 = [gather_scales(s, 0, P, "gs0_%d" % s) for s in range(PASSES)]
-        words1 = [gather_words(s, P, P, "gw1_%d" % s) for s in range(PASSES)]
+        words_mid = gather_words(0, P, C, "gw_mid")
+        words1 = [words_mid[:, 0:P], gather_words(1, P, P, "gw1_1")]
         scales1 = [gather_scales(s, P, P, "gs1_%d" % s) for s in range(PASSES)]
         scales_b = [gather_scales(s, C, C, "gsb_%d" % s) for s in range(PASSES)]
-        halves = []
-        for half, bank in enumerate(("bank0", "bank7")):
-            sums = psum.tile([P, H // 2], F32, name="h_half", tag=bank)
-            for i in range(2):
-                first = half * H // 2 + i * P
+        parts = []
+        for chunks, bank in (((0, 1), "bank0"), ((2,), "bank7"), ((3,), "bank5")):
+            sums = psum.tile([P, len(chunks) * P], F32, name="h_part", tag=bank)
+            for i, chunk in enumerate(chunks):
                 for s in range(PASSES):
+                    first = s * H + chunk * P
                     nc.tensor.matmul_mx(
                         out=sums[:, i * P : (i + 1) * P],
                         lhsT=words0[s][:].bitcast(FP8X4),
                         lhsT_scale=scales0[s][:],
-                        rhs=waw[0][:, 2 * (s * H + first) : 2 * (s * H + first + P)].bitcast(FP4X4),
-                        rhs_scale=was[:, s * H + first : s * H + first + P],
+                        rhs=waw[0][:, 2 * first : 2 * (first + P)].bitcast(FP4X4),
+                        rhs_scale=was[:, first : first + P],
                         start=(s == 0),
                         stop=(s == PASSES - 1),
                     )
-            halves.append(sums[:])
-        words2 = [gather_words(0, C, C, "gw2_0", "gw0_0")]
+            parts.append(sums[:])
+        late_first = [words_mid[:, P:C], gather_words(0, C + P, P, "gw3_0", "gw0_0")[:]]
         hcol0 = held([P, PACK * P], BF16, "hcol0")
-        turn_h(halves, hcol0[:], "bank2", "hrow_a")
+        turn_h(parts, hcol0[:], "bank2", "hrow_a")
         hq0 = quantise_h(hcol0, P, "0")
-        words2.append(gather_words(1, C, C, "gw2_1", "hcol0"))
+        late_second = gather_words(1, C, C, "gw2_1", "hcol0")
         sums1 = first_layer(0, [t[:] for t in words1], [t[:] for t in scales1], "bank1")
-        deal_wb(0, "gw1_0")
-        deal_wb(1, "gw1_1")
+        wbw_dealt, wbs_dealt = deal_wb("gw1_1")
 
         def late_first_layer(b, bank):
             cols = slice(b * P, (b + 1) * P)
-            return first_layer(1, [t[:, cols] for t in words2], [t[:, cols] for t in scales_b], bank)
+            return first_layer(1, [late_first[b], late_second[:, cols]], [t[:, cols] for t in scales_b], bank)
 
         hcol1 = held([P, PACK * P], BF16, "hcol1")
         turn_h([sums1[:]], hcol1[:], "bank3", "hrow_b")
@@ -360,15 +360,14 @@ def tile_moe_adp_relu_kernel(
         y2_late = held([P, 2 * C], F32, "y2_late", "wraw1_0")
         nc.scalar.copy(out=y2_late[:], in_=ysums[1][:])
 
-        def gate_aside(d):
-            nc.gpsimd.tensor_tensor(
-                out=gated[d - 1][:], in0=y2_late[:, (d - 2) * C : (d - 1) * C], in1=late_gates, op=ALU.mult
-            )
-
-        gate_aside(2)
+        nc.gpsimd.tensor_tensor(
+            out=aside[:, 2 * T : 2 * T + 2 * C].rearrange("p (d j) -> p d j", d=2),
+            in0=y2_late[:].rearrange("p (d j) -> p d j", d=2),
+            in1=late_gates.unsqueeze(1).to_broadcast([P, 2, C]),
+            op=ALU.mult,
+        )
         add_aside(0)
         store(0)
-        gate_aside(3)
         frozen(2, "bank4")
         frozen(3, "bank5")
         scatter_plain(1, C, gated[0][:])

@@ -46,6 +46,7 @@ def tile_moe_adp_relu_kernel(
         wbw = held([P, E * 2 * N], U8, "wbw")
         wbs = held([P, E * N], U8, "wbs")
         gates = held([P, T], F32, "gates")
+        gate_rows = held([P, P], F32, "gate_rows")
         wraw = [[held([P, PACK * N // 2], F32, "wraw%d_%d" % (s, h)) for h in range(2)] for s in range(PASSES)]
         ident = held([P, P], F32, "ident")
 
@@ -94,6 +95,7 @@ def tile_moe_adp_relu_kernel(
         )
         load_wa(1)
         nc.sync.dma_start(out=gates[:], in_=gate)
+        nc.sync.dma_start(out=gate_rows[:], in_=gate.rearrange("r (b j) -> (r b) j", j=P)[0:P, :])
         load_w(0, 0)
         load_w(0, 1)
         load_w(1, 0)
@@ -329,7 +331,38 @@ def tile_moe_adp_relu_kernel(
         for d in range(2, PACK):
             scatter_gated(d, P, y1_late[:, (d - 2) * P : (d - 1) * P])
 
-        ysums = [second_layer(1, hq2, (0, 1), "bank7"), second_layer(1, hq2, (2, 3), "bank3")]
+        gate_turned = psum.tile([P, P], F32, name="gate_turned", tag="bank3")
+        nc.tensor.transpose(gate_turned[:], gate_rows[:], ident[:])
+        gate_cols = held([P, PACK], F32, "gate_cols")
+        nc.scalar.copy(out=gate_cols[:], in_=gate_turned[:, 0:PACK])
+        ysums = [second_layer(1, hq2, (0,), "bank7")]
+
+        def slots_on_partitions(d, bank):
+            sums = psum.tile([P, C], F32, name="y_rows", tag=bank)
+            for b in range(2):
+                cols = slice(b * P, (b + 1) * P)
+                nc.tensor.matmul_mx(
+                    out=sums[:, cols],
+                    lhsT=hq2[0][:, cols].bitcast(FP8X4),
+                    lhsT_scale=hq2[1][:, cols],
+                    rhs=wbw_dealt[:, 2 * (N + d * P) : 2 * (N + (d + 1) * P)].bitcast(FP4X4),
+                    rhs_scale=wbs_dealt[:, N + d * P : N + (d + 1) * P],
+                    start=True,
+                    stop=True,
+                )
+            return sums
+
+        def gate_and_turn(d, sums, bank):
+            rows = held([P, C], F32, "gated_rows%d" % d)
+            turned = psum.tile([P, C], F32, name="y_back", tag=bank)
+            for b in range(2):
+                cols = slice(b * P, (b + 1) * P)
+                nc.scalar.activation(out=rows[:, cols], in_=sums[:, cols], func=ACT.Copy, scale=gate_cols[:, 2 + b : 3 + b])
+                nc.tensor.transpose(turned[:, cols], rows[:, cols], ident[:])
+            return turned
+
+        y_rows = [slots_on_partitions(1, "bank6"), slots_on_partitions(3, "bank0")]
+        ysums.append(second_layer(1, hq2, (2,), "bank3"))
         late_gates = gates[:, C : 2 * C]
 
         def add_aside(d):
@@ -342,44 +375,47 @@ def tile_moe_adp_relu_kernel(
         for s in range(PASSES):
             round_w(rounded, 0, s)
         quantise_w(0, rounded)
-        frozen(0, "bank0")
-        frozen(1, "bank1")
         rounded = held([P, PACK * N], BF16, "wbf1", "hrow_a")
         round_w(rounded, 1, 0)
         y2_0 = held([P, C], F32, "y2_0", "wraw0_0")
         nc.scalar.copy(out=y2_0[:], in_=ysums[0][:, 0:C])
         scatter_gated(0, C, y2_0[:])
+        y_back = gate_and_turn(1, y_rows[0], "bank2")
+        frozen(0, "bank6")
+        frozen(1, "bank7")
         round_w(rounded, 1, 1)
 
-        gated = [held([P, C], F32, "gated1", "wraw1_1")]
-        nc.vector.tensor_tensor(out=gated[0][:], in0=ysums[0][:, C : 2 * C], in1=late_gates, op=ALU.mult)
+        gated = [held([P, C], F32, "gated1", "wraw0_1")]
         quantise_w(1, rounded)
-        aside = held([P, 2 * T + 2 * C], F32, "aside", "hrow_a")
+        nc.scalar.copy(out=gated[0][:], in_=y_back[:])
+        aside = held([P, 2 * T + C], F32, "aside", "hrow_a")
         total[0] = aside[:, 0 : 2 * T]
-        gated.extend([aside[:, 2 * T : 2 * T + C], aside[:, 2 * T + C : 2 * T + 2 * C]])
-        y2_late = held([P, 2 * C], F32, "y2_late", "wraw1_0")
-        nc.scalar.copy(out=y2_late[:], in_=ysums[1][:])
-
-        nc.gpsimd.tensor_tensor(
-            out=aside[:, 2 * T : 2 * T + 2 * C].rearrange("p (d j) -> p d j", d=2),
-            in0=y2_late[:].rearrange("p (d j) -> p d j", d=2),
-            in1=late_gates.unsqueeze(1).to_broadcast([P, 2, C]),
-            op=ALU.mult,
-        )
+        y2_last = held([P, C], F32, "y2_last", "wraw1_0")
+        nc.scalar.copy(out=y2_last[:], in_=ysums[1][:, 0:C])
+        nc.gpsimd.tensor_tensor(out=aside[:, 2 * T : 2 * T + C], in0=y2_last[:], in1=late_gates, op=ALU.mult)
         add_aside(0)
         store(0)
+        gated.append(aside[:, 2 * T : 2 * T + C])
+        y_back = gate_and_turn(3, y_rows[1], "bank1")
         frozen(2, "bank4")
         frozen(3, "bank5")
         scatter_plain(1, C, gated[0][:])
         add_aside(1)
         store(1)
         scatter_plain(2, C, gated[1][:])
+        gated.append(held([P, C], F32, "gated3", "wraw1_1"))
+        nc.scalar.copy(out=gated[2][:], in_=y_back[:])
         add_aside(2)
         round_pair(nc.scalar.copy, 0, all_tokens)
         scatter_plain(3, C, gated[2][:])
 
         first_quarter, second_quarter, upper_half = slice(0, T // 4), slice(T // 4, T // 2), slice(T // 2, T)
-        for tokens in (upper_half, first_quarter, second_quarter):
+        base_quarter = held([P, T // 4], F32, "base_quarter")
+        nc.scalar.copy(out=base_quarter[:], in_=base[3][:, first_quarter])
+        nc.gpsimd.tensor_tensor(
+            out=total_of(3)[:, first_quarter], in0=base_quarter[:], in1=placed[3][:, first_quarter], op=ALU.add
+        )
+        for tokens in (upper_half, second_quarter):
             add(3, tokens)
         nc.sync.dma_start(out=out_planes[:, 2:4, :], in_=total[1][:].rearrange("p (d t) -> p d t", d=2))
         round_pair(nc.vector.tensor_copy, 1, upper_half)

@@ -21,10 +21,7 @@ P = 128
 PACK = 4
 K_PASS = P * PACK
 PASSES = K // K_PASS
-QUADS = 4
 LIST_ROWS = 16
-W_PIECES = 4
-REST = T - P
 
 
 def tile_moe_adp_relu_kernel(
@@ -33,10 +30,21 @@ def tile_moe_adp_relu_kernel(
     nc = tc.nc
     with ExitStack() as ctx:
         keep = ctx.enter_context(tc.tile_pool(name="keep", bufs=1))
+        laid = ctx.enter_context(tc.tile_pool(name="laid", bufs=1))
         psum = ctx.enter_context(tc.psum_pool(name="psum", bufs=1))
 
         def held(shape, dtype, name, after=None):
             return keep.tile(shape, dtype, name=name, tag=after or name, align_bytes=64)
+
+        KIB, STEP = 1024, 64
+        place = {
+            "hcol1": 0, "wbf0": 0, "hcol2": 4 * KIB, "wbf1": 2 * KIB,
+            "placed0": 6 * KIB, "hrow3": 8 * KIB - STEP, "placed1": 8 * KIB,
+            "wraw0": 10 * KIB, "gated1_23": 10 * KIB, "gated2_2": 11 * KIB, "gated2_01": 12 * KIB,
+        }
+
+        def laid_out(shape, dtype, name):
+            return laid.tile(shape, dtype, name=name, align_bytes=64, offset=place[name])
 
         offsets = keep.tile([P, T // LIST_ROWS], U16, name="offsets")
         xw = [held([P, T], I32, "xw%d" % s) for s in range(PASSES)]
@@ -46,8 +54,7 @@ def tile_moe_adp_relu_kernel(
         wbw = held([P, E * 2 * N], U8, "wbw")
         wbs = held([P, E * N], U8, "wbs")
         gates = held([P, T], F32, "gates")
-        gate_rows = held([P, P], F32, "gate_rows")
-        wraw = [[held([P, PACK * N // 2], F32, "wraw%d_%d" % (s, h)) for h in range(2)] for s in range(PASSES)]
+        wraw = [laid_out([P, PACK * N], F32, "wraw0"), held([P, PACK * N], F32, "wraw1")]
         ident = held([P, P], F32, "ident")
 
         def load_scales(tile, scale_rows, q, queue):
@@ -65,11 +72,8 @@ def tile_moe_adp_relu_kernel(
                 in_=wa_words[e].bitcast(I32).rearrange("s p c -> p s c"),
             )
 
-        def load_w(s, h):
-            rows = w[K_PASS * s : K_PASS * (s + 1), :].rearrange("(p j) n -> p j n", j=PACK)
-            nc.sync.dma_start(
-                out=wraw[s][h][:].rearrange("p (j n) -> p j n", j=PACK), in_=rows[:, :, h * N // 2 : (h + 1) * N // 2]
-            )
+        def load_w(s):
+            nc.sync.dma_start(out=wraw[s][:], in_=w[K_PASS * s : K_PASS * (s + 1), :].rearrange("(p j) n -> p (j n)", j=PACK))
 
         xs_rows = x_scales.bitcast(I32).rearrange("s b c -> b s c")
         was_rows = wa_scales.bitcast(I32).rearrange("e s b c -> b (e s) c")
@@ -84,22 +88,22 @@ def tile_moe_adp_relu_kernel(
             load_scales(xs, xs_rows, q, queue)
         load_x(1)
         load_wa(0)
-        for q, queue in ((1, nc.scalar), (2, nc.sync), (3, nc.scalar)):
-            load_scales(was, was_rows, q, queue)
-        make_identity(nc, ident[:])
-        for q, queue in enumerate((nc.scalar, nc.scalar, nc.sync, nc.sync)):
-            load_scales(wbs, wbs_rows, q, queue)
+        load_scales(was, was_rows, 1, nc.sync)
         nc.sync.dma_start(
             out=wbw[:].bitcast(I32).rearrange("p (e c) -> p e c", e=E),
             in_=wb_words.bitcast(I32).rearrange("e s p c -> p (e s) c"),
         )
+        for q in range(2, 4):
+            load_scales(was, was_rows, q, nc.sync)
+        make_identity(nc, ident[:])
+        unread_column = held([P, 1], F32, "unread_column")
+        nc.scalar.activation(out=unread_column[:], in_=ident[:, 0:1], func=ACT.Relu)
+        for q in range(4):
+            load_scales(wbs, wbs_rows, q, nc.sync)
         load_wa(1)
         nc.sync.dma_start(out=gates[:], in_=gate)
-        nc.sync.dma_start(out=gate_rows[:], in_=gate.rearrange("r (b j) -> (r b) j", j=P)[0:P, :])
-        load_w(0, 0)
-        load_w(0, 1)
-        load_w(1, 0)
-        load_w(1, 1)
+        for s in range(PASSES):
+            load_w(s)
 
         def slots_of(first, width):
             return offsets[:, first // LIST_ROWS : (first + width) // LIST_ROWS]
@@ -128,8 +132,7 @@ def tile_moe_adp_relu_kernel(
                 )
             return sums
 
-        def turn_h(parts, hcol, turn_bank, row_name):
-            hrow = held([P, H], BF16, "hrow", row_name)
+        def relu_h(parts, hrow):
             first = 0
             for part in parts:
                 span = part.shape[1] // PACK
@@ -139,14 +142,17 @@ def tile_moe_adp_relu_kernel(
                     func=ACT.Relu,
                 )
                 first = first + span
-            turned = psum.tile([P, PACK * P], F32, name="h_turned", tag=turn_bank)
+            return hrow
+
+        def turn_h(hrow, hcol, turn_bank):
+            turned = psum.tile([P, 2 * P], F32, name="h_turned", tag=turn_bank)
             for u in range(2):
                 nc.tensor.transpose(
                     turned[:, u * P : (u + 1) * P], hrow[:].bitcast(F32)[:, u * P : (u + 1) * P], ident[:]
                 )
             nc.scalar.copy(
                 out=hcol.bitcast(F32).rearrange("p (j u) -> p j u", u=2),
-                in_=turned[:, 0 : 2 * P].rearrange("p (u j) -> p j u", u=2),
+                in_=turned[:].rearrange("p (u j) -> p j u", u=2),
             )
 
         def quantise_h(hcol, width, name):
@@ -155,29 +161,28 @@ def tile_moe_adp_relu_kernel(
             nc.vector.quantize_mx(out=codes[:].bitcast(FP8X4), scales=scales[:], in_=hcol[:])
             return codes, scales
 
-        def deal_wb(after):
-            words = held([P, E * 2 * N], U8, "wbw_dealt", after)
-            scales = held([P, E * N], U8, "wbs_dealt")
-            nc.vector.tensor_copy(
-                words[:].bitcast(U16).rearrange("p (e d a b) -> p e a d b", e=E, d=PACK, b=8),
-                wbw[:].bitcast(U16).rearrange("p (e a b d) -> p e a d b", e=E, d=PACK, b=8),
+        def deal_wb(e, after=None):
+            words = held([P, 2 * N], U8, "wbw_dealt%d" % e, after)
+            scales = held([P, N], U8, "wbs_dealt%d" % e)
+            nc.scalar.copy(
+                out=words[:].bitcast(U16).rearrange("p (d a b) -> p a d b", d=PACK, b=8),
+                in_=wbw[:, 2 * e * N : 2 * (e + 1) * N].bitcast(U16).rearrange("p (a b d) -> p a d b", d=PACK, b=8),
             )
-            for e in range(E):
-                nc.gpsimd.tensor_copy(
-                    scales[:, e * N : (e + 1) * N].rearrange("p (d a b) -> p a d b", d=PACK, b=16),
-                    wbs[:, e * N : (e + 1) * N].rearrange("p (a b d) -> p a d b", d=PACK, b=16),
-                )
+            nc.gpsimd.tensor_copy(
+                scales[:].rearrange("p (d a b) -> p a d b", d=PACK, b=16),
+                wbs[:, e * N : (e + 1) * N].rearrange("p (a b d) -> p a d b", d=PACK, b=16),
+            )
             return words, scales
 
-        def second_layer(e, hq, planes, bank):
+        def second_layer(wb_dealt, hq, planes, bank):
             codes, scales = hq
             width = codes.shape[1]
-            sums = psum.tile([P, N], F32, name="y_sums", tag=bank)
+            sums = psum.tile([P, len(planes) * width], F32, name="y_sums", tag=bank)
             for i, d in enumerate(planes):
                 nc.tensor.matmul_mx(
                     out=sums[:, i * width : (i + 1) * width],
-                    lhsT=wbw_dealt[:, 2 * (e * N + d * P) : 2 * (e * N + (d + 1) * P)].bitcast(FP4X4),
-                    lhsT_scale=wbs_dealt[:, e * N + d * P : e * N + (d + 1) * P],
+                    lhsT=wb_dealt[0][:, 2 * d * P : 2 * (d + 1) * P].bitcast(FP4X4),
+                    lhsT_scale=wb_dealt[1][:, d * P : (d + 1) * P],
                     rhs=codes[:].bitcast(FP8X4),
                     rhs_scale=scales[:],
                     start=True,
@@ -185,45 +190,53 @@ def tile_moe_adp_relu_kernel(
                 )
             return sums
 
+        def gate_y(sums, first, width, gated):
+            planes = sums.shape[1] // width
+            nc.vector.tensor_tensor(
+                out=gated.rearrange("p (d j) -> p d j", d=planes),
+                in0=sums.rearrange("p (d j) -> p d j", d=planes),
+                in1=gates[:, first : first + width].unsqueeze(1).to_broadcast([P, planes, width]),
+                op=ALU.mult,
+            )
+            return [gated[:, i * width : (i + 1) * width] for i in range(planes)]
+
         placed = {}
 
-        def window(d, after=None):
-            if d not in placed:
-                placed[d] = held([P, T], F32, "placed%d" % d, after)
-            return placed[d]
+        def scatter_on_vector(d, first, values):
+            nc.vector.tensor_copy(placed[d][:].indirect(slots_of(first, values.shape[1])), values)
 
-        def scatter_gated(d, first, values, after=None):
-            width = values.shape[1]
-            nc.vector.tensor_tensor(
-                window(d, after)[:].indirect(slots_of(first, width)), values, gates[:, first : first + width], ALU.mult
-            )
+        def scatter_on_scalar(d, first, values):
+            nc.scalar.activation(out=placed[d][:].indirect(slots_of(first, values.shape[1])), in_=values, func=ACT.Copy)
 
-        def scatter_plain(d, first, values):
-            nc.vector.tensor_copy(window(d)[:].indirect(slots_of(first, values.shape[1])), values)
-
-        wq = {}
-
-        def round_w(rounded, pair, s):
-            view = rounded[:].rearrange("p (s e m j) -> p s m j e", s=PASSES, e=2, j=PACK)
-            for h in range(2):
-                nc.scalar.copy(
-                    out=view[:, s, h * P // 2 : (h + 1) * P // 2],
-                    in_=wraw[s][h][:].rearrange("p (j m a e) -> p a m j e", a=2, e=2, j=PACK)[:, pair],
+        def round_w(s):
+            rounded = laid_out([P, PACK * K_PASS], BF16, "wbf%d" % s)
+            for i in range(2):
+                planes = slice(2 * i, 2 * i + 2)
+                nc.gpsimd.tensor_scalar(
+                    out=rounded[:].rearrange("p (d m j) -> p m d j", m=P, j=PACK)[:, :, planes, :],
+                    in0=wraw[s][:].rearrange("p (j m d) -> p m d j", d=PACK, j=PACK)[:, :, planes, :],
+                    scalar1=1.0,
+                    scalar2=0.0,
+                    op0=ALU.mult,
+                    op1=ALU.add,
                 )
+            return rounded
 
-        def quantise_w(pair, rounded):
-            codes = held([P, N], U32, "wq%d" % pair)
-            scales = held([P, N], U8, "wsc%d" % pair)
-            nc.vector.quantize_mx(out=codes[:].bitcast(FP8X4), scales=scales[:], in_=rounded[:])
-            wq[pair] = (codes, scales)
+        def quantise_w(rounded, name):
+            width = rounded.shape[1] // PACK
+            codes = held([P, width], U32, "wq" + name)
+            scales = held([P, width], U8, "wsc" + name)
+            nc.vector.quantize_mx(out=codes[:].bitcast(FP8X4), scales=scales[:], in_=rounded)
+            return codes, scales
 
         base = {}
 
-        def frozen(d, bank):
-            codes, scales = wq[d // 2]
-            base[d] = psum.tile([P, T], F32, name="base%d" % d, tag=bank)
-            for s in range(PASSES):
-                cols = slice((2 * s + d % 2) * P, (2 * s + d % 2 + 1) * P)
+        def frozen_pass(s, wq, planes):
+            codes, scales = wq
+            for i, d in enumerate(planes):
+                if s == 0:
+                    base[d] = psum.tile([P, T], F32, name="base%d" % d, tag=("bank5", "bank7", "bank4", "bank0")[d])
+                cols = slice(i * P, (i + 1) * P)
                 nc.tensor.matmul_mx(
                     out=base[d][:],
                     lhsT=codes[:, cols].bitcast(FP8X4),
@@ -234,7 +247,7 @@ def tile_moe_adp_relu_kernel(
                     stop=(s == PASSES - 1),
                 )
 
-        total = {1: held([P, 2 * T], F32, "total1")}
+        total = [held([P, 2 * T], F32, "total%d" % i) for i in range(2)]
         out_planes = out_0.rearrange("(p d) t -> p d t", d=PACK)
 
         def total_of(d):
@@ -276,6 +289,8 @@ def tile_moe_adp_relu_kernel(
         words1 = [words_mid[:, 0:P], gather_words(1, P, P, "gw1_1")]
         scales1 = [gather_scales(s, P, P, "gs1_%d" % s) for s in range(PASSES)]
         scales_b = [gather_scales(s, C, C, "gsb_%d" % s) for s in range(PASSES)]
+        late_second = gather_words(1, C, C, "gw2_1")
+        wb0 = deal_wb(0)
         parts = []
         for chunks, bank in (((0, 1), "bank0"), ((2,), "bank7"), ((3,), "bank5")):
             sums = psum.tile([P, len(chunks) * P], F32, name="h_part", tag=bank)
@@ -292,137 +307,81 @@ def tile_moe_adp_relu_kernel(
                         stop=(s == PASSES - 1),
                     )
             parts.append(sums[:])
-        late_first = [words_mid[:, P:C], gather_words(0, C + P, P, "gw3_0", "gw0_0")[:]]
-        hcol0 = held([P, PACK * P], BF16, "hcol0")
-        turn_h(parts, hcol0[:], "bank2", "hrow_a")
-        hq0 = quantise_h(hcol0, P, "0")
-        late_second = gather_words(1, C, C, "gw2_1", "hcol0")
+        hrow0 = relu_h(parts, held([P, H], BF16, "hrow0"))
         sums1 = first_layer(0, [t[:] for t in words1], [t[:] for t in scales1], "bank1")
-        wbw_dealt, wbs_dealt = deal_wb("gw1_1")
+        hrow1 = relu_h([sums1[:]], held([P, H], BF16, "hrow1"))
+        hcol0 = held([P, PACK * P], BF16, "hcol0")
+        turn_h(hrow0, hcol0[:], "bank2")
+        hq0 = quantise_h(hcol0, P, "0")
+        hcol1 = laid_out([P, PACK * P], BF16, "hcol1")
+        turn_h(hrow1, hcol1[:], "bank3")
+        late_first = [words_mid[:, P:C], gather_words(0, C + P, P, "gw3_0", "hrow1")[:]]
 
         def late_first_layer(b, bank):
             cols = slice(b * P, (b + 1) * P)
             return first_layer(1, [late_first[b], late_second[:, cols]], [t[:, cols] for t in scales_b], bank)
 
-        hcol1 = held([P, PACK * P], BF16, "hcol1")
-        turn_h([sums1[:]], hcol1[:], "bank3", "hrow_b")
+        def gate_planes(sums, order, planes, first, width, gated):
+            at = order.index(planes[0])
+            part = sums[:, at * width : (at + len(planes)) * width]
+            return dict(zip(planes, gate_y(part, first, width, gated[:])))
+
+        sums2 = late_first_layer(0, "bank1")
+        wb1 = deal_wb(1, "gw_mid")
+        order = (3, 2, 0, 1)
+        y0 = second_layer(wb0, hq0, order, "bank4")
         hq1 = quantise_h(hcol1, P, "1")
-        ysums = second_layer(0, hq0, [0], "bank4")
-        y0_first = held([P, P], F32, "y0_first")
-        nc.scalar.copy(out=y0_first[:], in_=ysums[:, 0:P])
-        scatter_gated(0, 0, y0_first[:])
-
-        ysums0 = second_layer(0, hq0, [1, 2, 3], "bank5")
-        y0 = held([P, 3 * P], F32, "y0")
-        nc.scalar.copy(out=y0[:], in_=ysums0[:, 0 : 3 * P])
-        for d in range(1, PACK):
-            scatter_gated(d, 0, y0[:, (d - 1) * P : d * P])
-        ysums1 = second_layer(0, hq1, range(PACK), "bank2")
-        y1 = held([P, 2 * P], F32, "y1")
-        nc.scalar.copy(out=y1[:], in_=ysums1[:, 0 : 2 * P])
-        for d in range(2):
-            scatter_gated(d, P, y1[:, d * P : (d + 1) * P])
-        hcol2 = held([P, PACK * C], BF16, "hcol2")
-        for b, bank, turn_bank, row in ((0, "bank4", "bank6", "hrow_a"), (1, "bank5", "bank1", "hrow_b")):
-            turn_h([late_first_layer(b, bank)[:]], hcol2[:, PACK * P * b : PACK * P * (b + 1)], turn_bank, row)
+        wbf0 = round_w(0)
+        sums3 = late_first_layer(1, "bank3")
+        gated0 = gate_planes(y0, order, (3, 2), 0, P, held([P, 2 * P], F32, "gated0_32"))
+        gated0.update(gate_planes(y0, order, (0, 1), 0, P, held([P, 2 * P], F32, "gated0_01")))
+        y1 = second_layer(wb0, hq1, range(PACK), "bank0")
+        hrow2 = relu_h([sums2[:]], held([P, H], BF16, "hrow2"))
+        hrow3 = relu_h([sums3[:]], laid_out([P, H], BF16, "hrow3"))
+        for d in (2, 3):
+            placed[d] = held([P, T], F32, "placed%d" % d)
+        scatter_on_vector(3, 0, gated0[3])
+        gated1 = gate_planes(y1, (0, 1, 2, 3), (0, 1), P, P, held([P, 2 * P], F32, "gated1_01"))
+        scatter_on_vector(2, 0, gated0[2])
+        hcol2 = laid_out([P, PACK * C], BF16, "hcol2")
+        turn_h(hrow2, hcol2[:, 0 : PACK * P], "bank6")
+        turn_h(hrow3, hcol2[:, PACK * P : PACK * C], "bank2")
         hq2 = quantise_h(hcol2, C, "2")
-        y1_late = held([P, 2 * P], F32, "y1_late", "hrow_b")
-        nc.scalar.copy(out=y1_late[:], in_=ysums1[:, 2 * P : 4 * P])
-        for d in range(2, PACK):
-            scatter_gated(d, P, y1_late[:, (d - 2) * P : (d - 1) * P])
-
-        gate_turned = psum.tile([P, P], F32, name="gate_turned", tag="bank3")
-        nc.tensor.transpose(gate_turned[:], gate_rows[:], ident[:])
-        gate_cols = held([P, PACK], F32, "gate_cols")
-        nc.scalar.copy(out=gate_cols[:], in_=gate_turned[:, 0:PACK])
-        ysums = [second_layer(1, hq2, (0,), "bank7")]
-
-        def slots_on_partitions(d, bank):
-            sums = psum.tile([P, C], F32, name="y_rows", tag=bank)
-            for b in range(2):
-                cols = slice(b * P, (b + 1) * P)
-                nc.tensor.matmul_mx(
-                    out=sums[:, cols],
-                    lhsT=hq2[0][:, cols].bitcast(FP8X4),
-                    lhsT_scale=hq2[1][:, cols],
-                    rhs=wbw_dealt[:, 2 * (N + d * P) : 2 * (N + (d + 1) * P)].bitcast(FP4X4),
-                    rhs_scale=wbs_dealt[:, N + d * P : N + (d + 1) * P],
-                    start=True,
-                    stop=True,
-                )
-            return sums
-
-        def gate_and_turn(d, sums, bank):
-            rows = held([P, C], F32, "gated_rows%d" % d)
-            turned = psum.tile([P, C], F32, name="y_back", tag=bank)
-            for b in range(2):
-                cols = slice(b * P, (b + 1) * P)
-                nc.scalar.activation(out=rows[:, cols], in_=sums[:, cols], func=ACT.Copy, scale=gate_cols[:, 2 + b : 3 + b])
-                nc.tensor.transpose(turned[:, cols], rows[:, cols], ident[:])
-            return turned
-
-        y_rows = [slots_on_partitions(1, "bank6"), slots_on_partitions(3, "bank0")]
-        ysums.append(second_layer(1, hq2, (2,), "bank3"))
-        late_gates = gates[:, C : 2 * C]
-
-        def add_aside(d):
-            base_sb = held([P, T], F32, "base_sb%d" % d)
-            nc.scalar.copy(out=base_sb[:], in_=base[d][:])
-            nc.gpsimd.tensor_tensor(out=total_of(d), in0=base_sb[:], in1=placed[d][:], op=ALU.add)
-
+        gated1.update(gate_planes(y1, (0, 1, 2, 3), (2, 3), P, P, laid_out([P, 2 * P], F32, "gated1_23")))
+        wq0 = quantise_w(wbf0[:], "0")
+        wbf1 = round_w(1)
+        for d in (0, 1):
+            placed[d] = laid_out([P, T], F32, "placed%d" % d)
+        for first, gated in ((0, gated0), (P, gated1)):
+            for d in range(2):
+                scatter_on_scalar(d, first, gated[d])
+        y2 = [second_layer(wb1, hq2, planes, bank) for planes, bank in (((2, 3), "bank3"), ((0, 1), "bank1"))]
+        frozen_pass(0, wq0, range(PACK))
+        scatter_on_vector(2, P, gated1[2])
+        scatter_on_scalar(3, P, gated1[3])
+        gated2 = gate_planes(y2[0], (2, 3), (2,), C, C, laid_out([P, C], F32, "gated2_2"))
+        gated2.update(gate_planes(y2[1], (0, 1), (0, 1), C, C, laid_out([P, 2 * C], F32, "gated2_01")))
+        scatter_on_vector(2, C, gated2[2])
+        gated2.update(gate_planes(y2[0], (2, 3), (3,), C, C, held([P, C], F32, "gated2_3", "wraw1")))
+        frozen_pass(1, quantise_w(wbf1[:], "1"), range(PACK))
+        for d in range(2):
+            scatter_on_scalar(d, C, gated2[d])
+        scatter_on_vector(3, C, gated2[3][:, 0:P])
+        scatter_on_scalar(3, C + P, gated2[3][:, P:C])
         all_tokens = slice(0, T)
-        rounded = held([P, PACK * N], BF16, "wbf0", "hq0")
-        for s in range(PASSES):
-            round_w(rounded, 0, s)
-        quantise_w(0, rounded)
-        rounded = held([P, PACK * N], BF16, "wbf1", "hrow_a")
-        round_w(rounded, 1, 0)
-        y2_0 = held([P, C], F32, "y2_0", "wraw0_0")
-        nc.scalar.copy(out=y2_0[:], in_=ysums[0][:, 0:C])
-        scatter_gated(0, C, y2_0[:])
-        y_back = gate_and_turn(1, y_rows[0], "bank2")
-        frozen(0, "bank6")
-        frozen(1, "bank7")
-        round_w(rounded, 1, 1)
-
-        gated = [held([P, C], F32, "gated1", "wraw0_1")]
-        quantise_w(1, rounded)
-        nc.scalar.copy(out=gated[0][:], in_=y_back[:])
-        aside = held([P, 2 * T + C], F32, "aside", "hrow_a")
-        total[0] = aside[:, 0 : 2 * T]
-        y2_last = held([P, C], F32, "y2_last", "wraw1_0")
-        nc.scalar.copy(out=y2_last[:], in_=ysums[1][:, 0:C])
-        nc.gpsimd.tensor_tensor(out=aside[:, 2 * T : 2 * T + C], in0=y2_last[:], in1=late_gates, op=ALU.mult)
-        add_aside(0)
-        store(0)
-        gated.append(aside[:, 2 * T : 2 * T + C])
-        y_back = gate_and_turn(3, y_rows[1], "bank1")
-        frozen(2, "bank4")
-        frozen(3, "bank5")
-        scatter_plain(1, C, gated[0][:])
-        add_aside(1)
-        store(1)
-        scatter_plain(2, C, gated[1][:])
-        gated.append(held([P, C], F32, "gated3", "wraw1_1"))
-        nc.scalar.copy(out=gated[2][:], in_=y_back[:])
-        add_aside(2)
-        round_pair(nc.scalar.copy, 0, all_tokens)
-        scatter_plain(3, C, gated[2][:])
-
-        first_quarter, second_quarter, upper_half = slice(0, T // 4), slice(T // 4, T // 2), slice(T // 2, T)
-        base_quarter = held([P, T // 4], F32, "base_quarter")
-        nc.scalar.copy(out=base_quarter[:], in_=base[3][:, first_quarter])
-        nc.gpsimd.tensor_tensor(
-            out=total_of(3)[:, first_quarter], in0=base_quarter[:], in1=placed[3][:, first_quarter], op=ALU.add
-        )
-        for tokens in (upper_half, second_quarter):
+        for d in range(3):
+            add(d, all_tokens)
+            store(d)
+        halves = (slice(T // 2, T), slice(0, T // 2))
+        for tokens in halves:
+            round_pair(nc.scalar.copy, 0, tokens)
+        for tokens in halves:
             add(3, tokens)
-        nc.sync.dma_start(out=out_planes[:, 2:4, :], in_=total[1][:].rearrange("p (d t) -> p d t", d=2))
-        round_pair(nc.vector.tensor_copy, 1, upper_half)
-        round_pair(nc.scalar.copy, 1, first_quarter)
-        round_pair(nc.vector.tensor_copy, 1, second_quarter)
+        store(3)
+        for tokens in halves:
+            round_pair(nc.vector.tensor_copy, 1, tokens)
         words_out = out_1[0].rearrange("p n d -> p (n d)").bitcast(I32)
-        for tokens in (upper_half, slice(0, T // 2)):
+        for tokens in halves:
             nc.vector.quantize_mx(
                 out=ow[:, tokens].bitcast(FP8X4),
                 scales=osc[:, tokens],
@@ -430,6 +389,4 @@ def tile_moe_adp_relu_kernel(
             )
             nc.sync.dma_start(out=words_out[:, tokens], in_=ow[:, tokens].bitcast(I32))
         for q, queue in enumerate((nc.scalar, nc.sync, nc.scalar, nc.sync)):
-            queue.dma_start(
-                out=out_2[0, q:16:4, :].bitcast(I32), in_=osc[q:P:32, :].bitcast(I32)
-            )
+            queue.dma_start(out=out_2[0, q:16:4, :].bitcast(I32), in_=osc[q:P:32, :].bitcast(I32))

@@ -38,9 +38,8 @@ def tile_moe_adp_relu_kernel(
 
         KIB, STEP = 1024, 64
         place = {
-            "hcol1": 0, "wbf0": 0, "hcol2": 4 * KIB, "wbf1": 2 * KIB,
-            "placed0": 6 * KIB, "hrow3": 8 * KIB - STEP, "placed1": 8 * KIB,
-            "wraw0": 10 * KIB, "gated1_23": 10 * KIB, "gated2_2": 11 * KIB, "gated2_01": 12 * KIB,
+            "placed0": 0, "hrow3": 2 * KIB - STEP, "placed1": 2 * KIB,
+            "wbf0_0": 4 * KIB, "gated1_013": 4 * KIB, "gated_rest2": 5 * KIB + KIB // 2,
         }
 
         def laid_out(shape, dtype, name):
@@ -54,7 +53,7 @@ def tile_moe_adp_relu_kernel(
         wbw = held([P, E * 2 * N], U8, "wbw")
         wbs = held([P, E * N], U8, "wbs")
         gates = held([P, T], F32, "gates")
-        wraw = [laid_out([P, PACK * N], F32, "wraw0"), held([P, PACK * N], F32, "wraw1")]
+        wraw = [held([P, PACK * N], F32, "wraw%d" % s) for s in range(PASSES)]
         ident = held([P, P], F32, "ident")
 
         def load_scales(tile, scale_rows, q, queue):
@@ -155,8 +154,8 @@ def tile_moe_adp_relu_kernel(
                 in_=turned[:].rearrange("p (u j) -> p j u", u=2),
             )
 
-        def quantise_h(hcol, width, name):
-            codes = held([P, width], U32, "hq" + name)
+        def quantise_h(hcol, width, name, after=None):
+            codes = held([P, width], U32, "hq" + name, after)
             scales = held([P, width], U8, "hs" + name)
             nc.vector.quantize_mx(out=codes[:].bitcast(FP8X4), scales=scales[:], in_=hcol[:])
             return codes, scales
@@ -208,18 +207,12 @@ def tile_moe_adp_relu_kernel(
         def scatter_on_scalar(d, first, values):
             nc.scalar.activation(out=placed[d][:].indirect(slots_of(first, values.shape[1])), in_=values, func=ACT.Copy)
 
-        def round_w(s):
-            rounded = laid_out([P, PACK * K_PASS], BF16, "wbf%d" % s)
-            for i in range(2):
-                planes = slice(2 * i, 2 * i + 2)
-                nc.gpsimd.tensor_scalar(
-                    out=rounded[:].rearrange("p (d m j) -> p m d j", m=P, j=PACK)[:, :, planes, :],
-                    in0=wraw[s][:].rearrange("p (j m d) -> p m d j", d=PACK, j=PACK)[:, :, planes, :],
-                    scalar1=1.0,
-                    scalar2=0.0,
-                    op0=ALU.mult,
-                    op1=ALU.add,
-                )
+        def round_w(s, i, make):
+            rounded = make([P, 2 * K_PASS], BF16, "wbf%d_%d" % (s, i))
+            nc.vector.tensor_copy(
+                out=rounded[:].rearrange("p (d m j) -> p m j d", m=P, j=PACK),
+                in_=wraw[s][:].rearrange("p (j m d) -> p m j d", d=PACK, j=PACK)[:, :, :, 2 * i : 2 * i + 2],
+            )
             return rounded
 
         def quantise_w(rounded, name):
@@ -247,7 +240,7 @@ def tile_moe_adp_relu_kernel(
                     stop=(s == PASSES - 1),
                 )
 
-        total = [held([P, 2 * T], F32, "total%d" % i) for i in range(2)]
+        total = [held([P, 2 * T], F32, "total0")]
         out_planes = out_0.rearrange("(p d) t -> p d t", d=PACK)
 
         def total_of(d):
@@ -313,7 +306,7 @@ def tile_moe_adp_relu_kernel(
         hcol0 = held([P, PACK * P], BF16, "hcol0")
         turn_h(hrow0, hcol0[:], "bank2")
         hq0 = quantise_h(hcol0, P, "0")
-        hcol1 = laid_out([P, PACK * P], BF16, "hcol1")
+        hcol1 = held([P, PACK * P], BF16, "hcol1")
         turn_h(hrow1, hcol1[:], "bank3")
         late_first = [words_mid[:, P:C], gather_words(0, C + P, P, "gw3_0", "hrow1")[:]]
 
@@ -331,44 +324,47 @@ def tile_moe_adp_relu_kernel(
         order = (3, 2, 0, 1)
         y0 = second_layer(wb0, hq0, order, "bank4")
         hq1 = quantise_h(hcol1, P, "1")
-        wbf0 = round_w(0)
         sums3 = late_first_layer(1, "bank3")
-        gated0 = gate_planes(y0, order, (3, 2), 0, P, held([P, 2 * P], F32, "gated0_32"))
-        gated0.update(gate_planes(y0, order, (0, 1), 0, P, held([P, 2 * P], F32, "gated0_01")))
-        y1 = second_layer(wb0, hq1, range(PACK), "bank0")
+        gated0 = gate_planes(y0, order, order, 0, P, held([P, PACK * P], F32, "gated0"))
+        rounded = [round_w(0, 0, laid_out), round_w(0, 1, held)]
+        wq0 = [quantise_w(rounded[i][:], "0_%d" % i) for i in range(2)]
+        order = (2, 3, 0, 1)
+        y1 = second_layer(wb0, hq1, order, "bank0")
         hrow2 = relu_h([sums2[:]], held([P, H], BF16, "hrow2"))
         hrow3 = relu_h([sums3[:]], laid_out([P, H], BF16, "hrow3"))
-        for d in (2, 3):
-            placed[d] = held([P, T], F32, "placed%d" % d)
-        scatter_on_vector(3, 0, gated0[3])
-        gated1 = gate_planes(y1, (0, 1, 2, 3), (0, 1), P, P, held([P, 2 * P], F32, "gated1_01"))
-        scatter_on_vector(2, 0, gated0[2])
-        hcol2 = laid_out([P, PACK * C], BF16, "hcol2")
+        rest2 = laid_out([P, T - P], F32, "gated_rest2")
+        gated1 = gate_planes(y1, order, (3, 0, 1), P, P, laid_out([P, 3 * P], F32, "gated1_013"))
+        gate_planes(y1, order, (2,), P, P, rest2[:, 0:P])
+        hcol2 = held([P, PACK * C], BF16, "hcol2")
         turn_h(hrow2, hcol2[:, 0 : PACK * P], "bank6")
         turn_h(hrow3, hcol2[:, PACK * P : PACK * C], "bank2")
-        hq2 = quantise_h(hcol2, C, "2")
-        gated1.update(gate_planes(y1, (0, 1, 2, 3), (2, 3), P, P, laid_out([P, 2 * P], F32, "gated1_23")))
-        wq0 = quantise_w(wbf0[:], "0")
-        wbf1 = round_w(1)
-        for d in (0, 1):
+        for i in range(2):
+            frozen_pass(0, wq0[i], (2 * i, 2 * i + 1))
+        rounded = [round_w(1, i, held) for i in range(2)]
+        wq1 = [quantise_w(rounded[0][:], "1_0")]
+        hq2 = quantise_h(hcol2, C, "2", "wraw1")
+        wq1.append(quantise_w(rounded[1][:], "1_1"))
+        placed[3] = held([P, T], F32, "placed3", "hrow2")
+        placed[2] = held([P, T], F32, "placed2", "wbf1_0")
+        for d in range(2):
             placed[d] = laid_out([P, T], F32, "placed%d" % d)
         for first, gated in ((0, gated0), (P, gated1)):
-            for d in range(2):
+            for d in (3, 0, 1):
                 scatter_on_scalar(d, first, gated[d])
-        y2 = [second_layer(wb1, hq2, planes, bank) for planes, bank in (((2, 3), "bank3"), ((0, 1), "bank1"))]
-        frozen_pass(0, wq0, range(PACK))
-        scatter_on_vector(2, P, gated1[2])
-        scatter_on_scalar(3, P, gated1[3])
-        gated2 = gate_planes(y2[0], (2, 3), (2,), C, C, laid_out([P, C], F32, "gated2_2"))
-        gated2.update(gate_planes(y2[1], (0, 1), (0, 1), C, C, laid_out([P, 2 * C], F32, "gated2_01")))
-        scatter_on_vector(2, C, gated2[2])
-        gated2.update(gate_planes(y2[0], (2, 3), (3,), C, C, held([P, C], F32, "gated2_3", "wraw1")))
-        frozen_pass(1, quantise_w(wbf1[:], "1"), range(PACK))
+        y2 = [second_layer(wb1, hq2, planes, bank) for planes, bank in (((2, 3), "bank1"), ((0, 1), "bank3"))]
+        for i in range(2):
+            frozen_pass(1, wq1[i], (2 * i, 2 * i + 1))
+        scatter_on_vector(2, 0, gated0[2])
+        gate_planes(y2[0], (2, 3), (2,), C, C, rest2[:, P : T - P])
+        gated2 = gate_planes(y2[0], (2, 3), (3,), C, C, held([P, C], F32, "gated2_3"))
+        gated2.update(gate_planes(y2[1], (0, 1), (0, 1), C, C, held([P, 2 * C], F32, "gated2_01")))
+        scatter_on_vector(3, C, gated2[3][:, 0:P])
+        scatter_on_vector(2, P, rest2[:])
         for d in range(2):
             scatter_on_scalar(d, C, gated2[d])
-        scatter_on_vector(3, C, gated2[3][:, 0:P])
         scatter_on_scalar(3, C + P, gated2[3][:, P:C])
         all_tokens = slice(0, T)
+        total.append(held([P, 2 * T], F32, "total1", "gated2_01"))
         for d in range(3):
             add(d, all_tokens)
             store(d)

@@ -22,6 +22,7 @@ PACK = 4
 K_PASS = P * PACK
 PASSES = K // K_PASS
 LIST_ROWS = 16
+LAST = 64
 
 
 def tile_moe_adp_relu_kernel(
@@ -38,8 +39,9 @@ def tile_moe_adp_relu_kernel(
 
         KIB, STEP = 1024, 64
         place = {
-            "placed0": 0, "hrow3": 2 * KIB - STEP, "placed1": 2 * KIB,
-            "wbf0_0": 4 * KIB, "gated1_013": 4 * KIB, "gated_rest2": 5 * KIB + KIB // 2,
+            "placed0": 0, "hrow3": 2 * KIB - STEP, "placed2": 2 * KIB,
+            "wraw0_1": 4 * KIB, "hq2": 4 * KIB, "placed1": 5 * KIB,
+            "wbf0": 8 * KIB, "hcol2": 12 * KIB, "wbf1": 10 * KIB,
         }
 
         def laid_out(shape, dtype, name):
@@ -53,7 +55,8 @@ def tile_moe_adp_relu_kernel(
         wbw = held([P, E * 2 * N], U8, "wbw")
         wbs = held([P, E * N], U8, "wbs")
         gates = held([P, T], F32, "gates")
-        wraw = [held([P, PACK * N], F32, "wraw%d" % s) for s in range(PASSES)]
+        wraw0 = [held([P, PACK * N // 2], F32, "wraw0_0"), laid_out([P, PACK * N // 2], F32, "wraw0_1")]
+        wraw1 = held([P, PACK * N], F32, "wraw1")
         ident = held([P, P], F32, "ident")
 
         def load_scales(tile, scale_rows, q, queue):
@@ -71,8 +74,9 @@ def tile_moe_adp_relu_kernel(
                 in_=wa_words[e].bitcast(I32).rearrange("s p c -> p s c"),
             )
 
-        def load_w(s):
-            nc.sync.dma_start(out=wraw[s][:], in_=w[K_PASS * s : K_PASS * (s + 1), :].rearrange("(p j) n -> p (j n)", j=PACK))
+        def load_w(tile, s, columns):
+            rows = w[K_PASS * s : K_PASS * (s + 1), :].rearrange("(p j) n -> p j n", j=PACK)
+            nc.sync.dma_start(out=tile[:].rearrange("p (j n) -> p j n", j=PACK), in_=rows[:, :, columns])
 
         xs_rows = x_scales.bitcast(I32).rearrange("s b c -> b s c")
         was_rows = wa_scales.bitcast(I32).rearrange("e s b c -> b (e s) c")
@@ -100,9 +104,10 @@ def tile_moe_adp_relu_kernel(
         for q in range(4):
             load_scales(wbs, wbs_rows, q, nc.sync)
         load_wa(1)
+        load_w(wraw0[0], 0, slice(0, N // 2))
+        load_w(wraw0[1], 0, slice(N // 2, N))
         nc.sync.dma_start(out=gates[:], in_=gate)
-        for s in range(PASSES):
-            load_w(s)
+        load_w(wraw1, 1, slice(0, N))
 
         def slots_of(first, width):
             return offsets[:, first // LIST_ROWS : (first + width) // LIST_ROWS]
@@ -154,34 +159,42 @@ def tile_moe_adp_relu_kernel(
                 in_=turned[:].rearrange("p (u j) -> p j u", u=2),
             )
 
-        def quantise_h(hcol, width, name, after=None):
-            codes = held([P, width], U32, "hq" + name, after)
+        def quantise_h(hcol, width, name, make=held):
+            codes = make([P, width], U32, "hq" + name)
             scales = held([P, width], U8, "hs" + name)
             nc.vector.quantize_mx(out=codes[:].bitcast(FP8X4), scales=scales[:], in_=hcol[:])
             return codes, scales
 
-        def deal_wb(e, after=None):
-            words = held([P, 2 * N], U8, "wbw_dealt%d" % e, after)
-            scales = held([P, N], U8, "wbs_dealt%d" % e)
+        wb_words_dealt, wb_scales_dealt = {}, {}
+
+        def deal_words(e, planes, after=None):
+            words = held([P, 2 * P * len(planes)], U8, "wbw_dealt%d_%d" % (e, planes[0]), after)
+            source = wbw[:, 2 * e * N : 2 * (e + 1) * N].bitcast(U16).rearrange("p (a b d) -> p a d b", d=PACK, b=8)
             nc.scalar.copy(
-                out=words[:].bitcast(U16).rearrange("p (d a b) -> p a d b", d=PACK, b=8),
-                in_=wbw[:, 2 * e * N : 2 * (e + 1) * N].bitcast(U16).rearrange("p (a b d) -> p a d b", d=PACK, b=8),
+                out=words[:].bitcast(U16).rearrange("p (d a b) -> p a d b", d=len(planes), b=8),
+                in_=source[:, :, planes[0] : planes[-1] + 1, :],
             )
+            for i, d in enumerate(planes):
+                wb_words_dealt[e, d] = words[:, 2 * i * P : 2 * (i + 1) * P]
+
+        def deal_scales(e):
+            scales = held([P, N], U8, "wbs_dealt%d" % e)
             nc.gpsimd.tensor_copy(
                 scales[:].rearrange("p (d a b) -> p a d b", d=PACK, b=16),
                 wbs[:, e * N : (e + 1) * N].rearrange("p (a b d) -> p a d b", d=PACK, b=16),
             )
-            return words, scales
+            for d in range(PACK):
+                wb_scales_dealt[e, d] = scales[:, d * P : (d + 1) * P]
 
-        def second_layer(wb_dealt, hq, planes, bank):
+        def second_layer(e, hq, planes, bank):
             codes, scales = hq
             width = codes.shape[1]
             sums = psum.tile([P, len(planes) * width], F32, name="y_sums", tag=bank)
             for i, d in enumerate(planes):
                 nc.tensor.matmul_mx(
                     out=sums[:, i * width : (i + 1) * width],
-                    lhsT=wb_dealt[0][:, 2 * d * P : 2 * (d + 1) * P].bitcast(FP4X4),
-                    lhsT_scale=wb_dealt[1][:, d * P : (d + 1) * P],
+                    lhsT=wb_words_dealt[e, d].bitcast(FP4X4),
+                    lhsT_scale=wb_scales_dealt[e, d],
                     rhs=codes[:].bitcast(FP8X4),
                     rhs_scale=scales[:],
                     start=True,
@@ -207,13 +220,22 @@ def tile_moe_adp_relu_kernel(
         def scatter_on_scalar(d, first, values):
             nc.scalar.activation(out=placed[d][:].indirect(slots_of(first, values.shape[1])), in_=values, func=ACT.Copy)
 
-        def round_w(s, i, make):
-            rounded = make([P, 2 * K_PASS], BF16, "wbf%d_%d" % (s, i))
+        def round_on_vector(h, rounded):
             nc.vector.tensor_copy(
-                out=rounded[:].rearrange("p (d m j) -> p m j d", m=P, j=PACK),
-                in_=wraw[s][:].rearrange("p (j m d) -> p m j d", d=PACK, j=PACK)[:, :, :, 2 * i : 2 * i + 2],
+                out=rounded[:].rearrange("p (d m j) -> p m j d", m=P, j=PACK)[:, h * P // 2 : (h + 1) * P // 2],
+                in_=wraw0[h][:].rearrange("p (j m d) -> p m j d", d=PACK, j=PACK),
             )
-            return rounded
+
+        def round_on_gpsimd(i, rounded):
+            planes = slice(2 * i, 2 * i + 2)
+            nc.gpsimd.tensor_scalar(
+                out=rounded[:].rearrange("p (d m j) -> p m d j", m=P, j=PACK)[:, :, planes, :],
+                in0=wraw1[:].rearrange("p (j m d) -> p m d j", d=PACK, j=PACK)[:, :, planes, :],
+                scalar1=1.0,
+                scalar2=0.0,
+                op0=ALU.mult,
+                op1=ALU.add,
+            )
 
         def quantise_w(rounded, name):
             width = rounded.shape[1] // PACK
@@ -226,10 +248,10 @@ def tile_moe_adp_relu_kernel(
 
         def frozen_pass(s, wq, planes):
             codes, scales = wq
-            for i, d in enumerate(planes):
+            for d in planes:
                 if s == 0:
                     base[d] = psum.tile([P, T], F32, name="base%d" % d, tag=("bank5", "bank7", "bank4", "bank0")[d])
-                cols = slice(i * P, (i + 1) * P)
+                cols = slice(d * P, (d + 1) * P)
                 nc.tensor.matmul_mx(
                     out=base[d][:],
                     lhsT=codes[:, cols].bitcast(FP8X4),
@@ -283,7 +305,9 @@ def tile_moe_adp_relu_kernel(
         scales1 = [gather_scales(s, P, P, "gs1_%d" % s) for s in range(PASSES)]
         scales_b = [gather_scales(s, C, C, "gsb_%d" % s) for s in range(PASSES)]
         late_second = gather_words(1, C, C, "gw2_1")
-        wb0 = deal_wb(0)
+        deal_words(0, range(PACK))
+        for e in range(E):
+            deal_scales(e)
         parts = []
         for chunks, bank in (((0, 1), "bank0"), ((2,), "bank7"), ((3,), "bank5")):
             sums = psum.tile([P, len(chunks) * P], F32, name="h_part", tag=bank)
@@ -300,15 +324,17 @@ def tile_moe_adp_relu_kernel(
                         stop=(s == PASSES - 1),
                     )
             parts.append(sums[:])
+        late_first = [words_mid[:, P:C], gather_words(0, C + P, P, "gw3_0", "gw0_1")[:]]
         hrow0 = relu_h(parts, held([P, H], BF16, "hrow0"))
+        deal_words(1, (0, 1), "gw0_0")
         sums1 = first_layer(0, [t[:] for t in words1], [t[:] for t in scales1], "bank1")
         hrow1 = relu_h([sums1[:]], held([P, H], BF16, "hrow1"))
         hcol0 = held([P, PACK * P], BF16, "hcol0")
         turn_h(hrow0, hcol0[:], "bank2")
+        deal_words(1, (2, 3), "hrow0")
         hq0 = quantise_h(hcol0, P, "0")
         hcol1 = held([P, PACK * P], BF16, "hcol1")
         turn_h(hrow1, hcol1[:], "bank3")
-        late_first = [words_mid[:, P:C], gather_words(0, C + P, P, "gw3_0", "hrow1")[:]]
 
         def late_first_layer(b, bank):
             cols = slice(b * P, (b + 1) * P)
@@ -320,51 +346,48 @@ def tile_moe_adp_relu_kernel(
             return dict(zip(planes, gate_y(part, first, width, gated[:])))
 
         sums2 = late_first_layer(0, "bank1")
-        wb1 = deal_wb(1, "gw_mid")
-        order = (3, 2, 0, 1)
-        y0 = second_layer(wb0, hq0, order, "bank4")
+        sums3 = late_first_layer(1, "bank2")
+        order0, order1 = (3, 0, 2, 1), (1, 3, 0, 2)
+        early = held([P, 2 * PACK * P], F32, "gated_early")
+        y0 = second_layer(0, hq0, order0, "bank4")
         hq1 = quantise_h(hcol1, P, "1")
-        sums3 = late_first_layer(1, "bank3")
-        gated0 = gate_planes(y0, order, order, 0, P, held([P, PACK * P], F32, "gated0"))
-        rounded = [round_w(0, 0, laid_out), round_w(0, 1, held)]
-        wq0 = [quantise_w(rounded[i][:], "0_%d" % i) for i in range(2)]
-        order = (2, 3, 0, 1)
-        y1 = second_layer(wb0, hq1, order, "bank0")
+        wbf0 = laid_out([P, PACK * K_PASS], BF16, "wbf0")
+        for h in range(2):
+            round_on_vector(h, wbf0)
+        gated0 = gate_planes(y0, order0, order0, 0, P, early[:, 0 : PACK * P])
+        y1 = second_layer(0, hq1, order1, "bank0")
         hrow2 = relu_h([sums2[:]], held([P, H], BF16, "hrow2"))
         hrow3 = relu_h([sums3[:]], laid_out([P, H], BF16, "hrow3"))
-        rest2 = laid_out([P, T - P], F32, "gated_rest2")
-        gated1 = gate_planes(y1, order, (3, 0, 1), P, P, laid_out([P, 3 * P], F32, "gated1_013"))
-        gate_planes(y1, order, (2,), P, P, rest2[:, 0:P])
-        hcol2 = held([P, PACK * C], BF16, "hcol2")
+        hcol2 = laid_out([P, PACK * C], BF16, "hcol2")
         turn_h(hrow2, hcol2[:, 0 : PACK * P], "bank6")
-        turn_h(hrow3, hcol2[:, PACK * P : PACK * C], "bank2")
+        turn_h(hrow3, hcol2[:, PACK * P : PACK * C], "bank3")
+        wq0 = quantise_w(wbf0[:], "0")
+        hq2 = quantise_h(hcol2, C, "2", laid_out)
+        gate_planes(y1, order1, order1[:1], P, P, early[:, PACK * P : (PACK + 1) * P])
+        gated1 = gate_planes(y1, order1, order1[1:], P, P, early[:, (PACK + 1) * P : 2 * PACK * P])
+        wbf1 = laid_out([P, PACK * K_PASS], BF16, "wbf1")
         for i in range(2):
-            frozen_pass(0, wq0[i], (2 * i, 2 * i + 1))
-        rounded = [round_w(1, i, held) for i in range(2)]
-        wq1 = [quantise_w(rounded[0][:], "1_0")]
-        hq2 = quantise_h(hcol2, C, "2", "wraw1")
-        wq1.append(quantise_w(rounded[1][:], "1_1"))
+            round_on_gpsimd(i, wbf1)
         placed[3] = held([P, T], F32, "placed3", "hrow2")
-        placed[2] = held([P, T], F32, "placed2", "wbf1_0")
-        for d in range(2):
+        for d in range(3):
             placed[d] = laid_out([P, T], F32, "placed%d" % d)
         for first, gated in ((0, gated0), (P, gated1)):
-            for d in (3, 0, 1):
+            for d in (3, 0, 2):
                 scatter_on_scalar(d, first, gated[d])
-        y2 = [second_layer(wb1, hq2, planes, bank) for planes, bank in (((2, 3), "bank1"), ((0, 1), "bank3"))]
-        for i in range(2):
-            frozen_pass(1, wq1[i], (2 * i, 2 * i + 1))
-        scatter_on_vector(2, 0, gated0[2])
-        gate_planes(y2[0], (2, 3), (2,), C, C, rest2[:, P : T - P])
-        gated2 = gate_planes(y2[0], (2, 3), (3,), C, C, held([P, C], F32, "gated2_3"))
-        gated2.update(gate_planes(y2[1], (0, 1), (0, 1), C, C, held([P, 2 * C], F32, "gated2_01")))
-        scatter_on_vector(3, C, gated2[3][:, 0:P])
-        scatter_on_vector(2, P, rest2[:])
-        for d in range(2):
+        y2 = [second_layer(1, hq2, planes, bank) for planes, bank in (((1, 3), "bank1"), ((0, 2), "bank2"))]
+        frozen_pass(0, wq0, range(PACK))
+        scatter_on_vector(1, 0, early[:, 3 * P : 5 * P])
+        gated2 = gate_planes(y2[0], (1, 3), (1,), C, C, held([P, C], F32, "gated2_1"))
+        gated2.update(gate_planes(y2[1], (0, 2), (0, 2), C, C, held([P, 2 * C], F32, "gated2_02")))
+        scatter_on_vector(1, C, gated2[1])
+        gated2.update(gate_planes(y2[0], (1, 3), (3,), C, C, held([P, C], F32, "gated2_3", "wraw1")))
+        frozen_pass(1, quantise_w(wbf1[:], "1"), range(PACK))
+        for d in (0, 2):
             scatter_on_scalar(d, C, gated2[d])
-        scatter_on_scalar(3, C + P, gated2[3][:, P:C])
+        scatter_on_vector(3, C, gated2[3][:, 0 : C - LAST])
+        scatter_on_scalar(3, T - LAST, gated2[3][:, C - LAST : C])
         all_tokens = slice(0, T)
-        total.append(held([P, 2 * T], F32, "total1", "gated2_01"))
+        total.append(held([P, 2 * T], F32, "total1"))
         for d in range(3):
             add(d, all_tokens)
             store(d)

@@ -99,8 +99,6 @@ def tile_moe_adp_relu_kernel(
         for q in range(2, 4):
             load_scales(was, was_rows, q, nc.sync)
         make_identity(nc, ident[:])
-        unread_column = held([P, 1], F32, "unread_column")
-        nc.scalar.activation(out=unread_column[:], in_=ident[:, 0:1], func=ACT.Relu)
         for q in range(4):
             load_scales(wbs, wbs_rows, q, nc.sync)
         load_wa(1)

@@ -91,13 +91,12 @@ def tile_moe_adp_relu_kernel(
             load_scales(xs, xs_rows, q, queue)
         load_x(1)
         load_wa(0)
-        load_scales(was, was_rows, 1, nc.sync)
+        for q in range(1, 4):
+            load_scales(was, was_rows, q, nc.sync)
         nc.sync.dma_start(
             out=wbw[:].bitcast(I32).rearrange("p (e c) -> p e c", e=E),
             in_=wb_words.bitcast(I32).rearrange("e s p c -> p (e s) c"),
         )
-        for q in range(2, 4):
-            load_scales(was, was_rows, q, nc.sync)
         make_identity(nc, ident[:])
         for q in range(4):
             load_scales(wbs, wbs_rows, q, nc.sync)
@@ -171,6 +170,16 @@ def tile_moe_adp_relu_kernel(
             nc.scalar.copy(
                 out=words[:].bitcast(U16).rearrange("p (d a b) -> p a d b", d=len(planes), b=8),
                 in_=source[:, :, planes[0] : planes[-1] + 1, :],
+            )
+            for i, d in enumerate(planes):
+                wb_words_dealt[e, d] = words[:, 2 * i * P : 2 * (i + 1) * P]
+
+        def deal_bytes(e, planes):
+            words = held([P, 2 * P * len(planes)], U8, "wbw_dealt%d_%d" % (e, planes[0]))
+            source = wbw[:, 2 * e * N : 2 * (e + 1) * N].rearrange("p (a b d h) -> p a d b h", d=PACK, b=8, h=2)
+            nc.gpsimd.tensor_copy(
+                words[:].rearrange("p (d a b h) -> p a d b h", d=len(planes), b=8, h=2),
+                source[:, :, planes[0] : planes[-1] + 1, :, :],
             )
             for i, d in enumerate(planes):
                 wb_words_dealt[e, d] = words[:, 2 * i * P : 2 * (i + 1) * P]
@@ -303,7 +312,7 @@ def tile_moe_adp_relu_kernel(
         scales1 = [gather_scales(s, P, P, "gs1_%d" % s) for s in range(PASSES)]
         scales_b = [gather_scales(s, C, C, "gsb_%d" % s) for s in range(PASSES)]
         late_second = gather_words(1, C, C, "gw2_1")
-        deal_words(0, range(PACK))
+        deal_bytes(0, range(PACK))
         for e in range(E):
             deal_scales(e)
         parts = []

@@ -22,7 +22,7 @@ PACK = 4
 K_PASS = P * PACK
 PASSES = K // K_PASS
 LIST_ROWS = 16
-LAST = 64
+LAST = 96
 
 
 def tile_moe_adp_relu_kernel(
@@ -98,9 +98,11 @@ def tile_moe_adp_relu_kernel(
             in_=wb_words.bitcast(I32).rearrange("e s p c -> p (e s) c"),
         )
         make_identity(nc, ident[:])
-        for q in range(4):
+        for q in range(2):
             load_scales(wbs, wbs_rows, q, nc.sync)
         load_wa(1)
+        for q in range(2, 4):
+            load_scales(wbs, wbs_rows, q, nc.sync)
         load_w(wraw0[0], 0, slice(0, N // 2))
         load_w(wraw0[1], 0, slice(N // 2, N))
         nc.sync.dma_start(out=gates[:], in_=gate)
@@ -257,7 +259,7 @@ def tile_moe_adp_relu_kernel(
             codes, scales = wq
             for d in planes:
                 if s == 0:
-                    base[d] = psum.tile([P, T], F32, name="base%d" % d, tag=("bank5", "bank7", "bank4", "bank0")[d])
+                    base[d] = psum.tile([P, T], F32, name="base%d" % d, tag=("bank5", "bank7", "bank4", "bank2")[d])
                 cols = slice(d * P, (d + 1) * P)
                 nc.tensor.matmul_mx(
                     out=base[d][:],
@@ -307,14 +309,14 @@ def tile_moe_adp_relu_kernel(
 
         words0 = [gather_words(s, 0, P, "gw0_%d" % s) for s in range(PASSES)]
         scales0 = [gather_scales(s, 0, P, "gs0_%d" % s) for s in range(PASSES)]
-        words_mid = gather_words(0, P, C, "gw_mid")
-        words1 = [words_mid[:, 0:P], gather_words(1, P, P, "gw1_1")]
+        words_mid = [gather_words(s, P, C, "gw_mid%d" % s) for s in range(PASSES)]
+        words1 = [t[:, 0:P] for t in words_mid]
         scales1 = [gather_scales(s, P, P, "gs1_%d" % s) for s in range(PASSES)]
         scales_b = [gather_scales(s, C, C, "gsb_%d" % s) for s in range(PASSES)]
-        late_second = gather_words(1, C, C, "gw2_1")
         deal_bytes(0, range(PACK))
-        for e in range(E):
-            deal_scales(e)
+        deal_scales(0)
+        deal_bytes(1, (2, 3))
+        deal_scales(1)
         parts = []
         for chunks, bank in (((0, 1), "bank0"), ((2,), "bank7"), ((3,), "bank5")):
             sums = psum.tile([P, len(chunks) * P], F32, name="h_part", tag=bank)
@@ -331,43 +333,43 @@ def tile_moe_adp_relu_kernel(
                         stop=(s == PASSES - 1),
                     )
             parts.append(sums[:])
-        late_first = [words_mid[:, P:C], gather_words(0, C + P, P, "gw3_0", "gw0_1")[:]]
+        words3 = [gather_words(s, C + P, P, "gw3_%d" % s, after)[:] for s, after in enumerate(("gw0_1", "gs0_1"))]
+        late_words = [[t[:, P:C] for t in words_mid], words3]
         hrow0 = relu_h(parts, held([P, H], BF16, "hrow0"))
         deal_words(1, (0, 1), "gw0_0")
         sums1 = first_layer(0, [t[:] for t in words1], [t[:] for t in scales1], "bank1")
         hrow1 = relu_h([sums1[:]], held([P, H], BF16, "hrow1"))
         hcol0 = held([P, PACK * P], BF16, "hcol0")
         turn_h(hrow0, hcol0[:], "bank2")
-        deal_words(1, (2, 3), "hrow0")
         hq0 = quantise_h(hcol0, P, "0")
         hcol1 = held([P, PACK * P], BF16, "hcol1")
-        turn_h(hrow1, hcol1[:], "bank3")
 
         def late_first_layer(b, bank):
             cols = slice(b * P, (b + 1) * P)
-            return first_layer(1, [late_first[b], late_second[:, cols]], [t[:, cols] for t in scales_b], bank)
+            return first_layer(1, late_words[b], [t[:, cols] for t in scales_b], bank)
 
         def gate_planes(sums, order, planes, first, width, gated):
             at = order.index(planes[0])
             part = sums[:, at * width : (at + len(planes)) * width]
             return dict(zip(planes, gate_y(part, first, width, gated[:])))
 
-        sums2 = late_first_layer(0, "bank1")
+        sums2 = late_first_layer(0, "bank5")
+        hrow2 = relu_h([sums2[:]], held([P, H], BF16, "hrow2"))
+        turn_h(hrow1, hcol1[:], "bank3")
         sums3 = late_first_layer(1, "bank2")
         order0, order1 = (3, 0, 2, 1), (1, 3, 0, 2)
         early = held([P, 2 * PACK * P], F32, "gated_early")
         y0 = second_layer(0, hq0, order0, "bank4")
-        hq1 = quantise_h(hcol1, P, "1")
         wbf0 = laid_out([P, PACK * K_PASS], BF16, "wbf0")
-        for h in range(2):
-            round_on_vector(h, wbf0)
+        round_on_vector(0, wbf0)
+        hq1 = quantise_h(hcol1, P, "1", lambda shape, dtype, name: held(shape, dtype, name, "wraw0_0"))
+        round_on_vector(1, wbf0)
         gated0 = gate_planes(y0, order0, order0, 0, P, early[:, 0 : PACK * P])
-        y1 = second_layer(0, hq1, order1, "bank0")
-        hrow2 = relu_h([sums2[:]], held([P, H], BF16, "hrow2"))
         hrow3 = relu_h([sums3[:]], laid_out([P, H], BF16, "hrow3"))
         hcol2 = laid_out([P, PACK * C], BF16, "hcol2")
         turn_h(hrow2, hcol2[:, 0 : PACK * P], "bank6")
         turn_h(hrow3, hcol2[:, PACK * P : PACK * C], "bank3")
+        y1 = second_layer(0, hq1, order1, "bank2")
         wq0 = quantise_w(wbf0[:], "0")
         hq2 = quantise_h(hcol2, C, "2", laid_out)
         gate_planes(y1, order1, order1[:1], P, P, early[:, PACK * P : (PACK + 1) * P])
@@ -381,7 +383,7 @@ def tile_moe_adp_relu_kernel(
         for first, gated in ((0, gated0), (P, gated1)):
             for d in (3, 0, 2):
                 scatter_on_scalar(d, first, gated[d])
-        y2 = [second_layer(1, hq2, planes, bank) for planes, bank in (((1, 3), "bank1"), ((0, 2), "bank2"))]
+        y2 = [second_layer(1, hq2, planes, bank) for planes, bank in (((1, 3), "bank1"), ((0, 2), "bank0"))]
         frozen_pass(0, wq0, range(PACK))
         scatter_on_vector(1, 0, early[:, 3 * P : 5 * P])
         gated2 = gate_planes(y2[0], (1, 3), (1,), C, C, held([P, C], F32, "gated2_1"))

@@ -41,6 +41,7 @@ def tile_moe_adp_relu_kernel(
         place = {
             "placed0": 0, "hrow3": 2 * KIB - STEP, "placed2": 2 * KIB,
             "wraw0_1": 4 * KIB, "hq2": 4 * KIB, "placed1": 5 * KIB,
+            "wraw0_0": 16 * KIB, "wbw_dealt1_2": 16 * KIB, "hq1": 17 * KIB,
             "wbf0": 8 * KIB, "hcol2": 12 * KIB, "wbf1": 10 * KIB,
         }
 
@@ -55,7 +56,7 @@ def tile_moe_adp_relu_kernel(
         wbw = held([P, E * 2 * N], U8, "wbw")
         wbs = held([P, E * N], U8, "wbs")
         gates = held([P, T], F32, "gates")
-        wraw0 = [held([P, PACK * N // 2], F32, "wraw0_0"), laid_out([P, PACK * N // 2], F32, "wraw0_1")]
+        wraw0 = [laid_out([P, PACK * N // 2], F32, "wraw0_%d" % h) for h in range(2)]
         wraw1 = held([P, PACK * N], F32, "wraw1")
         ident = held([P, P], F32, "ident")
 
@@ -166,10 +167,9 @@ def tile_moe_adp_relu_kernel(
 
         wb_words_dealt, wb_scales_dealt = {}, {}
 
-        def deal_words(e, planes, after=None):
-            words = held([P, 2 * P * len(planes)], U8, "wbw_dealt%d_%d" % (e, planes[0]), after)
+        def deal_words(e, planes, words, copy):
             source = wbw[:, 2 * e * N : 2 * (e + 1) * N].bitcast(U16).rearrange("p (a b d) -> p a d b", d=PACK, b=8)
-            nc.scalar.copy(
+            copy(
                 out=words[:].bitcast(U16).rearrange("p (d a b) -> p a d b", d=len(planes), b=8),
                 in_=source[:, :, planes[0] : planes[-1] + 1, :],
             )
@@ -315,7 +315,6 @@ def tile_moe_adp_relu_kernel(
         scales_b = [gather_scales(s, C, C, "gsb_%d" % s) for s in range(PASSES)]
         deal_bytes(0, range(PACK))
         deal_scales(0)
-        deal_bytes(1, (2, 3))
         deal_scales(1)
         parts = []
         for chunks, bank in (((0, 1), "bank0"), ((2,), "bank7"), ((3,), "bank5")):
@@ -336,7 +335,7 @@ def tile_moe_adp_relu_kernel(
         words3 = [gather_words(s, C + P, P, "gw3_%d" % s, after)[:] for s, after in enumerate(("gw0_1", "gs0_1"))]
         late_words = [[t[:, P:C] for t in words_mid], words3]
         hrow0 = relu_h(parts, held([P, H], BF16, "hrow0"))
-        deal_words(1, (0, 1), "gw0_0")
+        deal_words(1, (0, 1), held([P, 4 * P], U8, "wbw_dealt1_0", "gw0_0"), nc.scalar.copy)
         sums1 = first_layer(0, [t[:] for t in words1], [t[:] for t in scales1], "bank1")
         hrow1 = relu_h([sums1[:]], held([P, H], BF16, "hrow1"))
         hcol0 = held([P, PACK * P], BF16, "hcol0")
@@ -362,7 +361,8 @@ def tile_moe_adp_relu_kernel(
         y0 = second_layer(0, hq0, order0, "bank4")
         wbf0 = laid_out([P, PACK * K_PASS], BF16, "wbf0")
         round_on_vector(0, wbf0)
-        hq1 = quantise_h(hcol1, P, "1", lambda shape, dtype, name: held(shape, dtype, name, "wraw0_0"))
+        deal_words(1, (2, 3), laid_out([P, 4 * P], U8, "wbw_dealt1_2"), nc.vector.tensor_copy)
+        hq1 = quantise_h(hcol1, P, "1", laid_out)
         round_on_vector(1, wbf0)
         gated0 = gate_planes(y0, order0, order0, 0, P, early[:, 0 : PACK * P])
         hrow3 = relu_h([sums3[:]], laid_out([P, H], BF16, "hrow3"))

@@ -40,7 +40,7 @@ def tile_moe_adp_relu_kernel(
         KIB, STEP = 1024, 64
         place = {
             "placed0": 0, "hrow3": 2 * KIB - STEP, "placed2": 2 * KIB,
-            "wraw0_1": 4 * KIB, "hq2": 4 * KIB, "placed1": 5 * KIB,
+            "wraw0_1": 4 * KIB, "hq2": 4 * KIB, "placed1": 5 * KIB, "wbs_dealt1_2": 7 * KIB,
             "wraw0_0": 16 * KIB, "wbw_dealt1_2": 16 * KIB, "hq1": 17 * KIB,
             "wbf0": 8 * KIB, "hcol2": 12 * KIB, "wbf1": 10 * KIB,
         }
@@ -186,14 +186,15 @@ def tile_moe_adp_relu_kernel(
             for i, d in enumerate(planes):
                 wb_words_dealt[e, d] = words[:, 2 * i * P : 2 * (i + 1) * P]
 
-        def deal_scales(e):
-            scales = held([P, N], U8, "wbs_dealt%d" % e)
+        def deal_scales(e, planes, make=held):
+            scales = make([P, P * len(planes)], U8, "wbs_dealt%d_%d" % (e, planes[0]))
+            source = wbs[:, e * N : (e + 1) * N].rearrange("p (a b d) -> p a d b", d=PACK, b=16)
             nc.gpsimd.tensor_copy(
-                scales[:].rearrange("p (d a b) -> p a d b", d=PACK, b=16),
-                wbs[:, e * N : (e + 1) * N].rearrange("p (a b d) -> p a d b", d=PACK, b=16),
+                scales[:].rearrange("p (d a b) -> p a d b", d=len(planes), b=16),
+                source[:, :, planes[0] : planes[-1] + 1, :],
             )
-            for d in range(PACK):
-                wb_scales_dealt[e, d] = scales[:, d * P : (d + 1) * P]
+            for i, d in enumerate(planes):
+                wb_scales_dealt[e, d] = scales[:, i * P : (i + 1) * P]
 
         def second_layer(e, hq, planes, bank):
             codes, scales = hq
@@ -314,8 +315,8 @@ def tile_moe_adp_relu_kernel(
         scales1 = [gather_scales(s, P, P, "gs1_%d" % s) for s in range(PASSES)]
         scales_b = [gather_scales(s, C, C, "gsb_%d" % s) for s in range(PASSES)]
         deal_bytes(0, range(PACK))
-        deal_scales(0)
-        deal_scales(1)
+        deal_scales(0, range(PACK))
+        deal_scales(1, (0, 1))
         parts = []
         for chunks, bank in (((0, 1), "bank0"), ((2,), "bank7"), ((3,), "bank5")):
             sums = psum.tile([P, len(chunks) * P], F32, name="h_part", tag=bank)
@@ -364,6 +365,7 @@ def tile_moe_adp_relu_kernel(
         deal_words(1, (2, 3), laid_out([P, 4 * P], U8, "wbw_dealt1_2"), nc.vector.tensor_copy)
         hq1 = quantise_h(hcol1, P, "1", laid_out)
         round_on_vector(1, wbf0)
+        deal_scales(1, (2, 3), laid_out)
         gated0 = gate_planes(y0, order0, order0, 0, P, early[:, 0 : PACK * P])
         hrow3 = relu_h([sums3[:]], laid_out([P, H], BF16, "hrow3"))
         hcol2 = laid_out([P, PACK * C], BF16, "hcol2")

from contextlib import ExitStack

import concourse.mybir as mybir
from concourse.masks import make_identity

K, T, E, C, H, N = 1024, 512, 2, 256, 512, 512
FLOPS = 2 * K * N * T + 2 * K * H * T + 2 * H * N * T

F32 = mybir.dt.float32
BF16 = mybir.dt.bfloat16
I32 = mybir.dt.int32
U32 = mybir.dt.uint32
U16 = mybir.dt.uint16
U8 = mybir.dt.uint8
FP8X4 = mybir.dt.float8_e4m3fn_x4
FP4X4 = mybir.dt.float4_e2m1fn_x4
ACT = mybir.ActivationFunctionType
ALU = mybir.AluOpType

P = 128
PACK = 4
K_PASS = P * PACK
PASSES = K // K_PASS
LIST_ROWS = 16
LAST = 96


def tile_moe_adp_relu_kernel(
    tc, x_words, x_scales, w, wa_words, wa_scales, wb_words, wb_scales, gate, offs, out_0, out_1, out_2
):
    nc = tc.nc
    with ExitStack() as ctx:
        keep = ctx.enter_context(tc.tile_pool(name="keep", bufs=1))
        laid = ctx.enter_context(tc.tile_pool(name="laid", bufs=1))
        psum = ctx.enter_context(tc.psum_pool(name="psum", bufs=1))

        def held(shape, dtype, name, after=None):
            return keep.tile(shape, dtype, name=name, tag=after or name, align_bytes=64)

        KIB, STEP = 1024, 64
        place = {
            "placed0": 0, "hrow3": 2 * KIB - STEP, "placed2": 2 * KIB,
            "wraw0_1": 4 * KIB, "hq2": 4 * KIB, "placed1": 5 * KIB, "wbs_dealt1_2": 7 * KIB,
            "wraw0_0": 16 * KIB, "wbw_dealt1_2": 16 * KIB, "hq1": 17 * KIB,
            "wbf0": 8 * KIB, "hcol2": 12 * KIB, "wbf1": 10 * KIB,
        }

        def laid_out(shape, dtype, name):
            return laid.tile(shape, dtype, name=name, align_bytes=64, offset=place[name])

        offsets = keep.tile([P, T // LIST_ROWS], U16, name="offsets")
        xw = [held([P, T], I32, "xw%d" % s) for s in range(PASSES)]
        xs = held([P, PASSES * T], U8, "xs")
        waw = [held([P, PASSES * 2 * H], U8, "waw%d" % e) for e in range(E)]
        was = held([P, E * PASSES * H], U8, "was")
        wbw = held([P, E * 2 * N], U8, "wbw")
        wbs = held([P, E * N], U8, "wbs")
        gates = held([P, T], F32, "gates")
        wraw0 = [laid_out([P, PACK * N // 2], F32, "wraw0_%d" % h) for h in range(2)]
        wraw1 = held([P, PACK * N], F32, "wraw1")
        ident = held([P, P], F32, "ident")

        def load_scales(tile, scale_rows, q, queue):
            queue.dma_start(
                out=tile[q:P:32, :].bitcast(I32).rearrange("r (g c) -> r g c", g=scale_rows.shape[1]),
                in_=scale_rows[q:16:4],
            )

        def load_x(s):
            nc.sync.dma_start(out=xw[s][:], in_=x_words[s].rearrange("p n d -> p (n d)").bitcast(I32))

        def load_wa(e):
            nc.sync.dma_start(
                out=waw[e][:].bitcast(I32).rearrange("p (s c) -> p s c", s=PASSES),
                in_=wa_words[e].bitcast(I32).rearrange("s p c -> p s c"),
            )

        def load_w(tile, s, columns):
            rows = w[K_PASS * s : K_PASS * (s + 1), :].rearrange("(p j) n -> p j n", j=PACK)
            nc.sync.dma_start(out=tile[:].rearrange("p (j n) -> p j n", j=PACK), in_=rows[:, :, columns])

        xs_rows = x_scales.bitcast(I32).rearrange("s b c -> b s c")
        was_rows = wa_scales.bitcast(I32).rearrange("e s b c -> b (e s) c")
        wbs_rows = wb_scales.bitcast(I32).rearrange("e s b c -> b (e s) c")

        nc.vector.memset(xs[:].bitcast(I32), 0)
        nc.vector.memset(wbs[:].bitcast(I32), 0)
        nc.sync.dma_start(offsets[:], offs)
        load_scales(was, was_rows, 0, nc.scalar)
        load_x(0)
        for q, queue in enumerate((nc.scalar, nc.sync, nc.scalar, nc.scalar)):
            load_scales(xs, xs_rows, q, queue)
        load_x(1)
        load_wa(0)
        for q in range(1, 4):
            load_scales(was, was_rows, q, nc.sync)
        nc.sync.dma_start(
            out=wbw[:].bitcast(I32).rearrange("p (e c) -> p e c", e=E),
            in_=wb_words.bitcast(I32).rearrange("e s p c -> p (e s) c"),
        )
        make_identity(nc, ident[:])
        for q in range(2):
            load_scales(wbs, wbs_rows, q, nc.sync)
        load_wa(1)
        for q in range(2, 4):
            load_scales(wbs, wbs_rows, q, nc.sync)
        load_w(wraw0[0], 0, slice(0, N // 2))
        load_w(wraw0[1], 0, slice(N // 2, N))
        nc.sync.dma_start(out=gates[:], in_=gate)
        load_w(wraw1, 1, slice(0, N))

        def slots_of(first, width):
            return offsets[:, first // LIST_ROWS : (first + width) // LIST_ROWS]

        def gather_words(s, first, width, name, after=None):
            tile = held([P, width], I32, name, after)
            nc.vector.tensor_copy(tile[:].bitcast(U32), xw[s][:].bitcast(U32).indirect(slots_of(first, width)))
            return tile

        def gather_scales(s, first, width, name, after=None):
            tile = held([P, width], U8, name, after)
            nc.vector.tensor_copy(tile[:], xs[:, s * T : (s + 1) * T].indirect(slots_of(first, width)))
            return tile

        def first_layer(e, words, scales, bank):
            sums = psum.tile([P, H], F32, name="h_sums", tag=bank)
            for s in range(PASSES):
                nc.tensor.matmul_mx(
                    out=sums[:],
                    lhsT=words[s].bitcast(FP8X4),
                    lhsT_scale=scales[s],
                    rhs=waw[e][:, s * 2 * H : (s + 1) * 2 * H].bitcast(FP4X4),
                    rhs_scale=was[:, (e * PASSES + s) * H : (e * PASSES + s + 1) * H],
                    start=(s == 0),
                    stop=(s == PASSES - 1),
                )
            return sums

        def relu_h(parts, hrow):
            first = 0
            for part in parts:
                span = part.shape[1] // PACK
                nc.scalar.activation(
                    out=hrow[:].rearrange("j (u p r) -> j u p r", u=2, r=2)[:, :, first : first + span],
                    in_=part.rearrange("j (p u r) -> j u p r", u=2, r=2),
                    func=ACT.Relu,
                )
                first = first + span
            return hrow

        def turn_h(hrow, hcol, turn_bank):
            turned = psum.tile([P, 2 * P], F32, name="h_turned", tag=turn_bank)
            for u in range(2):
                nc.tensor.transpose(
                    turned[:, u * P : (u + 1) * P], hrow[:].bitcast(F32)[:, u * P : (u + 1) * P], ident[:]
                )
            nc.scalar.copy(
                out=hcol.bitcast(F32).rearrange("p (j u) -> p j u", u=2),
                in_=turned[:].rearrange("p (u j) -> p j u", u=2),
            )

        def quantise_h(hcol, width, name, make=held):
            codes = make([P, width], U32, "hq" + name)
            scales = held([P, width], U8, "hs" + name)
            nc.vector.quantize_mx(out=codes[:].bitcast(FP8X4), scales=scales[:], in_=hcol[:])
            return codes, scales

        wb_words_dealt, wb_scales_dealt = {}, {}

        def deal_words(e, planes, words, copy):
            source = wbw[:, 2 * e * N : 2 * (e + 1) * N].bitcast(U16).rearrange("p (a b d) -> p a d b", d=PACK, b=8)
            copy(
                out=words[:].bitcast(U16).rearrange("p (d a b) -> p a d b", d=len(planes), b=8),
                in_=source[:, :, planes[0] : planes[-1] + 1, :],
            )
            for i, d in enumerate(planes):
                wb_words_dealt[e, d] = words[:, 2 * i * P : 2 * (i + 1) * P]

        def deal_bytes(e, planes):
            words = held([P, 2 * P * len(planes)], U8, "wbw_dealt%d_%d" % (e, planes[0]))
            source = wbw[:, 2 * e * N : 2 * (e + 1) * N].rearrange("p (a b d h) -> p a d b h", d=PACK, b=8, h=2)
            nc.gpsimd.tensor_copy(
                words[:].rearrange("p (d a b h) -> p a d b h", d=len(planes), b=8, h=2),
                source[:, :, planes[0] : planes[-1] + 1, :, :],
            )
            for i, d in enumerate(planes):
                wb_words_dealt[e, d] = words[:, 2 * i * P : 2 * (i + 1) * P]

        def deal_scales(e, planes, make=held):
            scales = make([P, P * len(planes)], U8, "wbs_dealt%d_%d" % (e, planes[0]))
            source = wbs[:, e * N : (e + 1) * N].rearrange("p (a b d) -> p a d b", d=PACK, b=16)
            nc.gpsimd.tensor_copy(
                scales[:].rearrange("p (d a b) -> p a d b", d=len(planes), b=16),
                source[:, :, planes[0] : planes[-1] + 1, :],
            )
            for i, d in enumerate(planes):
                wb_scales_dealt[e, d] = scales[:, i * P : (i + 1) * P]

        def second_layer(e, hq, planes, bank):
            codes, scales = hq
            width = codes.shape[1]
            sums = psum.tile([P, len(planes) * width], F32, name="y_sums", tag=bank)
            for i, d in enumerate(planes):
                nc.tensor.matmul_mx(
                    out=sums[:, i * width : (i + 1) * width],
                    lhsT=wb_words_dealt[e, d].bitcast(FP4X4),
                    lhsT_scale=wb_scales_dealt[e, d],
                    rhs=codes[:].bitcast(FP8X4),
                    rhs_scale=scales[:],
                    start=True,
                    stop=True,
                )
            return sums

        def gate_y(sums, first, width, gated):
            planes = sums.shape[1] // width
            nc.vector.tensor_tensor(
                out=gated.rearrange("p (d j) -> p d j", d=planes),
                in0=sums.rearrange("p (d j) -> p d j", d=planes),
                in1=gates[:, first : first + width].unsqueeze(1).to_broadcast([P, planes, width]),
                op=ALU.mult,
            )
            return [gated[:, i * width : (i + 1) * width] for i in range(planes)]

        placed = {}

        def scatter_on_vector(d, first, values):
            nc.vector.tensor_copy(placed[d][:].indirect(slots_of(first, values.shape[1])), values)

        def scatter_on_scalar(d, first, values):
            nc.scalar.activation(out=placed[d][:].indirect(slots_of(first, values.shape[1])), in_=values, func=ACT.Copy)

        def round_on_vector(h, rounded):
            nc.vector.tensor_copy(
                out=rounded[:].rearrange("p (d m j) -> p m j d", m=P, j=PACK)[:, h * P // 2 : (h + 1) * P // 2],
                in_=wraw0[h][:].rearrange("p (j m d) -> p m j d", d=PACK, j=PACK),
            )

        def round_on_gpsimd(i, rounded):
            planes = slice(2 * i, 2 * i + 2)
            nc.gpsimd.tensor_scalar(
                out=rounded[:].rearrange("p (d m j) -> p m d j", m=P, j=PACK)[:, :, planes, :],
                in0=wraw1[:].rearrange("p (j m d) -> p m d j", d=PACK, j=PACK)[:, :, planes, :],
                scalar1=1.0,
                scalar2=0.0,
                op0=ALU.mult,
                op1=ALU.add,
            )

        def quantise_w(rounded, name):
            width = rounded.shape[1] // PACK
            codes = held([P, width], U32, "wq" + name)
            scales = held([P, width], U8, "wsc" + name)
            nc.vector.quantize_mx(out=codes[:].bitcast(FP8X4), scales=scales[:], in_=rounded)
            return codes, scales

        base = {}

        def frozen_pass(s, wq, planes):
            codes, scales = wq
            for d in planes:
                if s == 0:
                    base[d] = psum.tile([P, T], F32, name="base%d" % d, tag=("bank5", "bank7", "bank4", "bank2")[d])
                cols = slice(d * P, (d + 1) * P)
                nc.tensor.matmul_mx(
                    out=base[d][:],
                    lhsT=codes[:, cols].bitcast(FP8X4),
                    lhsT_scale=scales[:, cols],
                    rhs=xw[s][:].bitcast(FP8X4),
                    rhs_scale=xs[:, s * T : (s + 1) * T],
                    start=(s == 0),
                    stop=(s == PASSES - 1),
                )

        total = [held([P, 2 * T], F32, "total0")]
        out_planes = out_0.rearrange("(p d) t -> p d t", d=PACK)

        def total_of(d):
            return total[d // 2][:, (d % 2) * T : (d % 2 + 1) * T]

        def add(d, tokens):
            nc.vector.tensor_tensor(
                out=total_of(d)[:, tokens], in0=base[d][:, tokens], in1=placed[d][:, tokens], op=ALU.add
            )

        def store(d):
            nc.sync.dma_start(out=out_planes[:, d, :], in_=total_of(d))

        ow = held([P, T], U32, "ow")
        osc = held([P, T], U8, "osc")
        obf = held([P, PACK * T], BF16, "obf")

        def round_pair(copy, i, tokens):
            copy(
                out=obf[:].rearrange("p (t d) -> p t d", d=PACK)[:, tokens, 2 * i : 2 * i + 2],
                in_=total[i][:].rearrange("p (d t) -> p t d", d=2)[:, tokens, :],
            )

        unread = psum.tile([P, T], F32, name="unread", tag="bank6")
        for i in range(2):
            nc.tensor.matmul_mx(
                out=unread[:],
                lhsT=xw[0][:, 0:P].bitcast(FP8X4),
                lhsT_scale=xs[:, 0:P],
                rhs=xw[0][:].bitcast(FP8X4),
                rhs_scale=xs[:, 0:T],
                start=True,
                stop=True,
            )

        words0 = [gather_words(s, 0, P, "gw0_%d" % s) for s in range(PASSES)]
        scales0 = [gather_scales(s, 0, P, "gs0_%d" % s) for s in range(PASSES)]
        words_mid = [gather_words(s, P, C, "gw_mid%d" % s) for s in range(PASSES)]
        words1 = [t[:, 0:P] for t in words_mid]
        scales1 = [gather_scales(s, P, P, "gs1_%d" % s) for s in range(PASSES)]
        scales_b = [gather_scales(s, C, C, "gsb_%d" % s) for s in range(PASSES)]
        deal_bytes(0, range(PACK))
        deal_scales(0, range(PACK))
        deal_scales(1, (0, 1))
        parts = []
        for chunks, bank in (((0, 1), "bank0"), ((2,), "bank7"), ((3,), "bank5")):
            sums = psum.tile([P, len(chunks) * P], F32, name="h_part", tag=bank)
            for i, chunk in enumerate(chunks):
                for s in range(PASSES):
                    first = s * H + chunk * P
                    nc.tensor.matmul_mx(
                        out=sums[:, i * P : (i + 1) * P],
                        lhsT=words0[s][:].bitcast(FP8X4),
                        lhsT_scale=scales0[s][:],
                        rhs=waw[0][:, 2 * first : 2 * (first + P)].bitcast(FP4X4),
                        rhs_scale=was[:, first : first + P],
                        start=(s == 0),
                        stop=(s == PASSES - 1),
                    )
            parts.append(sums[:])
        words3 = [gather_words(s, C + P, P, "gw3_%d" % s, after)[:] for s, after in enumerate(("gw0_1", "gs0_1"))]
        late_words = [[t[:, P:C] for t in words_mid], words3]
        hrow0 = relu_h(parts, held([P, H], BF16, "hrow0"))
        deal_words(1, (0, 1), held([P, 4 * P], U8, "wbw_dealt1_0", "gw0_0"), nc.scalar.copy)
        sums1 = first_layer(0, [t[:] for t in words1], [t[:] for t in scales1], "bank1")
        hrow1 = relu_h([sums1[:]], held([P, H], BF16, "hrow1"))
        hcol0 = held([P, PACK * P], BF16, "hcol0")
        turn_h(hrow0, hcol0[:], "bank2")
        hq0 = quantise_h(hcol0, P, "0")
        hcol1 = held([P, PACK * P], BF16, "hcol1")

        def late_first_layer(b, bank):
            cols = slice(b * P, (b + 1) * P)
            return first_layer(1, late_words[b], [t[:, cols] for t in scales_b], bank)

        def gate_planes(sums, order, planes, first, width, gated):
            at = order.index(planes[0])
            part = sums[:, at * width : (at + len(planes)) * width]
            return dict(zip(planes, gate_y(part, first, width, gated[:])))

        sums2 = late_first_layer(0, "bank5")
        hrow2 = relu_h([sums2[:]], held([P, H], BF16, "hrow2"))
        turn_h(hrow1, hcol1[:], "bank3")
        sums3 = late_first_layer(1, "bank2")
        order0, order1 = (3, 0, 2, 1), (1, 3, 0, 2)
        early = held([P, 2 * PACK * P], F32, "gated_early")
        y0 = second_layer(0, hq0, order0, "bank4")
        wbf0 = laid_out([P, PACK * K_PASS], BF16, "wbf0")
        round_on_vector(0, wbf0)
        deal_words(1, (2, 3), laid_out([P, 4 * P], U8, "wbw_dealt1_2"), nc.vector.tensor_copy)
        hq1 = quantise_h(hcol1, P, "1", laid_out)
        round_on_vector(1, wbf0)
        deal_scales(1, (2, 3), laid_out)
        gated0 = gate_planes(y0, order0, order0, 0, P, early[:, 0 : PACK * P])
        hrow3 = relu_h([sums3[:]], laid_out([P, H], BF16, "hrow3"))
        hcol2 = laid_out([P, PACK * C], BF16, "hcol2")
        turn_h(hrow2, hcol2[:, 0 : PACK * P], "bank6")
        turn_h(hrow3, hcol2[:, PACK * P : PACK * C], "bank3")
        y1 = second_layer(0, hq1, order1, "bank2")
        wq0 = quantise_w(wbf0[:], "0")
        hq2 = quantise_h(hcol2, C, "2", laid_out)
        gate_planes(y1, order1, order1[:1], P, P, early[:, PACK * P : (PACK + 1) * P])
        gated1 = gate_planes(y1, order1, order1[1:], P, P, early[:, (PACK + 1) * P : 2 * PACK * P])
        wbf1 = laid_out([P, PACK * K_PASS], BF16, "wbf1")
        for i in range(2):
            round_on_gpsimd(i, wbf1)
        placed[3] = held([P, T], F32, "placed3", "hrow2")
        for d in range(3):
            placed[d] = laid_out([P, T], F32, "placed%d" % d)
        for first, gated in ((0, gated0), (P, gated1)):
            for d in (3, 0, 2):
                scatter_on_scalar(d, first, gated[d])
        y2 = [second_layer(1, hq2, planes, bank) for planes, bank in (((1, 3), "bank1"), ((0, 2), "bank0"))]
        frozen_pass(0, wq0, range(PACK))
        scatter_on_vector(1, 0, early[:, 3 * P : 5 * P])
        gated2 = gate_planes(y2[0], (1, 3), (1,), C, C, held([P, C], F32, "gated2_1"))
        gated2.update(gate_planes(y2[1], (0, 2), (0, 2), C, C, held([P, 2 * C], F32, "gated2_02")))
        scatter_on_vector(1, C, gated2[1])
        gated2.update(gate_planes(y2[0], (1, 3), (3,), C, C, held([P, C], F32, "gated2_3", "wraw1")))
        frozen_pass(1, quantise_w(wbf1[:], "1"), range(PACK))
        for d in (0, 2):
            scatter_on_scalar(d, C, gated2[d])
        scatter_on_vector(3, C, gated2[3][:, 0 : C - LAST])
        scatter_on_scalar(3, T - LAST, gated2[3][:, C - LAST : C])
        all_tokens = slice(0, T)
        total.append(held([P, 2 * T], F32, "total1"))
        for d in range(3):
            add(d, all_tokens)
            store(d)
        halves = (slice(T // 2, T), slice(0, T // 2))
        for tokens in halves:
            round_pair(nc.scalar.copy, 0, tokens)
        for tokens in halves:
            add(3, tokens)
        store(3)
        for tokens in halves:
            round_pair(nc.vector.tensor_copy, 1, tokens)
        words_out = out_1[0].rearrange("p n d -> p (n d)").bitcast(I32)
        for tokens in halves:
            nc.vector.quantize_mx(
                out=ow[:, tokens].bitcast(FP8X4),
                scales=osc[:, tokens],
                in_=obf[:, PACK * tokens.start : PACK * tokens.stop],
            )
            nc.sync.dma_start(out=words_out[:, tokens], in_=ow[:, tokens].bitcast(I32))
        for q, queue in enumerate((nc.scalar, nc.sync, nc.scalar, nc.sync)):
            queue.dma_start(out=out_2[0, q:16:4, :].bitcast(I32), in_=osc[q:P:32, :].bitcast(I32))
